import numpy as np
import ml_dtypes


def mxq(x, axis, fmt="e4m3"):
    dtype, down = {"e4m3": (ml_dtypes.float8_e4m3fn, 7), "e5m2": (ml_dtypes.float8_e5m2, 14)}[fmt]
    v = np.moveaxis(np.asarray(x, np.float32).astype(ml_dtypes.bfloat16).astype(np.float64), axis, -1)
    blocks = v.reshape(v.shape[:-1] + (-1, 32))
    amax = np.abs(blocks).max(-1, keepdims=True)
    byte = np.maximum(np.where(amax > 0, np.frexp(amax)[1] - 1 + 127, 0) - down, 1)
    scale = np.exp2(byte - 127.0)
    codes = (blocks / scale).astype(np.float32).astype(dtype).astype(np.float64)
    return np.moveaxis((codes * scale).reshape(v.shape), -1, axis)


WIDE = False


def mx_kscale(k):
    if not WIDE:
        return np.ones(k)
    levels = np.array([10, -10, 5, -5, 0])
    if k % 512:
        return np.exp2(np.random.permutation(np.resize(levels, k // 32))).repeat(32)
    a = np.empty((k // 512, 16))
    for p in range(k // 512):
        a[p, :8] = np.random.permutation(np.resize(levels, 8))
        for g in range(8):
            far = levels[np.abs(levels - a[p, g]) >= 10]
            a[p, g + 8] = far[np.random.randint(len(far))]
    return np.exp2(a.ravel()).repeat(32)


def f64(x):
    return np.asarray(x).astype(np.float64)


def striped(idx):
    return np.tile(idx.reshape(-1, 16).T, (8, 1)).astype(np.uint16)


def unstriped(offs):
    return offs[:16].T.reshape(-1).astype(np.int64)


E2M1 = np.array([0.0, 0.5, 1.0, 1.5, 2.0, 3.0, 4.0, 6.0, -0.0, -0.5, -1.0, -1.5, -2.0, -3.0, -4.0, -6.0])


def pack_weight(w, fmt):
    k, n = w.shape
    w = f64(np.asarray(w, np.float32).astype(ml_dtypes.bfloat16)).reshape(k // 32, 32, n)
    amax = np.abs(w).max(1)
    if fmt == "e4m3":
        byte = np.frexp(amax)[1] - 1 + 127 - 7
    else:
        mant, ex = np.frexp(amax / 6.0)
        byte = np.where(mant > 0.5, ex, ex - 1) + 127
    byte = np.clip(np.where(amax > 0, byte, 1), 1, 254)
    scaled = (w * np.exp2(127.0 - byte)[:, None, :]).reshape(k, n).astype(np.float32)
    by_word = np.ascontiguousarray(scaled.reshape(k // 512, 128, 4, n).transpose(0, 1, 3, 2))
    if fmt == "e4m3":
        words = by_word.astype(ml_dtypes.float8_e4m3fn).view(np.uint8)
    else:
        c = by_word.astype(ml_dtypes.float4_e2m1fn).view(np.uint8) & 0xF
        words = (c[..., 0::2] | (c[..., 1::2] << 4)).reshape(k // 512, 128, 2 * n)
    return np.ascontiguousarray(words), np.ascontiguousarray(byte.astype(np.uint8).reshape(k // 512, 16, n))


def unpack_weight(words, scales, fmt):
    g, _, n = scales.shape
    words = np.ascontiguousarray(words).reshape(g, 128, n, -1)
    if fmt == "e4m3":
        vals = words.view(ml_dtypes.float8_e4m3fn).astype(np.float64)
    else:
        nib = np.empty((g, 128, n, 4), np.uint8)
        nib[..., 0::2] = words & 0xF
        nib[..., 1::2] = words >> 4
        vals = E2M1[nib]
    vals = vals * np.repeat(np.exp2(scales.astype(np.float64) - 127.0), 8, axis=1)[..., None]
    return vals.transpose(0, 1, 3, 2).reshape(g * 512, n)


def gelu(v):
    return 0.5 * v * (1.0 + np.tanh(np.sqrt(2.0 / np.pi) * (v + 0.044715 * v**3)))


def bf(x):
    return np.asarray(x, np.float32).astype(ml_dtypes.bfloat16)


def planes(Y):
    n, m = Y.shape
    b = f64(bf(Y)).reshape(n // 32, 32, m)
    amax = np.abs(b).max(1)
    byte = np.clip(np.where(amax > 0, np.frexp(amax)[1] - 1 + 127 - 7, 1), 1, 254)
    codes = (b * np.exp2(127.0 - byte)[:, None, :]).reshape(n, m).astype(np.float32).astype(ml_dtypes.float8_e4m3fn).view(np.uint8)
    words = codes.reshape(n // 512, 128, 4, m).transpose(0, 1, 3, 2)
    return np.ascontiguousarray(words), np.ascontiguousarray(byte.astype(np.uint8).reshape(n // 512, 16, m))


K, H, N, T, S, T2, P = 1024, 1024, 512, 2048, 1024, 2048, 1024

def setup_inputs():
    n = np.random.standard_normal
    s = mx_kscale(K)[:, None]
    u = mx_kscale(H)[:, None]
    tab_words, tab_scales = pack_weight(n((K, T)) * s, "e4m3")
    w1 = 1.3 * n((K, H)) / np.sqrt(K) / s * u.T
    w2_words, w2_scales = pack_weight(n((K, H)) / np.sqrt(K) / s, "e2m1")
    w3 = n((H, N)) * np.exp(0.8 * n((1, N))) / np.sqrt(H) / u
    w3_words, w3_scales = pack_weight(w3, "e4m3")
    perm = np.random.permutation(T2)
    return {
        "tab_words": tab_words, "tab_scales": tab_scales,
        "offs": striped(np.random.permutation(T)[:S]),
        "offs2": striped(np.random.permutation(T2)[:S]),
        "offs3": striped(perm[:P]),
        "offs4": striped(perm[P:]),
        "w1": w1.astype(np.float32),
        "w2_words": w2_words, "w2_scales": w2_scales,
        "w3_words": w3_words, "w3_scales": w3_scales,
        "wgs": np.exp(0.3 * n((128, S))).astype(np.float32),
        "page0": (0.8 * n((H, T2)) * u).astype(np.float32),
    }

def reference(tab_words, tab_scales, offs, offs2, offs3, offs4, w1, w2_words, w2_scales,
              w3_words, w3_scales, wgs, page0):
    v = unpack_weight(tab_words, tab_scales, "e4m3")[:, unstriped(offs)]
    a = mxq(f64(w1), 0, "e4m3").T @ v
    b = unpack_weight(w2_words, w2_scales, "e2m1").T @ v
    h = a / (1.0 + np.abs(b))
    page = f64(page0).copy()
    page[:, unstriped(offs2)] = np.tile(f64(wgs), (H // 128, 1)) * h
    z = page[:, unstriped(offs3)] - page[:, unstriped(offs4)]
    w3 = unpack_weight(w3_words, w3_scales, "e4m3")
    y = np.abs(w3.T @ mxq(z, 0, "e4m3"))
    words, scales = planes(y)
    return y, words, scales

@@ -1,0 +1,356 @@
+from contextlib import ExitStack
+
+import concourse.mybir as mybir
+from concourse.masks import make_identity
+
+K, H, N, T, S, T2, M = 1024, 1024, 512, 2048, 1024, 2048, 1024
+FLOPS = 2 * K * H * S * 2 + 2 * H * N * M
+
+F32 = mybir.dt.float32
+BF16 = mybir.dt.bfloat16
+I32 = mybir.dt.int32
+U32 = mybir.dt.uint32
+U16 = mybir.dt.uint16
+U8 = mybir.dt.uint8
+FP8X4 = mybir.dt.float8_e4m3fn_x4
+FP4X4 = mybir.dt.float4_e2m1fn_x4
+ALU = mybir.AluOpType
+ACT = mybir.ActivationFunctionType
+
+P = 128
+PACK = 4
+PASS = P * PACK
+BANK = 512
+CHUNK = 256
+UNIT = 128
+LIST_ROWS = 16
+
+
+def tile_list_stemma_deviation_kernel(
+    tc, tab_words, tab_scales, offs, offs2, offs3, offs4, w1, w2_words, w2_scales,
+    w3_words, w3_scales, wgs, page0, out_0, out_1, out_2,
+):
+    nc = tc.nc
+    with ExitStack() as ctx:
+        keep = ctx.enter_context(tc.tile_pool(name="keep", bufs=1))
+        psum = ctx.enter_context(tc.psum_pool(name="psum", bufs=2))
+
+        def sb(name, shape, dtype, tag=None, bufs=1):
+            return keep.tile(shape, dtype, name=name, tag=tag or name, bufs=bufs, align_bytes=64)
+
+        def entries(lst, first, count):
+            return lst[:, first // LIST_ROWS : (first + count) // LIST_ROWS]
+
+        lists = [keep.tile([P, S // LIST_ROWS], U16, name="list%d" % i) for i in range(4)]
+        idx, idx2, idx3, idx4 = lists
+
+        tab_s = sb("tab_s", [P, 2 * T], U8)
+        w2_s = sb("w2_s", [P, 2 * H], U8)
+        w3_s_raw = sb("w3_s_raw", [P, N], U8)
+        nc.vector.memset(tab_s[:].bitcast(I32), 0)
+        nc.gpsimd.memset(w2_s[:].bitcast(I32), 0)
+        nc.gpsimd.memset(w3_s_raw[:].bitcast(I32), 0)
+        ident = sb("ident", [P, P], F32)
+        make_identity(nc, ident[:])
+        warm = sb("warm", [P, 1], F32)
+        nc.scalar.activation(out=warm[:], in_=ident[:, 0:1], func=ACT.Abs_reciprocal_sqrt, bias=1.0)
+
+        tab_w = [sb("tab_w%d" % a, [P, T], I32) for a in range(2)]
+        w2_w = [sb("w2_w%d" % g, [P, 2, 2 * PASS], U8) for g in range(2)]
+        wgs4 = [sb("wgs_first", [P, 1, S], F32), sb("wgs_rest", [P, 3, S], F32)]
+        w3_w_raw = sb("w3_w_raw", [P, 2, N], I32)
+
+        def load_tab_words(a):
+            nc.sync.dma_start(
+                out=tab_w[a][:],
+                in_=tab_words[a].rearrange("p t i -> p (t i)").bitcast(I32),
+            )
+
+        def load_scale_rows(dst, src):
+            for q in range(4):
+                nc.sync.dma_start(
+                    out=dst[32 * q : 32 * q + 4, :].bitcast(I32).rearrange("r (a c) -> r a c", a=2),
+                    in_=src[:, 4 * q : 4 * q + 4, :].bitcast(I32).rearrange("a r c -> r a c"),
+                )
+
+        def load_w2_words(g):
+            nc.sync.dma_start(
+                out=w2_w[g][:].bitcast(I32),
+                in_=w2_words[:, :, g * 2 * PASS : (g + 1) * 2 * PASS].bitcast(I32).rearrange("a p c -> p a c"),
+            )
+
+        w1_raw = {}
+
+        def load_w1(a, g):
+            if (a, g) == (0, 0):
+                raw = sb("w1_raw00", [P, PACK, PASS], F32, tag="b_abs")
+            else:
+                raw = sb("w1_raw%d%d" % (a, g), [P, PACK, PASS], F32, tag="w1_then_y", bufs=3)
+            nc.sync.dma_start(
+                out=raw[:],
+                in_=w1[a * PASS : (a + 1) * PASS, g * PASS : (g + 1) * PASS].rearrange("(p i) c -> p i c", i=PACK),
+            )
+            w1_raw[a, g] = raw
+
+        def load_wgs(dst, t0, t1):
+            rows = wgs.rearrange("(q t) j -> q t j", t=PACK)
+            for quad in range(4):
+                nc.sync.dma_start(out=dst[32 * quad : 32 * quad + 32, :, :], in_=rows[:, t0:t1, :])
+
+        pages = {}
+
+        def load_page(i):
+            g, t = divmod(i, PACK)
+            page = sb("page%d" % i, [P, T2], F32, tag="page", bufs=6)
+            nc.sync.dma_start(
+                out=page[:],
+                in_=page0[g * PASS : (g + 1) * PASS, :].rearrange("(p t) c -> t p c", t=PACK)[t],
+            )
+            pages[i] = page
+
+        nc.sync.dma_start(idx[:], offs)
+        load_tab_words(0)
+        load_tab_words(1)
+        load_scale_rows(tab_s, tab_scales)
+        load_w2_words(0)
+        load_scale_rows(w2_s, w2_scales)
+        load_w1(0, 0)
+        load_w1(1, 0)
+        nc.sync.dma_start(idx2[:], offs2)
+        load_wgs(wgs4[0], 0, 1)
+        load_page(0)
+        nc.sync.dma_start(idx4[:], offs4)
+        nc.sync.dma_start(idx3[:], offs3)
+        load_page(1)
+        load_wgs(wgs4[1], 1, 4)
+        load_w2_words(1)
+        load_w1(0, 1)
+        load_w1(1, 1)
+        load_page(2)
+        nc.sync.dma_start(
+            out=w3_w_raw[:],
+            in_=w3_words.rearrange("a p c i -> p a (c i)").bitcast(I32),
+        )
+        for q in range(4):
+            nc.sync.dma_start(
+                out=w3_s_raw[32 * q : 32 * q + 8, :].bitcast(I32),
+                in_=w3_scales[:, 4 * q : 4 * q + 4, :].bitcast(I32),
+            )
+        for i in range(3, 6):
+            load_page(i)
+
+        v_w = [sb("v_w%d" % a, [P, S], U32) for a in range(2)]
+        v_s = [sb("v_s%d" % a, [P, S], U8) for a in range(2)]
+
+        def gather_words(a):
+            nc.vector.tensor_copy(v_w[a][:], tab_w[a][:].bitcast(U32).indirect(idx[:]))
+
+        def gather_scales(half):
+            cols = slice(half * BANK, (half + 1) * BANK)
+            picks = entries(idx, half * BANK, BANK)
+            for a in range(2):
+                nc.vector.tensor_copy(v_s[a][:, cols], tab_s[:, a * T : (a + 1) * T].indirect(picks))
+
+        def abs_b(b_abs, g, jb):
+            bank = psum.tile([P, BANK], F32, name="b_bank", tag="b_bank")
+            cols = slice(jb * P, (jb + 1) * P)
+            for a in range(2):
+                nc.tensor.matmul_mx(
+                    out=bank[:],
+                    lhsT=v_w[a][:, cols].bitcast(FP8X4),
+                    lhsT_scale=v_s[a][:, cols],
+                    rhs=w2_w[g][:, a, :].bitcast(FP4X4),
+                    rhs_scale=w2_s[:, a * H + g * PASS : a * H + (g + 1) * PASS],
+                    start=(a == 0),
+                    stop=(a == 1),
+                )
+            nc.scalar.activation(
+                out=b_abs[:, jb, :].rearrange("j (t p) -> j t p", t=PACK),
+                in_=bank[:].rearrange("j (p t) -> j t p", t=PACK),
+                func=ACT.Abs,
+            )
+
+        w1_w = [sb("w1_w%d" % a, [P, H], U32) for a in range(2)]
+        w1_s = [sb("w1_s%d" % a, [P, H], U8) for a in range(2)]
+
+        def quantize_w1(a, g, on_vector):
+            grouped = sb("w1_bf%d%d" % (a, g), [P, PASS * PACK], BF16, tag="bf", bufs=3)
+            src = w1_raw[a, g][:].rearrange("p i (m t) -> p m t i", t=PACK)
+            dst = grouped[:].rearrange("p (t m i) -> p m t i", t=PACK, i=PACK)
+            if on_vector:
+                nc.vector.tensor_copy(out=dst, in_=src)
+            else:
+                nc.scalar.copy(out=dst, in_=src)
+            cols = slice(g * PASS, (g + 1) * PASS)
+            nc.vector.quantize_mx(out=w1_w[a][:, cols].bitcast(FP8X4), scales=w1_s[a][:, cols], in_=grouped[:])
+
+        damp_ring = [sb("damp%d" % i, [P, S], F32) for i in range(3)]
+        root = sb("root", [P, S], F32)
+        h_ring = [sb("h%d" % i, [P, S], F32) for i in range(2)]
+
+        def make_h(b_abs, i, half, root_half=None):
+            g, t = divmod(i, PACK)
+            cols = slice(half * BANK, (half + 1) * BANK)
+            turned = psum.tile([P, BANK], F32, name="turned", tag="turned")
+            for q in range(4):
+                nc.tensor.transpose(
+                    turned[:, q * P : (q + 1) * P], b_abs[:, half * 4 + q, t * P : (t + 1) * P], ident[:]
+                )
+            if root_half is None:
+                root_half = root[:, cols]
+            nc.scalar.activation(out=root_half, in_=turned[:], func=ACT.Abs_reciprocal_sqrt, bias=1.0)
+            damp = damp_ring[i % 3]
+            nc.scalar.activation(out=damp[:, cols], in_=root_half, func=ACT.Square)
+            acc = psum.tile([P, BANK], F32, name="acc", tag="acc", bufs=4)
+            wcols = slice(i * P, (i + 1) * P)
+            for a in range(2):
+                nc.tensor.matmul_mx(
+                    out=acc[:],
+                    lhsT=w1_w[a][:, wcols].bitcast(FP8X4),
+                    lhsT_scale=w1_s[a][:, wcols],
+                    rhs=v_w[a][:, cols].bitcast(FP8X4),
+                    rhs_scale=v_s[a][:, cols],
+                    start=(a == 0),
+                    stop=(a == 1),
+                )
+            return acc
+
+        def multiply_h(acc, i, half):
+            cols = slice(half * BANK, (half + 1) * BANK)
+            nc.vector.tensor_tensor(h_ring[i % 2][:, cols], acc[:], damp_ring[i % 3][:, cols], ALU.mult)
+
+        def scatter(i, first, count):
+            t = i % PACK
+            factors = wgs4[0][:, 0, :] if t == 0 else wgs4[1][:, t - 1, :]
+            cols = slice(first, first + count)
+            nc.vector.tensor_tensor(
+                pages[i][:].indirect(entries(idx2, first, count)), h_ring[i % 2][:, cols], factors[:, cols], ALU.mult
+            )
+
+        def fetch_exemplar(dst, i, first, count):
+            nc.vector.tensor_copy(dst, pages[i][:].indirect(entries(idx4, first, count)))
+
+        def fetch_difference(dst, exemplar, i, first, count):
+            nc.vector.tensor_tensor(dst, pages[i][:].indirect(entries(idx3, first, count)), exemplar, ALU.subtract)
+
+        z_w = [sb("z_w%d" % g, [P, M], U32) for g in range(2)]
+        z_s = [sb("z_s%d" % g, [P, M], U8) for g in range(2)]
+
+        def quantize_z(z, grouped, g, first, count):
+            nc.scalar.copy(
+                out=grouped.rearrange("p (c i t) -> p c t i", i=4, t=PACK),
+                in_=z.rearrange("p (t c i) -> p c t i", i=4, t=PACK),
+            )
+            cols = slice(first, first + count)
+            nc.vector.quantize_mx(out=z_w[g][:, cols].bitcast(FP8X4), scales=z_s[g][:, cols], in_=grouped)
+
+        gather_words(0)
+        gather_words(1)
+        gather_scales(0)
+        gather_scales(1)
+        quantize_w1(0, 0, False)
+        b_abs0 = sb("b_abs0", [P, 8, PASS], F32, tag="b_abs")
+        for jb in range(4):
+            abs_b(b_abs0, 0, jb)
+        quantize_w1(1, 0, True)
+        multiply_h(make_h(b_abs0, 0, 0, b_abs0[:, 4, :]), 0, 0)
+        scatter(0, 0, BANK)
+        for jb in range(4, 8):
+            abs_b(b_abs0, 0, jb)
+        multiply_h(make_h(b_abs0, 0, 1), 0, 1)
+        scatter(0, BANK, BANK)
+
+        z0 = sb("z0", [P, PACK * M], F32)
+        b_abs1 = None
+        for i in range(PACK):
+            if i == PACK - 1:
+                b_abs1 = sb("b_abs1", [P, 8, PASS], F32, tag="b_abs")
+                for jb in range(8):
+                    abs_b(b_abs1, 1, jb)
+            b_next = b_abs1 if i == PACK - 1 else b_abs0
+            accs = [make_h(b_next, i + 1, half) for half in range(2)]
+            multiply_h(accs[0], i + 1, 0)
+            fetch_exemplar(root[:], i, 0, M)
+            multiply_h(accs[1], i + 1, 1)
+            fetch_difference(z0[:, i * M : (i + 1) * M], root[:], i, 0, M)
+            scatter(i + 1, 0, S)
+            if i < 2:
+                load_page(6 + i)
+                quantize_w1(i, 1, False)
+
+        w3_w = sb("w3_w", [P, 2, N], I32)
+        w3_s = sb("w3_s", [P, N], U8)
+        nc.vector.tensor_copy(
+            out=w3_w[:].rearrange("p a (t m) -> p a t m", t=PACK),
+            in_=w3_w_raw[:].rearrange("p a (m t) -> p a t m", t=PACK),
+        )
+        nc.vector.tensor_copy(
+            out=w3_s[:].rearrange("p (t m) -> p t m", t=PACK),
+            in_=w3_s_raw[:].rearrange("p (m t) -> p t m", t=PACK),
+        )
+
+        for i in range(PACK + 1, 2 * PACK):
+            for half in range(2):
+                multiply_h(make_h(b_abs1, i, half), i, half)
+            scatter(i, 0, S)
+
+        z0_bf = sb("z0_bf", [P, PACK * M], BF16, tag="b_abs")
+        quantize_z(z0[:], z0_bf[:], 0, 0, M)
+
+        y_w = sb("y_w", [P, M], U32)
+        y_s = sb("y_s", [P, M], U8)
+        y_rows = out_0.rearrange("(p t) m -> p t m", t=PACK)
+        y_words = out_1[0].rearrange("p m t -> p (m t)").bitcast(I32)
+        last = 2 * PACK - 1
+        exemplar4 = h_ring[last % 2]
+        z1 = sb("z1", [P, PACK * CHUNK], F32)
+        def finish(first, count, z):
+            cols = slice(first, first + count)
+            z_bf = sb("z1_bf%d" % first, [P, PACK * count], BF16, tag="bf", bufs=3)
+            quantize_z(z, z_bf[:], 1, first, count)
+            y = sb("y%d" % first, [P, PACK, count], F32, tag="w1_then_y", bufs=3)
+            y_bf = sb("y_bf%d" % first, [P, count * PACK], BF16, tag="bf", bufs=3)
+            for u in range(count // UNIT):
+                ucols = slice(first + u * UNIT, first + (u + 1) * UNIT)
+                acc = psum.tile([P, PACK, UNIT], F32, name="y_acc", tag=("b_bank", "turned")[(first // UNIT + u) % 2])
+                for g in range(2):
+                    for t in range(PACK):
+                        nc.tensor.matmul_mx(
+                            out=acc[:, t, :],
+                            lhsT=w3_w[:, g, t * P : (t + 1) * P].bitcast(FP8X4),
+                            lhsT_scale=w3_s[4 * g : P, t * P : (t + 1) * P],
+                            rhs=z_w[g][:, ucols].bitcast(FP8X4),
+                            rhs_scale=z_s[g][:, ucols],
+                            start=(g == 0 and t == 0),
+                            stop=(g == 1 and t == PACK - 1),
+                        )
+                nc.scalar.activation(
+                    out=y_bf[:, u * UNIT * PACK : (u + 1) * UNIT * PACK].rearrange("p (m t) -> p m t", t=PACK),
+                    in_=acc[:].rearrange("p t m -> p m t"),
+                    func=ACT.Abs,
+                )
+                nc.scalar.activation(out=y[:, :, u * UNIT : (u + 1) * UNIT], in_=acc[:], func=ACT.Abs)
+            nc.vector.quantize_mx(out=y_w[:, cols].bitcast(FP8X4), scales=y_s[:, cols], in_=y_bf[:])
+            nc.sync.dma_start(out=y_rows[:, :, cols], in_=y[:])
+            nc.sync.dma_start(out=y_words[:, cols], in_=y_w[:, cols].bitcast(I32))
+
+        chunks = M // CHUNK
+        for c in range(chunks):
+            for t in range(PACK):
+                fetch_exemplar(exemplar4[:, t * CHUNK : (t + 1) * CHUNK], PACK + t, c * CHUNK, CHUNK)
+            count = UNIT if c == chunks - 1 else CHUNK
+            for start in range(0, CHUNK, count):
+                z = z1[:, PACK * start : PACK * (start + count)]
+                for t in range(PACK):
+                    fetch_difference(
+                        z[:, t * count : (t + 1) * count],
+                        exemplar4[:, t * CHUNK + start : t * CHUNK + start + count],
+                        PACK + t,
+                        c * CHUNK + start,
+                        count,
+                    )
+                finish(c * CHUNK + start, count, z)
+        for q in range(4):
+            nc.sync.dma_start(
+                out=out_2[0, 4 * q : 4 * q + 4, :].bitcast(I32), in_=y_s[32 * q : 32 * q + 4, :].bitcast(I32)
+            )

@@ -33,7 +33,7 @@ def tile_list_stemma_deviation_kernel(
     nc = tc.nc
     with ExitStack() as ctx:
         keep = ctx.enter_context(tc.tile_pool(name="keep", bufs=1))
-        psum = ctx.enter_context(tc.psum_pool(name="psum", bufs=2))
+        psum = ctx.enter_context(tc.psum_pool(name="psum", bufs=1))
 
         def sb(name, shape, dtype, tag=None, bufs=1):
             return keep.tile(shape, dtype, name=name, tag=tag or name, bufs=bufs, align_bytes=64)
@@ -49,7 +49,7 @@ def tile_list_stemma_deviation_kernel(
         w3_s_raw = sb("w3_s_raw", [P, N], U8)
         nc.vector.memset(tab_s[:].bitcast(I32), 0)
         nc.gpsimd.memset(w2_s[:].bitcast(I32), 0)
-        nc.gpsimd.memset(w3_s_raw[:].bitcast(I32), 0)
+        nc.vector.memset(w3_s_raw[:].bitcast(I32), 0)
         ident = sb("ident", [P, P], F32)
         make_identity(nc, ident[:])
         warm = sb("warm", [P, 1], F32)
@@ -57,7 +57,8 @@ def tile_list_stemma_deviation_kernel(
 
         tab_w = [sb("tab_w%d" % a, [P, T], I32) for a in range(2)]
         w2_w = [sb("w2_w%d" % g, [P, 2, 2 * PASS], U8) for g in range(2)]
-        wgs4 = [sb("wgs_first", [P, 1, S], F32), sb("wgs_rest", [P, 3, S], F32)]
+        wgs4 = [sb("wgs_t%d" % t, [P, S], F32) for t in range(2)]
+        wgs_rows = sb("wgs_rows", [P, S], F32)
         w3_w_raw = sb("w3_w_raw", [P, 2, N], I32)
 
         def load_tab_words(a):
@@ -66,9 +67,9 @@ def tile_list_stemma_deviation_kernel(
                 in_=tab_words[a].rearrange("p t i -> p (t i)").bitcast(I32),
             )
 
-        def load_scale_rows(dst, src):
+        def load_scale_rows(queue, dst, src):
             for q in range(4):
-                nc.sync.dma_start(
+                queue.dma_start(
                     out=dst[32 * q : 32 * q + 4, :].bitcast(I32).rearrange("r (a c) -> r a c", a=2),
                     in_=src[:, 4 * q : 4 * q + 4, :].bitcast(I32).rearrange("a r c -> r a c"),
                 )
@@ -82,51 +83,50 @@ def tile_list_stemma_deviation_kernel(
         w1_raw = {}
 
         def load_w1(a, g):
-            if (a, g) == (0, 0):
-                raw = sb("w1_raw00", [P, PACK, PASS], F32, tag="b_abs")
-            else:
-                raw = sb("w1_raw%d%d" % (a, g), [P, PACK, PASS], F32, tag="w1_then_y", bufs=3)
+            tag = {(0, 0): "b_abs", (1, 0): "slot0", (0, 1): "slot1", (1, 1): "slot2"}[a, g]
+            raw = sb("w1_raw%d%d" % (a, g), [P, PACK, PASS], F32, tag=tag)
             nc.sync.dma_start(
                 out=raw[:],
                 in_=w1[a * PASS : (a + 1) * PASS, g * PASS : (g + 1) * PASS].rearrange("(p i) c -> p i c", i=PACK),
             )
             w1_raw[a, g] = raw
 
-        def load_wgs(dst, t0, t1):
+        def load_wgs(t):
             rows = wgs.rearrange("(q t) j -> q t j", t=PACK)
             for quad in range(4):
-                nc.sync.dma_start(out=dst[32 * quad : 32 * quad + 32, :, :], in_=rows[:, t0:t1, :])
+                nc.sync.dma_start(out=wgs4[t][32 * quad : 32 * quad + 32, :], in_=rows[:, t, :])
 
         pages = {}
 
         def load_page(i):
             g, t = divmod(i, PACK)
-            page = sb("page%d" % i, [P, T2], F32, tag="page", bufs=6)
+            page = sb("page%d" % i, [P, T2], F32, tag="page", bufs=5)
             nc.sync.dma_start(
                 out=page[:],
                 in_=page0[g * PASS : (g + 1) * PASS, :].rearrange("(p t) c -> t p c", t=PACK)[t],
             )
             pages[i] = page
 
+        load_scale_rows(nc.sync, w2_s, w2_scales)
         nc.sync.dma_start(idx[:], offs)
         load_tab_words(0)
         load_tab_words(1)
-        load_scale_rows(tab_s, tab_scales)
-        load_w2_words(0)
-        load_scale_rows(w2_s, w2_scales)
         load_w1(0, 0)
+        load_scale_rows(nc.sync, tab_s, tab_scales)
+        load_w2_words(0)
         load_w1(1, 0)
-        nc.sync.dma_start(idx2[:], offs2)
-        load_wgs(wgs4[0], 0, 1)
+        load_wgs(0)
         load_page(0)
+        nc.sync.dma_start(idx2[:], offs2)
         nc.sync.dma_start(idx4[:], offs4)
         nc.sync.dma_start(idx3[:], offs3)
+        load_wgs(1)
         load_page(1)
-        load_wgs(wgs4[1], 1, 4)
-        load_w2_words(1)
+        nc.sync.dma_start(out=wgs_rows[:], in_=wgs)
         load_w1(0, 1)
         load_w1(1, 1)
         load_page(2)
+        load_w2_words(1)
         nc.sync.dma_start(
             out=w3_w_raw[:],
             in_=w3_words.rearrange("a p c i -> p a (c i)").bitcast(I32),
@@ -136,7 +136,7 @@ def tile_list_stemma_deviation_kernel(
                 out=w3_s_raw[32 * q : 32 * q + 8, :].bitcast(I32),
                 in_=w3_scales[:, 4 * q : 4 * q + 4, :].bitcast(I32),
             )
-        for i in range(3, 6):
+        for i in range(3, 5):
             load_page(i)
 
         v_w = [sb("v_w%d" % a, [P, S], U32) for a in range(2)]
@@ -151,8 +151,14 @@ def tile_list_stemma_deviation_kernel(
             for a in range(2):
                 nc.vector.tensor_copy(v_s[a][:, cols], tab_s[:, a * T : (a + 1) * T].indirect(picks))
 
-        def abs_b(b_abs, g, jb):
-            bank = psum.tile([P, BANK], F32, name="b_bank", tag="b_bank")
+        def take_bank(k, name):
+            return psum.tile([P, BANK], F32, name=name, tag="bank%d" % k)
+
+        def turn_bank(half):
+            return take_bank(6 + half, "turned")
+
+        def abs_b(dst, g, jb, k):
+            bank = take_bank(k, "b_bank")
             cols = slice(jb * P, (jb + 1) * P)
             for a in range(2):
                 nc.tensor.matmul_mx(
@@ -165,49 +171,37 @@ def tile_list_stemma_deviation_kernel(
                     stop=(a == 1),
                 )
             nc.scalar.activation(
-                out=b_abs[:, jb, :].rearrange("j (t p) -> j t p", t=PACK),
+                out=dst.rearrange("j (t p) -> j t p", t=PACK),
                 in_=bank[:].rearrange("j (p t) -> j t p", t=PACK),
                 func=ACT.Abs,
             )
 
-        w1_w = [sb("w1_w%d" % a, [P, H], U32) for a in range(2)]
-        w1_s = [sb("w1_s%d" % a, [P, H], U8) for a in range(2)]
+        w1_w = [sb("w1_w%d" % g, [P, 2 * PASS], U32) for g in range(2)]
+        w1_s = [sb("w1_s%d" % g, [P, 2 * PASS], U8) for g in range(2)]
 
-        def quantize_w1(a, g, on_vector):
-            grouped = sb("w1_bf%d%d" % (a, g), [P, PASS * PACK], BF16, tag="bf", bufs=3)
-            src = w1_raw[a, g][:].rearrange("p i (m t) -> p m t i", t=PACK)
-            dst = grouped[:].rearrange("p (t m i) -> p m t i", t=PACK, i=PACK)
-            if on_vector:
-                nc.vector.tensor_copy(out=dst, in_=src)
-            else:
-                nc.scalar.copy(out=dst, in_=src)
-            cols = slice(g * PASS, (g + 1) * PASS)
-            nc.vector.quantize_mx(out=w1_w[a][:, cols].bitcast(FP8X4), scales=w1_s[a][:, cols], in_=grouped[:])
+        def round_w1(a, g, grouped, copy):
+            copy(
+                out=grouped.rearrange("p (t m i) -> p m t i", t=PACK, i=PACK),
+                in_=w1_raw[a, g][:].rearrange("p i (m t) -> p m t i", t=PACK),
+            )
+
+        def quantize_w1(g, first, count, grouped):
+            cols = slice(first, first + count)
+            nc.vector.quantize_mx(out=w1_w[g][:, cols].bitcast(FP8X4), scales=w1_s[g][:, cols], in_=grouped)
 
         damp_ring = [sb("damp%d" % i, [P, S], F32) for i in range(3)]
-        root = sb("root", [P, S], F32)
         h_ring = [sb("h%d" % i, [P, S], F32) for i in range(2)]
 
-        def make_h(b_abs, i, half, root_half=None):
-            g, t = divmod(i, PACK)
+        def product_a(i, half, k):
             cols = slice(half * BANK, (half + 1) * BANK)
-            turned = psum.tile([P, BANK], F32, name="turned", tag="turned")
-            for q in range(4):
-                nc.tensor.transpose(
-                    turned[:, q * P : (q + 1) * P], b_abs[:, half * 4 + q, t * P : (t + 1) * P], ident[:]
-                )
-            if root_half is None:
-                root_half = root[:, cols]
-            nc.scalar.activation(out=root_half, in_=turned[:], func=ACT.Abs_reciprocal_sqrt, bias=1.0)
-            damp = damp_ring[i % 3]
-            nc.scalar.activation(out=damp[:, cols], in_=root_half, func=ACT.Square)
-            acc = psum.tile([P, BANK], F32, name="acc", tag="acc", bufs=4)
-            wcols = slice(i * P, (i + 1) * P)
+            acc = take_bank(k, "acc")
+            g, t = divmod(i, PACK)
             for a in range(2):
+                wcols = slice(a * PASS + t * P, a * PASS + (t + 1) * P)
                 nc.tensor.matmul_mx(
                     out=acc[:],
-                    lhsT=w1_w[a][:, wcols].bitcast(FP8X4),
-                    lhsT_scale=w1_s[a][:, wcols],
+                    lhsT=w1_w[g][:, wcols].bitcast(FP8X4),
+                    lhsT_scale=w1_s[g][:, wcols],
                     rhs=v_w[a][:, cols].bitcast(FP8X4),
                     rhs_scale=v_s[a][:, cols],
                     start=(a == 0),
@@ -215,16 +209,43 @@ def tile_list_stemma_deviation_kernel(
                 )
             return acc
 
+        def blocks(ap):
+            return ap.rearrange("p (b j) -> p b j", j=P)
+
+        def damp_by_root(b_abs, i, half, root_half):
+            cols = slice(half * BANK, (half + 1) * BANK)
+            turned = turn_bank(half)
+            for q in range(4):
+                nc.tensor.transpose(
+                    turned[:, q * P : (q + 1) * P], b_abs[:, half * 4 + q, i * P : (i + 1) * P], ident[:]
+                )
+            nc.scalar.activation(out=root_half, in_=blocks(turned[:]), func=ACT.Abs_reciprocal_sqrt, bias=1.0)
+            nc.scalar.activation(out=blocks(damp_ring[i % 3][:, cols]), in_=root_half, func=ACT.Square)
+            return product_a(i, half, (3, 5)[half])
+
         def multiply_h(acc, i, half):
             cols = slice(half * BANK, (half + 1) * BANK)
-            nc.vector.tensor_tensor(h_ring[i % 2][:, cols], acc[:], damp_ring[i % 3][:, cols], ALU.mult)
+            nc.vector.tensor_tensor(h_ring[i % 2][:, cols], acc[:], damp_ring[i][:, cols], ALU.mult)
 
-        def scatter(i, first, count):
+        def factor_by_logs(log_blocks, i, a_dst):
             t = i % PACK
-            factors = wgs4[0][:, 0, :] if t == 0 else wgs4[1][:, t - 1, :]
+            for half in range(2):
+                cols = slice(half * BANK, (half + 1) * BANK)
+                turned = turn_bank(half)
+                for q in range(4):
+                    block = turned[:, q * P : (q + 1) * P]
+                    neg = neg_log_w[half][:, (t * 4 + q) * P : (t * 4 + q + 1) * P]
+                    nc.tensor.matmul(block, log_blocks(half * 4 + q), ident[:], start=True, stop=False, is_transpose=True)
+                    nc.tensor.matmul(block, neg, ident[:], start=False, stop=True, is_transpose=True)
+                nc.scalar.activation(out=damp_ring[i % 3][:, cols], in_=turned[:], func=ACT.Exp, scale=-1.0)
+            for half in range(2):
+                cols = slice(half * BANK, (half + 1) * BANK)
+                nc.scalar.copy(out=a_dst[:, cols], in_=product_a(i, half, 6 + half)[:])
+
+        def scatter(i, values, factors, first, count):
             cols = slice(first, first + count)
             nc.vector.tensor_tensor(
-                pages[i][:].indirect(entries(idx2, first, count)), h_ring[i % 2][:, cols], factors[:, cols], ALU.mult
+                pages[i][:].indirect(entries(idx2, first, count)), values[:, cols], factors[:, cols], ALU.mult
             )
 
         def fetch_exemplar(dst, i, first, count):
@@ -236,8 +257,8 @@ def tile_list_stemma_deviation_kernel(
         z_w = [sb("z_w%d" % g, [P, M], U32) for g in range(2)]
         z_s = [sb("z_s%d" % g, [P, M], U8) for g in range(2)]
 
-        def quantize_z(z, grouped, g, first, count):
-            nc.scalar.copy(
+        def quantize_z(z, grouped, g, first, count, copy):
+            copy(
                 out=grouped.rearrange("p (c i t) -> p c t i", i=4, t=PACK),
                 in_=z.rearrange("p (t c i) -> p c t i", i=4, t=PACK),
             )
@@ -248,35 +269,82 @@ def tile_list_stemma_deviation_kernel(
         gather_words(1)
         gather_scales(0)
         gather_scales(1)
-        quantize_w1(0, 0, False)
+        w1_bf0 = sb("w1_bf0", [P, 2 * PASS * PACK], BF16, tag="exemplar0")
+        round_w1(0, 0, w1_bf0[:, 0 : PASS * PACK], nc.scalar.copy)
         b_abs0 = sb("b_abs0", [P, 8, PASS], F32, tag="b_abs")
         for jb in range(4):
-            abs_b(b_abs0, 0, jb)
-        quantize_w1(1, 0, True)
-        multiply_h(make_h(b_abs0, 0, 0, b_abs0[:, 4, :]), 0, 0)
-        scatter(0, 0, BANK)
-        for jb in range(4, 8):
-            abs_b(b_abs0, 0, jb)
-        multiply_h(make_h(b_abs0, 0, 1), 0, 1)
-        scatter(0, BANK, BANK)
+            abs_b(b_abs0[:, jb, :], 0, jb, jb)
+        round_w1(1, 0, w1_bf0[:, PASS * PACK : 2 * PASS * PACK], nc.vector.tensor_copy)
+        quantize_w1(0, 0, 2 * PASS, w1_bf0[:])
+        multiply_h(damp_by_root(b_abs0, 0, 0, b_abs0[:, 4:8, 0:P]), 0, 0)
+        scatter(0, h_ring[0], wgs4[0], 0, BANK)
+        for jb, k in zip(range(4, 8), (0, 1, 2, 4)):
+            abs_b(b_abs0[:, jb, :], 0, jb, k)
+        root = sb("root", [P, BANK], F32, tag="bf1")
+        multiply_h(damp_by_root(b_abs0, 0, 1, blocks(root[:])), 0, 1)
+        scatter(0, h_ring[0], wgs4[0], BANK, BANK)
 
         z0 = sb("z0", [P, PACK * M], F32)
-        b_abs1 = None
-        for i in range(PACK):
-            if i == PACK - 1:
-                b_abs1 = sb("b_abs1", [P, 8, PASS], F32, tag="b_abs")
-                for jb in range(8):
-                    abs_b(b_abs1, 1, jb)
-            b_next = b_abs1 if i == PACK - 1 else b_abs0
-            accs = [make_h(b_next, i + 1, half) for half in range(2)]
-            multiply_h(accs[0], i + 1, 0)
-            fetch_exemplar(root[:], i, 0, M)
-            multiply_h(accs[1], i + 1, 1)
-            fetch_difference(z0[:, i * M : (i + 1) * M], root[:], i, 0, M)
-            scatter(i + 1, 0, S)
-            if i < 2:
-                load_page(6 + i)
-                quantize_w1(i, 1, False)
+        z0_t = [z0[:, t * M : (t + 1) * M] for t in range(PACK)]
+        exemplars = [sb("exemplar%d" % k, [P, M], F32) for k in range(2)]
+        logs = sb("logs", [P, 3 * S], F32, tag="tab_s")
+        straddle = S - BANK // 2
+        acc0 = damp_by_root(b_abs0, 1, 0, blocks(root[:]))
+        acc1 = damp_by_root(b_abs0, 1, 1, blocks(logs[:, straddle : straddle + BANK]))
+        multiply_h(acc0, 1, 0)
+        fetch_exemplar(exemplars[0][:], 0, 0, M)
+        multiply_h(acc1, 1, 1)
+        fetch_difference(z0_t[0], exemplars[0][:], 0, 0, M)
+        scatter(1, h_ring[1], wgs4[1], 0, S)
+        load_page(5)
+        fetch_exemplar(exemplars[1][:], 1, 0, M)
+
+        log_w = logs[:, 0:S]
+        log_b0 = logs[:, S : 3 * S]
+        nc.scalar.activation(out=log_w, in_=wgs_rows[:], func=ACT.Ln)
+        nc.scalar.activation(
+            out=log_b0.rearrange("j (t b p) -> j b t p", t=2, b=8),
+            in_=b_abs0[:, :, 2 * P : 4 * P].rearrange("j b (t p) -> j b t p", t=2),
+            func=ACT.Ln,
+            bias=1.0,
+        )
+        neg_log_w = [sb("neg_log_w%d" % half, [P, PACK * BANK], F32, tag="tab_w%d" % half) for half in range(2)]
+        log_w_turned = []
+        for half in range(2):
+            bank = take_bank(half, "log_w_turned")
+            for q in range(4):
+                jb = half * 4 + q
+                nc.tensor.transpose(bank[:, q * P : (q + 1) * P], log_w[:, jb * P : (jb + 1) * P], ident[:])
+            log_w_turned.append(bank)
+
+        def spread_log_w(t):
+            for half in range(2):
+                src = log_w_turned[half][:].rearrange("j (b q t) -> j t b q", t=PACK, b=4)[:, t]
+                nc.scalar.activation(
+                    out=neg_log_w[half][:, t * BANK : (t + 1) * BANK].rearrange("j (b r q) -> j b r q", r=4, q=32),
+                    in_=src.unsqueeze(2).to_broadcast([P, 4, 4, 32]),
+                    func=ACT.Copy,
+                    scale=-1.0,
+                )
+
+        for i in (2, 3):
+            spread_log_w(i)
+            factor_by_logs(lambda jb: log_b0[:, ((i - 2) * 8 + jb) * P : ((i - 2) * 8 + jb + 1) * P], i, z0_t[i - 1])
+            scatter(i, z0_t[i - 1], damp_ring[i % 3], 0, S)
+            fetch_difference(z0_t[i - 1], exemplars[(i - 1) % 2][:], i - 1, 0, M)
+            load_page(4 + i)
+            fetch_exemplar(exemplars[i % 2][:], i, 0, M)
+            if i == 2:
+                for a in range(2):
+                    w1_bf1 = sb("w1_bf1%d" % a, [P, PASS * PACK], BF16, tag="bf%d" % (a + 1))
+                    round_w1(a, 1, w1_bf1[:], nc.scalar.copy)
+                    quantize_w1(1, a * PASS, PASS, w1_bf1[:])
+
+        log_b1 = [sb("log_b1_%d" % half, [P, 4, PASS], F32, tag="slot%d" % (half + 1)) for half in range(2)]
+        for jb, k in enumerate((2, 3, 4, 7, 5, 2, 3, 7)):
+            abs_b(log_b1[jb // 4][:, jb % 4, :], 1, jb, k)
+        for half in range(2):
+            nc.scalar.activation(out=log_b1[half][:], in_=log_b1[half][:], func=ACT.Ln, bias=1.0)
 
         w3_w = sb("w3_w", [P, 2, N], I32)
         w3_s = sb("w3_s", [P, N], U8)
@@ -289,13 +357,18 @@ def tile_list_stemma_deviation_kernel(
             in_=w3_s_raw[:].rearrange("p (m t) -> p t m", t=PACK),
         )
 
-        for i in range(PACK + 1, 2 * PACK):
-            for half in range(2):
-                multiply_h(make_h(b_abs1, i, half), i, half)
-            scatter(i, 0, S)
+        for i in range(PACK, 2 * PACK):
+            t = i - PACK
+            if t < 2:
+                spread_log_w(t)
+            a_dst = z0_t[PACK - 1] if t == 0 else h_ring[i % 2]
+            factor_by_logs(lambda jb: log_b1[jb // 4][:, jb % 4, t * P : (t + 1) * P], i, a_dst)
+            scatter(i, a_dst, damp_ring[i % 3], 0, S)
+            if t == 0:
+                fetch_difference(z0_t[PACK - 1], exemplars[1][:], PACK - 1, 0, M)
 
-        z0_bf = sb("z0_bf", [P, PACK * M], BF16, tag="b_abs")
-        quantize_z(z0[:], z0_bf[:], 0, 0, M)
+        z0_bf = sb("z0_bf", [P, PACK * M], BF16, tag="slot2")
+        quantize_z(z0[:], z0_bf[:], 0, 0, M, nc.scalar.copy)
 
         y_w = sb("y_w", [P, M], U32)
         y_s = sb("y_s", [P, M], U8)
@@ -306,13 +379,13 @@ def tile_list_stemma_deviation_kernel(
         z1 = sb("z1", [P, PACK * CHUNK], F32)
         def finish(first, count, z):
             cols = slice(first, first + count)
-            z_bf = sb("z1_bf%d" % first, [P, PACK * count], BF16, tag="bf", bufs=3)
-            quantize_z(z, z_bf[:], 1, first, count)
-            y = sb("y%d" % first, [P, PACK, count], F32, tag="w1_then_y", bufs=3)
-            y_bf = sb("y_bf%d" % first, [P, count * PACK], BF16, tag="bf", bufs=3)
+            z_bf = sb("z1_bf%d" % first, [P, PACK * count], BF16, tag="bf%d" % (first // UNIT % 2 * 2))
+            quantize_z(z, z_bf[:], 1, first, count, nc.scalar.copy if count == CHUNK else nc.vector.tensor_copy)
+            y = sb("y%d" % first, [P, PACK, count], F32, tag=("b_abs", "slot0", "slot1")[first // CHUNK % 3] if first % CHUNK == 0 else "slot2")
+            y_bf = sb("y_bf%d" % first, [P, count * PACK], BF16, tag="bf1" if first % CHUNK == 0 else "tab_s")
             for u in range(count // UNIT):
                 ucols = slice(first + u * UNIT, first + (u + 1) * UNIT)
-                acc = psum.tile([P, PACK, UNIT], F32, name="y_acc", tag=("b_bank", "turned")[(first // UNIT + u) % 2])
+                acc = take_bank(first // UNIT + u, "y_acc")[:].rearrange("p (t m) -> p t m", t=PACK)
                 for g in range(2):
                     for t in range(PACK):
                         nc.tensor.matmul_mx(
@@ -324,12 +397,18 @@ def tile_list_stemma_deviation_kernel(
                             start=(g == 0 and t == 0),
                             stop=(g == 1 and t == PACK - 1),
                         )
-                nc.scalar.activation(
-                    out=y_bf[:, u * UNIT * PACK : (u + 1) * UNIT * PACK].rearrange("p (m t) -> p m t", t=PACK),
-                    in_=acc[:].rearrange("p t m -> p m t"),
-                    func=ACT.Abs,
-                )
-                nc.scalar.activation(out=y[:, :, u * UNIT : (u + 1) * UNIT], in_=acc[:], func=ACT.Abs)
+                nc.scalar.activation(out=y[:, :, u * UNIT : (u + 1) * UNIT], in_=acc, func=ACT.Abs)
+                if count == CHUNK:
+                    nc.scalar.activation(
+                        out=y_bf[:, u * UNIT * PACK : (u + 1) * UNIT * PACK].rearrange("p (m t) -> p m t", t=PACK),
+                        in_=acc.rearrange("p t m -> p m t"),
+                        func=ACT.Abs,
+                    )
+                else:
+                    nc.vector.tensor_copy(
+                        out=y_bf[:].rearrange("p (c i t) -> p c t i", i=4, t=PACK),
+                        in_=y[:].rearrange("p t (c i) -> p c t i", i=4),
+                    )
             nc.vector.quantize_mx(out=y_w[:, cols].bitcast(FP8X4), scales=y_s[:, cols], in_=y_bf[:])
             nc.sync.dma_start(out=y_rows[:, :, cols], in_=y[:])
             nc.sync.dma_start(out=y_words[:, cols], in_=y_w[:, cols].bitcast(I32))

@@ -44,11 +44,13 @@ def tile_list_stemma_deviation_kernel(
         lists = [keep.tile([P, S // LIST_ROWS], U16, name="list%d" % i) for i in range(4)]
         idx, idx2, idx3, idx4 = lists
 
-        tab_s = sb("tab_s", [P, 2 * T], U8)
+        tab_s = sb("tab_s", [P, T], U8)
+        v_s_moved = sb("v_s_moved", [P, S], U8)
         w2_s = sb("w2_s", [P, 2 * H], U8)
         w3_s_raw = sb("w3_s_raw", [P, N], U8)
-        nc.vector.memset(tab_s[:].bitcast(I32), 0)
-        nc.gpsimd.memset(w2_s[:].bitcast(I32), 0)
+        nc.gpsimd.memset(tab_s[:].bitcast(I32), 0)
+        nc.vector.memset(w2_s[:].bitcast(I32), 0)
+        nc.vector.memset(v_s_moved[:].bitcast(I32), 0)
         nc.vector.memset(w3_s_raw[:].bitcast(I32), 0)
         ident = sb("ident", [P, P], F32)
         make_identity(nc, ident[:])
@@ -74,6 +76,12 @@ def tile_list_stemma_deviation_kernel(
                     in_=src[:, 4 * q : 4 * q + 4, :].bitcast(I32).rearrange("a r c -> r a c"),
                 )
 
+        def load_packed_scale_rows(dst, src):
+            for q in range(4):
+                nc.sync.dma_start(
+                    out=dst[32 * q : 32 * q + 8, :].bitcast(I32), in_=src[:, 4 * q : 4 * q + 4, :].bitcast(I32)
+                )
+
         def load_w2_words(g):
             nc.sync.dma_start(
                 out=w2_w[g][:].bitcast(I32),
@@ -83,7 +91,7 @@ def tile_list_stemma_deviation_kernel(
         w1_raw = {}
 
         def load_w1(a, g):
-            tag = {(0, 0): "b_abs", (1, 0): "slot0", (0, 1): "slot1", (1, 1): "slot2"}[a, g]
+            tag = {(0, 0): "z0", (1, 0): "slot0", (0, 1): "slot1", (1, 1): "slot2"}[a, g]
             raw = sb("w1_raw%d%d" % (a, g), [P, PACK, PASS], F32, tag=tag)
             nc.sync.dma_start(
                 out=raw[:],
@@ -107,49 +115,40 @@ def tile_list_stemma_deviation_kernel(
             )
             pages[i] = page
 
-        load_scale_rows(nc.sync, w2_s, w2_scales)
+        load_packed_scale_rows(tab_s, tab_scales)
         nc.sync.dma_start(idx[:], offs)
         load_tab_words(0)
         load_tab_words(1)
-        load_w1(0, 0)
-        load_scale_rows(nc.sync, tab_s, tab_scales)
         load_w2_words(0)
+        load_scale_rows(nc.sync, w2_s, w2_scales)
+        load_w1(0, 0)
+        v_s = sb("v_s", [P, S], U8)
+        nc.vector.tensor_copy(v_s[:], tab_s[:].indirect(idx[:]))
+        nc.sync.dma_start(out=v_s_moved[0:100, :].bitcast(I32), in_=v_s[4:104, :].bitcast(I32))
         load_w1(1, 0)
+        nc.sync.dma_start(idx2[:], offs2)
         load_wgs(0)
         load_page(0)
-        nc.sync.dma_start(idx2[:], offs2)
+        nc.sync.dma_start(out=w3_w_raw[:], in_=w3_words.rearrange("a p c i -> p a (c i)").bitcast(I32))
+        nc.sync.dma_start(out=wgs_rows[:], in_=wgs)
         nc.sync.dma_start(idx4[:], offs4)
         nc.sync.dma_start(idx3[:], offs3)
-        load_wgs(1)
         load_page(1)
-        nc.sync.dma_start(out=wgs_rows[:], in_=wgs)
+        load_wgs(1)
         load_w1(0, 1)
         load_w1(1, 1)
         load_page(2)
         load_w2_words(1)
-        nc.sync.dma_start(
-            out=w3_w_raw[:],
-            in_=w3_words.rearrange("a p c i -> p a (c i)").bitcast(I32),
-        )
-        for q in range(4):
-            nc.sync.dma_start(
-                out=w3_s_raw[32 * q : 32 * q + 8, :].bitcast(I32),
-                in_=w3_scales[:, 4 * q : 4 * q + 4, :].bitcast(I32),
-            )
+        load_packed_scale_rows(w3_s_raw, w3_scales)
         for i in range(3, 5):
             load_page(i)
 
         v_w = [sb("v_w%d" % a, [P, S], U32) for a in range(2)]
-        v_s = [sb("v_s%d" % a, [P, S], U8) for a in range(2)]
 
-        def gather_words(a):
-            nc.vector.tensor_copy(v_w[a][:], tab_w[a][:].bitcast(U32).indirect(idx[:]))
-
-        def gather_scales(half):
-            cols = slice(half * BANK, (half + 1) * BANK)
-            picks = entries(idx, half * BANK, BANK)
-            for a in range(2):
-                nc.vector.tensor_copy(v_s[a][:, cols], tab_s[:, a * T : (a + 1) * T].indirect(picks))
+        def gather_words(a, first, count):
+            nc.vector.tensor_copy(
+                v_w[a][:, first : first + count], tab_w[a][:].bitcast(U32).indirect(entries(idx, first, count))
+            )
 
         def take_bank(k, name):
             return psum.tile([P, BANK], F32, name=name, tag="bank%d" % k)
@@ -164,7 +163,7 @@ def tile_list_stemma_deviation_kernel(
                 nc.tensor.matmul_mx(
                     out=bank[:],
                     lhsT=v_w[a][:, cols].bitcast(FP8X4),
-                    lhsT_scale=v_s[a][:, cols],
+                    lhsT_scale=(v_s, v_s_moved)[a][:, cols],
                     rhs=w2_w[g][:, a, :].bitcast(FP4X4),
                     rhs_scale=w2_s[:, a * H + g * PASS : a * H + (g + 1) * PASS],
                     start=(a == 0),
@@ -203,7 +202,7 @@ def tile_list_stemma_deviation_kernel(
                     lhsT=w1_w[g][:, wcols].bitcast(FP8X4),
                     lhsT_scale=w1_s[g][:, wcols],
                     rhs=v_w[a][:, cols].bitcast(FP8X4),
-                    rhs_scale=v_s[a][:, cols],
+                    rhs_scale=v_s[4 * a : P, cols],
                     start=(a == 0),
                     stop=(a == 1),
                 )
@@ -221,13 +220,18 @@ def tile_list_stemma_deviation_kernel(
                 )
             nc.scalar.activation(out=root_half, in_=blocks(turned[:]), func=ACT.Abs_reciprocal_sqrt, bias=1.0)
             nc.scalar.activation(out=blocks(damp_ring[i % 3][:, cols]), in_=root_half, func=ACT.Square)
-            return product_a(i, half, (3, 5)[half])
+            return product_a(i, half, 3 + half)
 
-        def multiply_h(acc, i, half):
+        def multiply_h(dst, acc, i, half):
             cols = slice(half * BANK, (half + 1) * BANK)
-            nc.vector.tensor_tensor(h_ring[i % 2][:, cols], acc[:], damp_ring[i][:, cols], ALU.mult)
+            nc.vector.tensor_tensor(dst, acc[:], damp_ring[i][:, cols], ALU.mult)
 
-        def factor_by_logs(log_blocks, i, a_dst):
+        def copy_a(i, a_dst):
+            for half in range(2):
+                cols = slice(half * BANK, (half + 1) * BANK)
+                nc.scalar.copy(out=a_dst[:, cols], in_=product_a(i, half, 6 + half)[:])
+
+        def factor_by_logs(log_blocks, i):
             t = i % PACK
             for half in range(2):
                 cols = slice(half * BANK, (half + 1) * BANK)
@@ -238,14 +242,10 @@ def tile_list_stemma_deviation_kernel(
                     nc.tensor.matmul(block, log_blocks(half * 4 + q), ident[:], start=True, stop=False, is_transpose=True)
                     nc.tensor.matmul(block, neg, ident[:], start=False, stop=True, is_transpose=True)
                 nc.scalar.activation(out=damp_ring[i % 3][:, cols], in_=turned[:], func=ACT.Exp, scale=-1.0)
-            for half in range(2):
-                cols = slice(half * BANK, (half + 1) * BANK)
-                nc.scalar.copy(out=a_dst[:, cols], in_=product_a(i, half, 6 + half)[:])
 
         def scatter(i, values, factors, first, count):
-            cols = slice(first, first + count)
             nc.vector.tensor_tensor(
-                pages[i][:].indirect(entries(idx2, first, count)), values[:, cols], factors[:, cols], ALU.mult
+                pages[i][:].indirect(entries(idx2, first, count)), values, factors[:, first : first + count], ALU.mult
             )
 
         def fetch_exemplar(dst, i, first, count):
@@ -265,49 +265,59 @@ def tile_list_stemma_deviation_kernel(
             cols = slice(first, first + count)
             nc.vector.quantize_mx(out=z_w[g][:, cols].bitcast(FP8X4), scales=z_s[g][:, cols], in_=grouped)
 
-        gather_words(0)
-        gather_words(1)
-        gather_scales(0)
-        gather_scales(1)
+        gather_words(0, 0, S)
+        gather_words(1, 0, BANK)
+        gather_words(1, BANK, BANK)
         w1_bf0 = sb("w1_bf0", [P, 2 * PASS * PACK], BF16, tag="exemplar0")
-        round_w1(0, 0, w1_bf0[:, 0 : PASS * PACK], nc.scalar.copy)
+        for a in range(2):
+            part = w1_bf0[:, a * PASS * PACK : (a + 1) * PASS * PACK]
+            round_w1(a, 0, part, nc.vector.tensor_copy)
+            quantize_w1(0, a * PASS, PASS, part)
         b_abs0 = sb("b_abs0", [P, 8, PASS], F32, tag="b_abs")
         for jb in range(4):
             abs_b(b_abs0[:, jb, :], 0, jb, jb)
-        round_w1(1, 0, w1_bf0[:, PASS * PACK : 2 * PASS * PACK], nc.vector.tensor_copy)
-        quantize_w1(0, 0, 2 * PASS, w1_bf0[:])
-        multiply_h(damp_by_root(b_abs0, 0, 0, b_abs0[:, 4:8, 0:P]), 0, 0)
-        scatter(0, h_ring[0], wgs4[0], 0, BANK)
+
+        w3_w = sb("w3_w", [P, 2, N], I32)
+        w3_s = sb("w3_s", [P, N], U8)
+        nc.vector.tensor_copy(
+            out=w3_w[:].rearrange("p a (t m) -> p a m t", t=PACK),
+            in_=w3_w_raw[:].rearrange("p a (m t) -> p a m t", t=PACK),
+        )
+        nc.vector.tensor_copy(
+            out=w3_s[:].rearrange("p (t m) -> p m t", t=PACK),
+            in_=w3_s_raw[:].rearrange("p (m t) -> p m t", t=PACK),
+        )
+
+        h_halves = [h_ring[1][:, 0:BANK], h_ring[1][:, BANK:S]]
+        multiply_h(h_halves[0], damp_by_root(b_abs0, 0, 0, b_abs0[:, 4:8, 0:P]), 0, 0)
+        scatter(0, h_halves[0], wgs4[0], 0, BANK)
         for jb, k in zip(range(4, 8), (0, 1, 2, 4)):
             abs_b(b_abs0[:, jb, :], 0, jb, k)
         root = sb("root", [P, BANK], F32, tag="bf1")
-        multiply_h(damp_by_root(b_abs0, 0, 1, blocks(root[:])), 0, 1)
-        scatter(0, h_ring[0], wgs4[0], BANK, BANK)
+        multiply_h(h_halves[0], damp_by_root(b_abs0, 0, 1, blocks(root[:])), 0, 1)
+        scatter(0, h_halves[0], wgs4[0], BANK, BANK)
 
         z0 = sb("z0", [P, PACK * M], F32)
         z0_t = [z0[:, t * M : (t + 1) * M] for t in range(PACK)]
         exemplars = [sb("exemplar%d" % k, [P, M], F32) for k in range(2)]
         logs = sb("logs", [P, 3 * S], F32, tag="tab_s")
-        straddle = S - BANK // 2
         acc0 = damp_by_root(b_abs0, 1, 0, blocks(root[:]))
-        acc1 = damp_by_root(b_abs0, 1, 1, blocks(logs[:, straddle : straddle + BANK]))
-        multiply_h(acc0, 1, 0)
+        acc1 = damp_by_root(b_abs0, 1, 1, blocks(logs[:])[:, 0:24:7, :])
+        multiply_h(h_halves[0], acc0, 1, 0)
         fetch_exemplar(exemplars[0][:], 0, 0, M)
-        multiply_h(acc1, 1, 1)
+        multiply_h(h_halves[1], acc1, 1, 1)
         fetch_difference(z0_t[0], exemplars[0][:], 0, 0, M)
-        scatter(1, h_ring[1], wgs4[1], 0, S)
+        scatter(1, h_ring[1][:], wgs4[1], 0, S)
         load_page(5)
         fetch_exemplar(exemplars[1][:], 1, 0, M)
 
         log_w = logs[:, 0:S]
         log_b0 = logs[:, S : 3 * S]
         nc.scalar.activation(out=log_w, in_=wgs_rows[:], func=ACT.Ln)
-        nc.scalar.activation(
-            out=log_b0.rearrange("j (t b p) -> j b t p", t=2, b=8),
-            in_=b_abs0[:, :, 2 * P : 4 * P].rearrange("j b (t p) -> j b t p", t=2),
-            func=ACT.Ln,
-            bias=1.0,
-        )
+        for t in (2, 3):
+            nc.scalar.activation(
+                out=blocks(log_b0[:, (t - 2) * S : (t - 1) * S]), in_=b_abs0[:, :, t * P : (t + 1) * P], func=ACT.Ln, bias=1.0
+            )
         neg_log_w = [sb("neg_log_w%d" % half, [P, PACK * BANK], F32, tag="tab_w%d" % half) for half in range(2)]
         log_w_turned = []
         for half in range(2):
@@ -328,8 +338,9 @@ def tile_list_stemma_deviation_kernel(
                 )
 
         for i in (2, 3):
+            copy_a(i, z0_t[i - 1])
             spread_log_w(i)
-            factor_by_logs(lambda jb: log_b0[:, ((i - 2) * 8 + jb) * P : ((i - 2) * 8 + jb + 1) * P], i, z0_t[i - 1])
+            factor_by_logs(lambda jb: log_b0[:, ((i - 2) * 8 + jb) * P : ((i - 2) * 8 + jb + 1) * P], i)
             scatter(i, z0_t[i - 1], damp_ring[i % 3], 0, S)
             fetch_difference(z0_t[i - 1], exemplars[(i - 1) % 2][:], i - 1, 0, M)
             load_page(4 + i)
@@ -346,23 +357,13 @@ def tile_list_stemma_deviation_kernel(
         for half in range(2):
             nc.scalar.activation(out=log_b1[half][:], in_=log_b1[half][:], func=ACT.Ln, bias=1.0)
 
-        w3_w = sb("w3_w", [P, 2, N], I32)
-        w3_s = sb("w3_s", [P, N], U8)
-        nc.vector.tensor_copy(
-            out=w3_w[:].rearrange("p a (t m) -> p a t m", t=PACK),
-            in_=w3_w_raw[:].rearrange("p a (m t) -> p a t m", t=PACK),
-        )
-        nc.vector.tensor_copy(
-            out=w3_s[:].rearrange("p (t m) -> p t m", t=PACK),
-            in_=w3_s_raw[:].rearrange("p (m t) -> p t m", t=PACK),
-        )
-
         for i in range(PACK, 2 * PACK):
             t = i - PACK
             if t < 2:
                 spread_log_w(t)
-            a_dst = z0_t[PACK - 1] if t == 0 else h_ring[i % 2]
-            factor_by_logs(lambda jb: log_b1[jb // 4][:, jb % 4, t * P : (t + 1) * P], i, a_dst)
+            a_dst = z0_t[PACK - 1] if t == 0 else h_ring[i % 2][:]
+            factor_by_logs(lambda jb: log_b1[jb // 4][:, jb % 4, t * P : (t + 1) * P], i)
+            copy_a(i, a_dst)
             scatter(i, a_dst, damp_ring[i % 3], 0, S)
             if t == 0:
                 fetch_difference(z0_t[PACK - 1], exemplars[1][:], PACK - 1, 0, M)

@@ -4,7 +4,7 @@ import concourse.mybir as mybir
 from concourse.masks import make_identity
 
 K, H, N, T, S, T2, M = 1024, 1024, 512, 2048, 1024, 2048, 1024
-FLOPS = 2 * K * H * S * 2 + 2 * H * N * M
+FLOPS = 2 * (2 * K * H * S) + 2 * H * N * M
 
 F32 = mybir.dt.float32
 BF16 = mybir.dt.bfloat16
@@ -21,9 +21,15 @@ P = 128
 PACK = 4
 PASS = P * PACK
 BANK = 512
+BLOCKS = S // P
+LINE = 4
+QUAD = 32
+LIST_ROWS = 16
+PAGE_SLOTS = 5
 CHUNK = 256
 UNIT = 128
-LIST_ROWS = 16
+A_BANK = 3
+TURN_BANK = 6
 
 
 def tile_list_stemma_deviation_kernel(
@@ -38,11 +44,19 @@ def tile_list_stemma_deviation_kernel(
         def sb(name, shape, dtype, tag=None, bufs=1):
             return keep.tile(shape, dtype, name=name, tag=tag or name, bufs=bufs, align_bytes=64)
 
+        def take_bank(k, name):
+            return psum.tile([P, BANK], F32, name=name, tag="bank%d" % k)
+
         def entries(lst, first, count):
             return lst[:, first // LIST_ROWS : (first + count) // LIST_ROWS]
 
-        lists = [keep.tile([P, S // LIST_ROWS], U16, name="list%d" % i) for i in range(4)]
-        idx, idx2, idx3, idx4 = lists
+        def half_cols(half):
+            return slice(half * BANK, (half + 1) * BANK)
+
+        def blocks(ap):
+            return ap.rearrange("p (b j) -> p b j", j=P)
+
+        idx, idx2, idx3, idx4 = [keep.tile([P, S // LIST_ROWS], U16, name="list%d" % i) for i in range(4)]
 
         tab_s = sb("tab_s", [P, T], U8)
         v_s_moved = sb("v_s_moved", [P, S], U8)
@@ -59,27 +73,26 @@ def tile_list_stemma_deviation_kernel(
 
         tab_w = [sb("tab_w%d" % a, [P, T], I32) for a in range(2)]
         w2_w = [sb("w2_w%d" % g, [P, 2, 2 * PASS], U8) for g in range(2)]
-        wgs4 = [sb("wgs_t%d" % t, [P, S], F32) for t in range(2)]
+        wgs_dealt = [sb("wgs_t%d" % t, [P, S], F32) for t in range(2)]
         wgs_rows = sb("wgs_rows", [P, S], F32)
         w3_w_raw = sb("w3_w_raw", [P, 2, N], I32)
+        w1_raw = {}
+        pages = {}
 
         def load_tab_words(a):
-            nc.sync.dma_start(
-                out=tab_w[a][:],
-                in_=tab_words[a].rearrange("p t i -> p (t i)").bitcast(I32),
-            )
+            nc.sync.dma_start(out=tab_w[a][:], in_=tab_words[a].rearrange("p t i -> p (t i)").bitcast(I32))
 
-        def load_scale_rows(queue, dst, src):
-            for q in range(4):
-                queue.dma_start(
-                    out=dst[32 * q : 32 * q + 4, :].bitcast(I32).rearrange("r (a c) -> r a c", a=2),
-                    in_=src[:, 4 * q : 4 * q + 4, :].bitcast(I32).rearrange("a r c -> r a c"),
-                )
-
-        def load_packed_scale_rows(dst, src):
+        def load_packed_scales(dst, src):
             for q in range(4):
                 nc.sync.dma_start(
-                    out=dst[32 * q : 32 * q + 8, :].bitcast(I32), in_=src[:, 4 * q : 4 * q + 4, :].bitcast(I32)
+                    out=dst[QUAD * q : QUAD * q + 8, :].bitcast(I32), in_=src[:, 4 * q : 4 * q + 4, :].bitcast(I32)
+                )
+
+        def load_w2_scales():
+            for q in range(4):
+                nc.sync.dma_start(
+                    out=w2_s[QUAD * q : QUAD * q + 4, :].bitcast(I32).rearrange("r (a c) -> r a c", a=2),
+                    in_=w2_scales[:, 4 * q : 4 * q + 4, :].bitcast(I32).rearrange("a r c -> r a c"),
                 )
 
         def load_w2_words(g):
@@ -88,75 +101,74 @@ def tile_list_stemma_deviation_kernel(
                 in_=w2_words[:, :, g * 2 * PASS : (g + 1) * 2 * PASS].bitcast(I32).rearrange("a p c -> p a c"),
             )
 
-        w1_raw = {}
-
-        def load_w1(a, g):
-            tag = {(0, 0): "z0", (1, 0): "slot0", (0, 1): "slot1", (1, 1): "slot2"}[a, g]
-            raw = sb("w1_raw%d%d" % (a, g), [P, PACK, PASS], F32, tag=tag)
+        def load_w1(a, g, tag):
+            w1_raw[a, g] = sb("w1_raw%d%d" % (a, g), [P, PACK, PASS], F32, tag=tag)
             nc.sync.dma_start(
-                out=raw[:],
+                out=w1_raw[a, g][:],
                 in_=w1[a * PASS : (a + 1) * PASS, g * PASS : (g + 1) * PASS].rearrange("(p i) c -> p i c", i=PACK),
             )
-            w1_raw[a, g] = raw
 
-        def load_wgs(t):
+        def load_wgs_dealt(t):
             rows = wgs.rearrange("(q t) j -> q t j", t=PACK)
             for quad in range(4):
-                nc.sync.dma_start(out=wgs4[t][32 * quad : 32 * quad + 32, :], in_=rows[:, t, :])
-
-        pages = {}
+                nc.sync.dma_start(out=wgs_dealt[t][QUAD * quad : QUAD * (quad + 1), :], in_=rows[:, t, :])
 
         def load_page(i):
             g, t = divmod(i, PACK)
-            page = sb("page%d" % i, [P, T2], F32, tag="page", bufs=5)
+            pages[i] = sb("page%d" % i, [P, T2], F32, tag="page", bufs=PAGE_SLOTS)
             nc.sync.dma_start(
-                out=page[:],
-                in_=page0[g * PASS : (g + 1) * PASS, :].rearrange("(p t) c -> t p c", t=PACK)[t],
+                out=pages[i][:], in_=page0[g * PASS : (g + 1) * PASS, :].rearrange("(p t) c -> t p c", t=PACK)[t]
             )
-            pages[i] = page
 
-        load_packed_scale_rows(tab_s, tab_scales)
+        load_packed_scales(tab_s, tab_scales)
         nc.sync.dma_start(idx[:], offs)
         load_tab_words(0)
         load_tab_words(1)
         load_w2_words(0)
-        load_scale_rows(nc.sync, w2_s, w2_scales)
-        load_w1(0, 0)
+        load_w2_scales()
+        load_w1(0, 0, "z0")
         v_s = sb("v_s", [P, S], U8)
         nc.vector.tensor_copy(v_s[:], tab_s[:].indirect(idx[:]))
-        nc.sync.dma_start(out=v_s_moved[0:100, :].bitcast(I32), in_=v_s[4:104, :].bitcast(I32))
-        load_w1(1, 0)
+        live_end = 3 * QUAD + 4
+        nc.sync.dma_start(out=v_s_moved[0:live_end, :].bitcast(I32), in_=v_s[4 : live_end + 4, :].bitcast(I32))
+        load_w1(1, 0, "slot0")
         nc.sync.dma_start(idx2[:], offs2)
-        load_wgs(0)
+        load_wgs_dealt(0)
         load_page(0)
         nc.sync.dma_start(out=w3_w_raw[:], in_=w3_words.rearrange("a p c i -> p a (c i)").bitcast(I32))
         nc.sync.dma_start(out=wgs_rows[:], in_=wgs)
         nc.sync.dma_start(idx4[:], offs4)
         nc.sync.dma_start(idx3[:], offs3)
         load_page(1)
-        load_wgs(1)
-        load_w1(0, 1)
-        load_w1(1, 1)
+        load_wgs_dealt(1)
+        load_w1(0, 1, "slot1")
+        load_w1(1, 1, "slot2")
         load_page(2)
         load_w2_words(1)
-        load_packed_scale_rows(w3_s_raw, w3_scales)
-        for i in range(3, 5):
+        load_packed_scales(w3_s_raw, w3_scales)
+        for i in range(3, PAGE_SLOTS):
             load_page(i)
 
         v_w = [sb("v_w%d" % a, [P, S], U32) for a in range(2)]
+        w1_w = [sb("w1_w%d" % g, [P, 2 * PASS], U32) for g in range(2)]
+        w1_s = [sb("w1_s%d" % g, [P, 2 * PASS], U8) for g in range(2)]
+        damp_ring = [sb("damp%d" % i, [P, S], F32) for i in range(3)]
+        h_ring = [sb("h%d" % i, [P, S], F32) for i in range(2)]
 
         def gather_words(a, first, count):
             nc.vector.tensor_copy(
                 v_w[a][:, first : first + count], tab_w[a][:].bitcast(U32).indirect(entries(idx, first, count))
             )
 
-        def take_bank(k, name):
-            return psum.tile([P, BANK], F32, name=name, tag="bank%d" % k)
+        def quantize_w1(a, g, grouped, copy):
+            copy(
+                out=grouped.rearrange("p (t m i) -> p m t i", t=PACK, i=PACK),
+                in_=w1_raw[a, g][:].rearrange("p i (m t) -> p m t i", t=PACK),
+            )
+            cols = slice(a * PASS, (a + 1) * PASS)
+            nc.vector.quantize_mx(out=w1_w[g][:, cols].bitcast(FP8X4), scales=w1_s[g][:, cols], in_=grouped)
 
-        def turn_bank(half):
-            return take_bank(6 + half, "turned")
-
-        def abs_b(dst, g, jb, k):
+        def abs_b(b_abs, g, jb, k):
             bank = take_bank(k, "b_bank")
             cols = slice(jb * P, (jb + 1) * P)
             for a in range(2):
@@ -170,29 +182,13 @@ def tile_list_stemma_deviation_kernel(
                     stop=(a == 1),
                 )
             nc.scalar.activation(
-                out=dst.rearrange("j (t p) -> j t p", t=PACK),
+                out=b_abs[:, jb, :].rearrange("j (t p) -> j t p", t=PACK),
                 in_=bank[:].rearrange("j (p t) -> j t p", t=PACK),
                 func=ACT.Abs,
             )
 
-        w1_w = [sb("w1_w%d" % g, [P, 2 * PASS], U32) for g in range(2)]
-        w1_s = [sb("w1_s%d" % g, [P, 2 * PASS], U8) for g in range(2)]
-
-        def round_w1(a, g, grouped, copy):
-            copy(
-                out=grouped.rearrange("p (t m i) -> p m t i", t=PACK, i=PACK),
-                in_=w1_raw[a, g][:].rearrange("p i (m t) -> p m t i", t=PACK),
-            )
-
-        def quantize_w1(g, first, count, grouped):
-            cols = slice(first, first + count)
-            nc.vector.quantize_mx(out=w1_w[g][:, cols].bitcast(FP8X4), scales=w1_s[g][:, cols], in_=grouped)
-
-        damp_ring = [sb("damp%d" % i, [P, S], F32) for i in range(3)]
-        h_ring = [sb("h%d" % i, [P, S], F32) for i in range(2)]
-
         def product_a(i, half, k):
-            cols = slice(half * BANK, (half + 1) * BANK)
+            cols = half_cols(half)
             acc = take_bank(k, "acc")
             g, t = divmod(i, PACK)
             for a in range(2):
@@ -208,40 +204,35 @@ def tile_list_stemma_deviation_kernel(
                 )
             return acc
 
-        def blocks(ap):
-            return ap.rearrange("p (b j) -> p b j", j=P)
-
-        def damp_by_root(b_abs, i, half, root_half):
-            cols = slice(half * BANK, (half + 1) * BANK)
-            turned = turn_bank(half)
+        def damp_by_root(b_abs, i, half, root):
+            turned = take_bank(TURN_BANK + half, "turned")
             for q in range(4):
                 nc.tensor.transpose(
                     turned[:, q * P : (q + 1) * P], b_abs[:, half * 4 + q, i * P : (i + 1) * P], ident[:]
                 )
-            nc.scalar.activation(out=root_half, in_=blocks(turned[:]), func=ACT.Abs_reciprocal_sqrt, bias=1.0)
-            nc.scalar.activation(out=blocks(damp_ring[i % 3][:, cols]), in_=root_half, func=ACT.Square)
-            return product_a(i, half, 3 + half)
+            nc.scalar.activation(out=root, in_=blocks(turned[:]), func=ACT.Abs_reciprocal_sqrt, bias=1.0)
+            nc.scalar.activation(out=blocks(damp_ring[i][:, half_cols(half)]), in_=root, func=ACT.Square)
+            return product_a(i, half, A_BANK + half)
 
         def multiply_h(dst, acc, i, half):
-            cols = slice(half * BANK, (half + 1) * BANK)
-            nc.vector.tensor_tensor(dst, acc[:], damp_ring[i][:, cols], ALU.mult)
+            nc.vector.tensor_tensor(dst, acc[:], damp_ring[i][:, half_cols(half)], ALU.mult)
 
-        def copy_a(i, a_dst):
+        def copy_a(i, dst, first_bank):
             for half in range(2):
-                cols = slice(half * BANK, (half + 1) * BANK)
-                nc.scalar.copy(out=a_dst[:, cols], in_=product_a(i, half, 6 + half)[:])
+                nc.scalar.copy(out=dst[:, half_cols(half)], in_=product_a(i, half, first_bank + half)[:])
 
-        def factor_by_logs(log_blocks, i):
+        def factor_by_logs(log_block, i):
             t = i % PACK
             for half in range(2):
-                cols = slice(half * BANK, (half + 1) * BANK)
-                turned = turn_bank(half)
+                turned = take_bank(TURN_BANK + half, "turned")
                 for q in range(4):
-                    block = turned[:, q * P : (q + 1) * P]
+                    dst = turned[:, q * P : (q + 1) * P]
                     neg = neg_log_w[half][:, (t * 4 + q) * P : (t * 4 + q + 1) * P]
-                    nc.tensor.matmul(block, log_blocks(half * 4 + q), ident[:], start=True, stop=False, is_transpose=True)
-                    nc.tensor.matmul(block, neg, ident[:], start=False, stop=True, is_transpose=True)
-                nc.scalar.activation(out=damp_ring[i % 3][:, cols], in_=turned[:], func=ACT.Exp, scale=-1.0)
+                    nc.tensor.matmul(dst, log_block(half * 4 + q), ident[:], start=True, stop=False, is_transpose=True)
+                    nc.tensor.matmul(dst, neg, ident[:], start=False, stop=True, is_transpose=True)
+                nc.scalar.activation(
+                    out=damp_ring[i % 3][:, half_cols(half)], in_=turned[:], func=ACT.Exp, scale=-1.0
+                )
 
         def scatter(i, values, factors, first, count):
             nc.vector.tensor_tensor(
@@ -254,14 +245,17 @@ def tile_list_stemma_deviation_kernel(
         def fetch_difference(dst, exemplar, i, first, count):
             nc.vector.tensor_tensor(dst, pages[i][:].indirect(entries(idx3, first, count)), exemplar, ALU.subtract)
 
+        def interleave(copy, grouped, slices):
+            copy(
+                out=grouped.rearrange("p (c i t) -> p c t i", i=LINE, t=PACK),
+                in_=slices.rearrange("p t (c i) -> p c t i", i=LINE),
+            )
+
         z_w = [sb("z_w%d" % g, [P, M], U32) for g in range(2)]
         z_s = [sb("z_s%d" % g, [P, M], U8) for g in range(2)]
 
         def quantize_z(z, grouped, g, first, count, copy):
-            copy(
-                out=grouped.rearrange("p (c i t) -> p c t i", i=4, t=PACK),
-                in_=z.rearrange("p (t c i) -> p c t i", i=4, t=PACK),
-            )
+            interleave(copy, grouped, z.rearrange("p (t m) -> p t m", t=PACK))
             cols = slice(first, first + count)
             nc.vector.quantize_mx(out=z_w[g][:, cols].bitcast(FP8X4), scales=z_s[g][:, cols], in_=grouped)
 
@@ -270,12 +264,10 @@ def tile_list_stemma_deviation_kernel(
         gather_words(1, BANK, BANK)
         w1_bf0 = sb("w1_bf0", [P, 2 * PASS * PACK], BF16, tag="exemplar0")
         for a in range(2):
-            part = w1_bf0[:, a * PASS * PACK : (a + 1) * PASS * PACK]
-            round_w1(a, 0, part, nc.vector.tensor_copy)
-            quantize_w1(0, a * PASS, PASS, part)
-        b_abs0 = sb("b_abs0", [P, 8, PASS], F32, tag="b_abs")
+            quantize_w1(a, 0, w1_bf0[:, a * PASS * PACK : (a + 1) * PASS * PACK], nc.vector.tensor_copy)
+        b_abs0 = sb("b_abs0", [P, BLOCKS, PASS], F32, tag="b_abs")
         for jb in range(4):
-            abs_b(b_abs0[:, jb, :], 0, jb, jb)
+            abs_b(b_abs0, 0, jb, jb)
 
         w3_w = sb("w3_w", [P, 2, N], I32)
         w3_s = sb("w3_s", [P, N], U8)
@@ -288,36 +280,34 @@ def tile_list_stemma_deviation_kernel(
             in_=w3_s_raw[:].rearrange("p (m t) -> p m t", t=PACK),
         )
 
-        h_halves = [h_ring[1][:, 0:BANK], h_ring[1][:, BANK:S]]
-        multiply_h(h_halves[0], damp_by_root(b_abs0, 0, 0, b_abs0[:, 4:8, 0:P]), 0, 0)
-        scatter(0, h_halves[0], wgs4[0], 0, BANK)
-        for jb, k in zip(range(4, 8), (0, 1, 2, 4)):
-            abs_b(b_abs0[:, jb, :], 0, jb, k)
+        h_first, h_second = h_ring[1][:, 0:BANK], h_ring[1][:, BANK:S]
+        multiply_h(h_first, damp_by_root(b_abs0, 0, 0, b_abs0[:, 4:8, 0:P]), 0, 0)
+        scatter(0, h_first, wgs_dealt[0], 0, BANK)
+        for jb, k in zip(range(4, BLOCKS), (0, 1, 2, A_BANK + 1)):
+            abs_b(b_abs0, 0, jb, k)
         root = sb("root", [P, BANK], F32, tag="bf1")
-        multiply_h(h_halves[0], damp_by_root(b_abs0, 0, 1, blocks(root[:])), 0, 1)
-        scatter(0, h_halves[0], wgs4[0], BANK, BANK)
+        multiply_h(h_first, damp_by_root(b_abs0, 0, 1, blocks(root[:])), 0, 1)
+        scatter(0, h_first, wgs_dealt[0], BANK, BANK)
 
         z0 = sb("z0", [P, PACK * M], F32)
         z0_t = [z0[:, t * M : (t + 1) * M] for t in range(PACK)]
         exemplars = [sb("exemplar%d" % k, [P, M], F32) for k in range(2)]
         logs = sb("logs", [P, 3 * S], F32, tag="tab_s")
-        acc0 = damp_by_root(b_abs0, 1, 0, blocks(root[:]))
-        acc1 = damp_by_root(b_abs0, 1, 1, blocks(logs[:])[:, 0:24:7, :])
-        multiply_h(h_halves[0], acc0, 1, 0)
+        acc_first = damp_by_root(b_abs0, 1, 0, blocks(root[:]))
+        acc_second = damp_by_root(b_abs0, 1, 1, blocks(logs[:])[:, 0 : 3 * BLOCKS : 7, :])
+        multiply_h(h_first, acc_first, 1, 0)
         fetch_exemplar(exemplars[0][:], 0, 0, M)
-        multiply_h(h_halves[1], acc1, 1, 1)
+        multiply_h(h_second, acc_second, 1, 1)
         fetch_difference(z0_t[0], exemplars[0][:], 0, 0, M)
-        scatter(1, h_ring[1][:], wgs4[1], 0, S)
+        scatter(1, h_ring[1][:], wgs_dealt[1], 0, S)
         load_page(5)
         fetch_exemplar(exemplars[1][:], 1, 0, M)
 
         log_w = logs[:, 0:S]
-        log_b0 = logs[:, S : 3 * S]
+        log_b0 = {t: logs[:, (t - 1) * S : t * S] for t in (2, 3)}
         nc.scalar.activation(out=log_w, in_=wgs_rows[:], func=ACT.Ln)
         for t in (2, 3):
-            nc.scalar.activation(
-                out=blocks(log_b0[:, (t - 2) * S : (t - 1) * S]), in_=b_abs0[:, :, t * P : (t + 1) * P], func=ACT.Ln, bias=1.0
-            )
+            nc.scalar.activation(out=blocks(log_b0[t]), in_=b_abs0[:, :, t * P : (t + 1) * P], func=ACT.Ln, bias=1.0)
         neg_log_w = [sb("neg_log_w%d" % half, [P, PACK * BANK], F32, tag="tab_w%d" % half) for half in range(2)]
         log_w_turned = []
         for half in range(2):
@@ -329,108 +319,118 @@ def tile_list_stemma_deviation_kernel(
 
         def spread_log_w(t):
             for half in range(2):
-                src = log_w_turned[half][:].rearrange("j (b q t) -> j t b q", t=PACK, b=4)[:, t]
+                rows = log_w_turned[half][:].rearrange("j (b q t) -> j t b q", t=PACK, b=4)[:, t]
                 nc.scalar.activation(
-                    out=neg_log_w[half][:, t * BANK : (t + 1) * BANK].rearrange("j (b r q) -> j b r q", r=4, q=32),
-                    in_=src.unsqueeze(2).to_broadcast([P, 4, 4, 32]),
+                    out=neg_log_w[half][:, t * BANK : (t + 1) * BANK].rearrange("j (b r q) -> j b r q", r=4, q=QUAD),
+                    in_=rows.unsqueeze(2).to_broadcast([P, 4, 4, QUAD]),
                     func=ACT.Copy,
                     scale=-1.0,
                 )
 
-        for i in (2, 3):
-            copy_a(i, z0_t[i - 1])
-            spread_log_w(i)
-            factor_by_logs(lambda jb: log_b0[:, ((i - 2) * 8 + jb) * P : ((i - 2) * 8 + jb + 1) * P], i)
-            scatter(i, z0_t[i - 1], damp_ring[i % 3], 0, S)
-            fetch_difference(z0_t[i - 1], exemplars[(i - 1) % 2][:], i - 1, 0, M)
-            load_page(4 + i)
-            fetch_exemplar(exemplars[i % 2][:], i, 0, M)
-            if i == 2:
-                for a in range(2):
-                    w1_bf1 = sb("w1_bf1%d" % a, [P, PASS * PACK], BF16, tag="bf%d" % (a + 1))
-                    round_w1(a, 1, w1_bf1[:], nc.scalar.copy)
-                    quantize_w1(1, a * PASS, PASS, w1_bf1[:])
+        copy_a(2, z0_t[1], TURN_BANK)
+        spread_log_w(2)
+        factor_by_logs(lambda jb: log_b0[2][:, jb * P : (jb + 1) * P], 2)
+        scatter(2, z0_t[1], damp_ring[2], 0, S)
+        fetch_difference(z0_t[1], exemplars[1][:], 1, 0, M)
+        load_page(6)
+        fetch_exemplar(exemplars[0][:], 2, 0, M)
+        for a in range(2):
+            w1_bf1 = sb("w1_bf1%d" % a, [P, PASS * PACK], BF16, tag="bf%d" % (a + 1))
+            quantize_w1(a, 1, w1_bf1[:], nc.scalar.copy)
+        a3 = sb("a3", [P, S], F32, tag="slot2")
+        copy_a(3, a3[:], TURN_BANK)
+        spread_log_w(3)
+        factor_by_logs(lambda jb: log_b0[3][:, jb * P : (jb + 1) * P], 3)
+        fetch_difference(z0_t[2], exemplars[0][:], 2, 0, M)
+        load_page(7)
+        scatter(3, a3[:], damp_ring[0], 0, S)
+        fetch_exemplar(exemplars[1][:], 3, 0, M)
 
-        log_b1 = [sb("log_b1_%d" % half, [P, 4, PASS], F32, tag="slot%d" % (half + 1)) for half in range(2)]
-        for jb, k in enumerate((2, 3, 4, 7, 5, 2, 3, 7)):
-            abs_b(log_b1[jb // 4][:, jb % 4, :], 1, jb, k)
-        for half in range(2):
-            nc.scalar.activation(out=log_b1[half][:], in_=log_b1[half][:], func=ACT.Ln, bias=1.0)
-
-        for i in range(PACK, 2 * PACK):
-            t = i - PACK
+        log_b1 = sb("log_b1", [P, BLOCKS, PASS], F32, tag="b_abs")
+        for jb in range(BLOCKS):
+            abs_b(log_b1, 1, jb, 2 + jb % 4 if jb < BLOCKS - 1 else TURN_BANK + 1)
+        nc.scalar.activation(out=log_b1[:], in_=log_b1[:], func=ACT.Ln, bias=1.0)
+        for t in range(PACK):
+            i = PACK + t
             if t < 2:
                 spread_log_w(t)
-            a_dst = z0_t[PACK - 1] if t == 0 else h_ring[i % 2][:]
-            factor_by_logs(lambda jb: log_b1[jb // 4][:, jb % 4, t * P : (t + 1) * P], i)
-            copy_a(i, a_dst)
-            scatter(i, a_dst, damp_ring[i % 3], 0, S)
+            factor_by_logs(lambda jb: log_b1[:, jb, t * P : (t + 1) * P], i)
             if t == 0:
+                copy_a(i, z0_t[PACK - 1], A_BANK)
+                scatter(i, z0_t[PACK - 1], damp_ring[i % 3], 0, S)
                 fetch_difference(z0_t[PACK - 1], exemplars[1][:], PACK - 1, 0, M)
+            else:
+                copy_a(i, h_ring[i % 2][:], TURN_BANK)
+                scatter(i, h_ring[i % 2][:], damp_ring[i % 3], 0, S)
 
-        z0_bf = sb("z0_bf", [P, PACK * M], BF16, tag="slot2")
+        z0_bf = sb("z0_bf", [P, PACK * M], BF16, tag="b_abs")
         quantize_z(z0[:], z0_bf[:], 0, 0, M, nc.scalar.copy)
 
         y_w = sb("y_w", [P, M], U32)
         y_s = sb("y_s", [P, M], U8)
         y_rows = out_0.rearrange("(p t) m -> p t m", t=PACK)
         y_words = out_1[0].rearrange("p m t -> p (m t)").bitcast(I32)
-        last = 2 * PACK - 1
-        exemplar4 = h_ring[last % 2]
+
+        def product_y(first):
+            cols = slice(first, first + UNIT)
+            acc = take_bank(first // UNIT, "y_acc")[:].rearrange("p (t m) -> p t m", t=PACK)
+            for g in range(2):
+                for t in range(PACK):
+                    nc.tensor.matmul_mx(
+                        out=acc[:, t, :],
+                        lhsT=w3_w[:, g, t * P : (t + 1) * P].bitcast(FP8X4),
+                        lhsT_scale=w3_s[4 * g : P, t * P : (t + 1) * P],
+                        rhs=z_w[g][:, cols].bitcast(FP8X4),
+                        rhs_scale=z_s[g][:, cols],
+                        start=(g == 0 and t == 0),
+                        stop=(g == 1 and t == PACK - 1),
+                    )
+            return acc
+
+        def fetch_z1(first, start, count):
+            z = z1[:, PACK * start : PACK * (start + count)]
+            for t in range(PACK):
+                exemplar = exemplar4[:, t * CHUNK + start : t * CHUNK + start + count]
+                fetch_difference(z[:, t * count : (t + 1) * count], exemplar, PACK + t, first + start, count)
+            return z
+
+        def store_planes(first, y_bf):
+            cols = slice(first, first + CHUNK)
+            nc.vector.quantize_mx(out=y_w[:, cols].bitcast(FP8X4), scales=y_s[:, cols], in_=y_bf[:])
+            nc.sync.dma_start(out=y_words[:, cols], in_=y_w[:, cols].bitcast(I32))
+
+        exemplar4 = h_ring[1]
         z1 = sb("z1", [P, PACK * CHUNK], F32)
-        def finish(first, count, z):
-            cols = slice(first, first + count)
-            z_bf = sb("z1_bf%d" % first, [P, PACK * count], BF16, tag="bf%d" % (first // UNIT % 2 * 2))
-            quantize_z(z, z_bf[:], 1, first, count, nc.scalar.copy if count == CHUNK else nc.vector.tensor_copy)
-            y = sb("y%d" % first, [P, PACK, count], F32, tag=("b_abs", "slot0", "slot1")[first // CHUNK % 3] if first % CHUNK == 0 else "slot2")
-            y_bf = sb("y_bf%d" % first, [P, count * PACK], BF16, tag="bf1" if first % CHUNK == 0 else "tab_s")
-            for u in range(count // UNIT):
-                ucols = slice(first + u * UNIT, first + (u + 1) * UNIT)
-                acc = take_bank(first // UNIT + u, "y_acc")[:].rearrange("p (t m) -> p t m", t=PACK)
-                for g in range(2):
-                    for t in range(PACK):
-                        nc.tensor.matmul_mx(
-                            out=acc[:, t, :],
-                            lhsT=w3_w[:, g, t * P : (t + 1) * P].bitcast(FP8X4),
-                            lhsT_scale=w3_s[4 * g : P, t * P : (t + 1) * P],
-                            rhs=z_w[g][:, ucols].bitcast(FP8X4),
-                            rhs_scale=z_s[g][:, ucols],
-                            start=(g == 0 and t == 0),
-                            stop=(g == 1 and t == PACK - 1),
-                        )
-                nc.scalar.activation(out=y[:, :, u * UNIT : (u + 1) * UNIT], in_=acc, func=ACT.Abs)
-                if count == CHUNK:
+        y_tags = ("b_abs", "slot0", "slot1")
+        for first in range(0, M, CHUNK):
+            for t in range(PACK):
+                fetch_exemplar(exemplar4[:, t * CHUNK : (t + 1) * CHUNK], PACK + t, first, CHUNK)
+            y_bf = sb("y_bf%d" % first, [P, CHUNK * PACK], BF16, tag="bf1")
+            y_bf_units = [y_bf[:, u * UNIT * PACK : (u + 1) * UNIT * PACK] for u in range(CHUNK // UNIT)]
+            if first + CHUNK < M:
+                z_bf = sb("z1_bf%d" % first, [P, PACK * CHUNK], BF16, tag="bf0")
+                quantize_z(fetch_z1(first, 0, CHUNK), z_bf[:], 1, first, CHUNK, nc.scalar.copy)
+                y = sb("y%d" % first, [P, PACK, CHUNK], F32, tag=y_tags[first // CHUNK])
+                for u in range(CHUNK // UNIT):
+                    acc = product_y(first + u * UNIT)
+                    nc.scalar.activation(out=y[:, :, u * UNIT : (u + 1) * UNIT], in_=acc, func=ACT.Abs)
                     nc.scalar.activation(
-                        out=y_bf[:, u * UNIT * PACK : (u + 1) * UNIT * PACK].rearrange("p (m t) -> p m t", t=PACK),
+                        out=y_bf_units[u].rearrange("p (m t) -> p m t", t=PACK),
                         in_=acc.rearrange("p t m -> p m t"),
                         func=ACT.Abs,
                     )
-                else:
-                    nc.vector.tensor_copy(
-                        out=y_bf[:].rearrange("p (c i t) -> p c t i", i=4, t=PACK),
-                        in_=y[:].rearrange("p t (c i) -> p c t i", i=4),
-                    )
-            nc.vector.quantize_mx(out=y_w[:, cols].bitcast(FP8X4), scales=y_s[:, cols], in_=y_bf[:])
-            nc.sync.dma_start(out=y_rows[:, :, cols], in_=y[:])
-            nc.sync.dma_start(out=y_words[:, cols], in_=y_w[:, cols].bitcast(I32))
-
-        chunks = M // CHUNK
-        for c in range(chunks):
-            for t in range(PACK):
-                fetch_exemplar(exemplar4[:, t * CHUNK : (t + 1) * CHUNK], PACK + t, c * CHUNK, CHUNK)
-            count = UNIT if c == chunks - 1 else CHUNK
-            for start in range(0, CHUNK, count):
-                z = z1[:, PACK * start : PACK * (start + count)]
-                for t in range(PACK):
-                    fetch_difference(
-                        z[:, t * count : (t + 1) * count],
-                        exemplar4[:, t * CHUNK + start : t * CHUNK + start + count],
-                        PACK + t,
-                        c * CHUNK + start,
-                        count,
-                    )
-                finish(c * CHUNK + start, count, z)
+                nc.sync.dma_start(out=y_rows[:, :, first : first + CHUNK], in_=y[:])
+            else:
+                for u, (z_tag, y_tag, queue) in enumerate((("bf0", "b_abs", nc.sync), ("bf2", "slot2", nc.scalar))):
+                    column = first + u * UNIT
+                    z_bf = sb("z1_bf%d" % column, [P, PACK * UNIT], BF16, tag=z_tag)
+                    quantize_z(fetch_z1(first, u * UNIT, UNIT), z_bf[:], 1, column, UNIT, nc.vector.tensor_copy)
+                    y = sb("y%d" % column, [P, PACK, UNIT], F32, tag=y_tag)
+                    nc.scalar.activation(out=y[:], in_=product_y(column), func=ACT.Abs)
+                    interleave(nc.vector.tensor_copy, y_bf_units[u], y[:])
+                    queue.dma_start(out=y_rows[:, :, column : column + UNIT], in_=y[:])
+            store_planes(first, y_bf)
         for q in range(4):
-            nc.sync.dma_start(
-                out=out_2[0, 4 * q : 4 * q + 4, :].bitcast(I32), in_=y_s[32 * q : 32 * q + 4, :].bitcast(I32)
+            (nc.sync, nc.scalar)[q % 2].dma_start(
+                out=out_2[0, 4 * q : 4 * q + 4, :].bitcast(I32), in_=y_s[QUAD * q : QUAD * q + 4, :].bitcast(I32)
             )

@@ -68,8 +68,6 @@ def tile_list_stemma_deviation_kernel(
         nc.vector.memset(w3_s_raw[:].bitcast(I32), 0)
         ident = sb("ident", [P, P], F32)
         make_identity(nc, ident[:])
-        warm = sb("warm", [P, 1], F32)
-        nc.scalar.activation(out=warm[:], in_=ident[:, 0:1], func=ACT.Abs_reciprocal_sqrt, bias=1.0)
 
         tab_w = [sb("tab_w%d" % a, [P, T], I32) for a in range(2)]
         w2_w = [sb("w2_w%d" % g, [P, 2, 2 * PASS], U8) for g in range(2)]

@@ -26,10 +26,11 @@ LINE = 4
 QUAD = 32
 LIST_ROWS = 16
 PAGE_SLOTS = 5
+RING = 3
 CHUNK = 256
 UNIT = 128
-A_BANK = 3
-TURN_BANK = 6
+EVEN_BANK = 4
+ODD_BANK = 6
 
 
 def tile_list_stemma_deviation_kernel(
@@ -71,7 +72,7 @@ def tile_list_stemma_deviation_kernel(
 
         tab_w = [sb("tab_w%d" % a, [P, T], I32) for a in range(2)]
         w2_w = [sb("w2_w%d" % g, [P, 2, 2 * PASS], U8) for g in range(2)]
-        wgs_dealt = [sb("wgs_t%d" % t, [P, S], F32) for t in range(2)]
+        wgs_dealt = sb("wgs_dealt", [P, S], F32)
         wgs_rows = sb("wgs_rows", [P, S], F32)
         w3_w_raw = sb("w3_w_raw", [P, 2, N], I32)
         w1_raw = {}
@@ -80,15 +81,15 @@ def tile_list_stemma_deviation_kernel(
         def load_tab_words(a):
             nc.sync.dma_start(out=tab_w[a][:], in_=tab_words[a].rearrange("p t i -> p (t i)").bitcast(I32))
 
-        def load_packed_scales(dst, src):
+        def load_packed_scales(queue, dst, src):
             for q in range(4):
-                nc.sync.dma_start(
+                queue.dma_start(
                     out=dst[QUAD * q : QUAD * q + 8, :].bitcast(I32), in_=src[:, 4 * q : 4 * q + 4, :].bitcast(I32)
                 )
 
-        def load_w2_scales():
+        def load_w2_scales(queue):
             for q in range(4):
-                nc.sync.dma_start(
+                queue.dma_start(
                     out=w2_s[QUAD * q : QUAD * q + 4, :].bitcast(I32).rearrange("r (a c) -> r a c", a=2),
                     in_=w2_scales[:, 4 * q : 4 * q + 4, :].bitcast(I32).rearrange("a r c -> r a c"),
                 )
@@ -99,17 +100,17 @@ def tile_list_stemma_deviation_kernel(
                 in_=w2_words[:, :, g * 2 * PASS : (g + 1) * 2 * PASS].bitcast(I32).rearrange("a p c -> p a c"),
             )
 
-        def load_w1(a, g, tag):
-            w1_raw[a, g] = sb("w1_raw%d%d" % (a, g), [P, PACK, PASS], F32, tag=tag)
+        def load_w1(a, g):
+            w1_raw[a, g] = sb("w1_raw%d%d" % (a, g), [P, PACK, PASS], F32)
             nc.sync.dma_start(
                 out=w1_raw[a, g][:],
                 in_=w1[a * PASS : (a + 1) * PASS, g * PASS : (g + 1) * PASS].rearrange("(p i) c -> p i c", i=PACK),
             )
 
-        def load_wgs_dealt(t):
+        def load_wgs_dealt():
             rows = wgs.rearrange("(q t) j -> q t j", t=PACK)
             for quad in range(4):
-                nc.sync.dma_start(out=wgs_dealt[t][QUAD * quad : QUAD * (quad + 1), :], in_=rows[:, t, :])
+                nc.sync.dma_start(out=wgs_dealt[QUAD * quad : QUAD * (quad + 1), :], in_=rows[:, 0, :])
 
         def load_page(i):
             g, t = divmod(i, PACK)
@@ -118,53 +119,58 @@ def tile_list_stemma_deviation_kernel(
                 out=pages[i][:], in_=page0[g * PASS : (g + 1) * PASS, :].rearrange("(p t) c -> t p c", t=PACK)[t]
             )
 
-        load_packed_scales(tab_s, tab_scales)
         nc.sync.dma_start(idx[:], offs)
+        nc.sync.dma_start(idx2[:], offs2)
+        load_w2_words(0)
+        load_packed_scales(nc.sync, tab_s, tab_scales)
         load_tab_words(0)
         load_tab_words(1)
-        load_w2_words(0)
-        load_w2_scales()
-        load_w1(0, 0, "z0")
+        load_w2_scales(nc.sync)
         v_s = sb("v_s", [P, S], U8)
         nc.vector.tensor_copy(v_s[:], tab_s[:].indirect(idx[:]))
         live_end = 3 * QUAD + 4
         nc.sync.dma_start(out=v_s_moved[0:live_end, :].bitcast(I32), in_=v_s[4 : live_end + 4, :].bitcast(I32))
-        load_w1(1, 0, "slot0")
-        nc.sync.dma_start(idx2[:], offs2)
-        load_wgs_dealt(0)
+        load_w1(0, 0)
+        load_w1(1, 0)
         load_page(0)
-        nc.sync.dma_start(out=w3_w_raw[:], in_=w3_words.rearrange("a p c i -> p a (c i)").bitcast(I32))
+        load_wgs_dealt()
         nc.sync.dma_start(out=wgs_rows[:], in_=wgs)
         nc.sync.dma_start(idx4[:], offs4)
         nc.sync.dma_start(idx3[:], offs3)
+        nc.sync.dma_start(out=w3_w_raw[:], in_=w3_words.rearrange("a p c i -> p a (c i)").bitcast(I32))
+        load_packed_scales(nc.sync, w3_s_raw, w3_scales)
         load_page(1)
-        load_wgs_dealt(1)
-        load_w1(0, 1, "slot1")
-        load_w1(1, 1, "slot2")
-        load_page(2)
         load_w2_words(1)
-        load_packed_scales(w3_s_raw, w3_scales)
-        for i in range(3, PAGE_SLOTS):
+        load_w1(0, 1)
+        load_w1(1, 1)
+        for i in range(2, PAGE_SLOTS):
             load_page(i)
 
-        v_w = [sb("v_w%d" % a, [P, S], U32) for a in range(2)]
+        v_both = sb("v_both", [P, 2 * S], U32, tag="tab_s")
+        v_w = [v_both[:, a * S : (a + 1) * S] for a in range(2)]
         w1_w = [sb("w1_w%d" % g, [P, 2 * PASS], U32) for g in range(2)]
         w1_s = [sb("w1_s%d" % g, [P, 2 * PASS], U8) for g in range(2)]
-        damp_ring = [sb("damp%d" % i, [P, S], F32) for i in range(3)]
-        h_ring = [sb("h%d" % i, [P, S], F32) for i in range(2)]
+        factor_ring = [sb("factor%d" % i, [P, S], F32) for i in range(RING)]
+        a_ring = [sb("a%d" % i, [P, S], F32) for i in range(RING)]
 
-        def gather_words(a, first, count):
+        def gather_words(a, half):
             nc.vector.tensor_copy(
-                v_w[a][:, first : first + count], tab_w[a][:].bitcast(U32).indirect(entries(idx, first, count))
+                v_w[a][:, half_cols(half)], tab_w[a][:].bitcast(U32).indirect(entries(idx, half * BANK, BANK))
             )
 
-        def quantize_w1(a, g, grouped, copy):
+        def round_w1(copy, grouped, g, pair, a):
             copy(
-                out=grouped.rearrange("p (t m i) -> p m t i", t=PACK, i=PACK),
-                in_=w1_raw[a, g][:].rearrange("p i (m t) -> p m t i", t=PACK),
+                out=grouped[:, a * 2 * PASS : (a + 1) * 2 * PASS].rearrange("p (u m i) -> p m u i", u=2, i=PACK),
+                in_=w1_raw[a, g][:].rearrange("p i (m t) -> p m t i", t=PACK)[:, :, 2 * pair : 2 * pair + 2, :],
             )
-            cols = slice(a * PASS, (a + 1) * PASS)
-            nc.vector.quantize_mx(out=w1_w[g][:, cols].bitcast(FP8X4), scales=w1_s[g][:, cols], in_=grouped)
+
+        def quantize_w1(grouped, g, pair, first_pass, passes):
+            cols = slice(pair * PASS + first_pass * 2 * P, pair * PASS + (first_pass + passes) * 2 * P)
+            nc.vector.quantize_mx(
+                out=w1_w[g][:, cols].bitcast(FP8X4),
+                scales=w1_s[g][:, cols],
+                in_=grouped[:, first_pass * 2 * PASS : (first_pass + passes) * 2 * PASS],
+            )
 
         def abs_b(b_abs, g, jb, k):
             bank = take_bank(k, "b_bank")
@@ -180,17 +186,18 @@ def tile_list_stemma_deviation_kernel(
                     stop=(a == 1),
                 )
             nc.scalar.activation(
-                out=b_abs[:, jb, :].rearrange("j (t p) -> j t p", t=PACK),
+                out=b_abs[:].rearrange("j (t s) -> j t s", t=PACK)[:, :, cols],
                 in_=bank[:].rearrange("j (p t) -> j t p", t=PACK),
                 func=ACT.Abs,
             )
 
-        def product_a(i, half, k):
+        def product_a(i, half, first_bank):
             cols = half_cols(half)
-            acc = take_bank(k, "acc")
+            acc = take_bank(first_bank + half, "acc")
             g, t = divmod(i, PACK)
             for a in range(2):
-                wcols = slice(a * PASS + t * P, a * PASS + (t + 1) * P)
+                first = (t // 2) * PASS + a * 2 * P + (t % 2) * P
+                wcols = slice(first, first + P)
                 nc.tensor.matmul_mx(
                     out=acc[:],
                     lhsT=w1_w[g][:, wcols].bitcast(FP8X4),
@@ -202,34 +209,37 @@ def tile_list_stemma_deviation_kernel(
                 )
             return acc
 
-        def damp_by_root(b_abs, i, half, root):
-            turned = take_bank(TURN_BANK + half, "turned")
+        def damped_a(half, root, h):
+            cols = half_cols(half)
+            turned = take_bank(ODD_BANK + half, "turned")
             for q in range(4):
-                nc.tensor.transpose(
-                    turned[:, q * P : (q + 1) * P], b_abs[:, half * 4 + q, i * P : (i + 1) * P], ident[:]
-                )
-            nc.scalar.activation(out=root, in_=blocks(turned[:]), func=ACT.Abs_reciprocal_sqrt, bias=1.0)
-            nc.scalar.activation(out=blocks(damp_ring[i][:, half_cols(half)]), in_=root, func=ACT.Square)
-            return product_a(i, half, A_BANK + half)
+                jb = half * 4 + q
+                nc.tensor.transpose(turned[:, q * P : (q + 1) * P], b_abs0[:, jb * P : (jb + 1) * P], ident[:])
+            nc.scalar.activation(out=root, in_=turned[:], func=ACT.Abs_reciprocal_sqrt, bias=1.0)
+            nc.scalar.activation(out=factor_ring[0][:, cols], in_=root, func=ACT.Square)
+            nc.vector.tensor_tensor(h, product_a(0, half, EVEN_BANK)[:], factor_ring[0][:, cols], ALU.mult)
 
-        def multiply_h(dst, acc, i, half):
-            nc.vector.tensor_tensor(dst, acc[:], damp_ring[i][:, half_cols(half)], ALU.mult)
+        def tile_banks(i):
+            return (EVEN_BANK, ODD_BANK)[i % 2]
 
-        def copy_a(i, dst, first_bank):
+        def copy_a(i, first_bank):
             for half in range(2):
-                nc.scalar.copy(out=dst[:, half_cols(half)], in_=product_a(i, half, first_bank + half)[:])
+                nc.scalar.copy(out=a_ring[i % RING][:, half_cols(half)], in_=product_a(i, half, first_bank)[:])
 
-        def factor_by_logs(log_block, i):
+        def factor_by_logs(log_b, i):
             t = i % PACK
             for half in range(2):
-                turned = take_bank(TURN_BANK + half, "turned")
+                turned = take_bank(tile_banks(i) + half, "turned")
                 for q in range(4):
+                    jb = half * 4 + q
                     dst = turned[:, q * P : (q + 1) * P]
                     neg = neg_log_w[half][:, (t * 4 + q) * P : (t * 4 + q + 1) * P]
-                    nc.tensor.matmul(dst, log_block(half * 4 + q), ident[:], start=True, stop=False, is_transpose=True)
+                    nc.tensor.matmul(
+                        dst, log_b[:, jb * P : (jb + 1) * P], ident[:], start=True, stop=False, is_transpose=True
+                    )
                     nc.tensor.matmul(dst, neg, ident[:], start=False, stop=True, is_transpose=True)
                 nc.scalar.activation(
-                    out=damp_ring[i % 3][:, half_cols(half)], in_=turned[:], func=ACT.Exp, scale=-1.0
+                    out=factor_ring[i % RING][:, half_cols(half)], in_=turned[:], func=ACT.Exp, scale=-1.0
                 )
 
         def scatter(i, values, factors, first, count):
@@ -242,6 +252,13 @@ def tile_list_stemma_deviation_kernel(
 
         def fetch_difference(dst, exemplar, i, first, count):
             nc.vector.tensor_tensor(dst, pages[i][:].indirect(entries(idx3, first, count)), exemplar, ALU.subtract)
+
+        def fetch_z0(i):
+            for half in range(2):
+                fetch_exemplar(exemplar0[:, half_cols(half)], i, half * BANK, BANK)
+            for half in range(2):
+                cols = half_cols(half)
+                fetch_difference(z0_t[i][:, cols], exemplar0[:, cols], i, half * BANK, BANK)
 
         def interleave(copy, grouped, slices):
             copy(
@@ -257,55 +274,35 @@ def tile_list_stemma_deviation_kernel(
             cols = slice(first, first + count)
             nc.vector.quantize_mx(out=z_w[g][:, cols].bitcast(FP8X4), scales=z_s[g][:, cols], in_=grouped)
 
-        gather_words(0, 0, S)
-        gather_words(1, 0, BANK)
-        gather_words(1, BANK, BANK)
-        w1_bf0 = sb("w1_bf0", [P, 2 * PASS * PACK], BF16, tag="exemplar0")
+        for half in range(2):
+            for a in range(2):
+                gather_words(a, half)
+        w1_bf = sb("w1_bf00", [P, 4 * PASS], BF16, tag="bf0")
         for a in range(2):
-            quantize_w1(a, 0, w1_bf0[:, a * PASS * PACK : (a + 1) * PASS * PACK], nc.vector.tensor_copy)
-        b_abs0 = sb("b_abs0", [P, BLOCKS, PASS], F32, tag="b_abs")
-        for jb in range(4):
-            abs_b(b_abs0, 0, jb, jb)
-
-        w3_w = sb("w3_w", [P, 2, N], I32)
-        w3_s = sb("w3_s", [P, N], U8)
-        nc.vector.tensor_copy(
-            out=w3_w[:].rearrange("p a (t m) -> p a m t", t=PACK),
-            in_=w3_w_raw[:].rearrange("p a (m t) -> p a m t", t=PACK),
-        )
-        nc.vector.tensor_copy(
-            out=w3_s[:].rearrange("p (t m) -> p m t", t=PACK),
-            in_=w3_s_raw[:].rearrange("p (m t) -> p m t", t=PACK),
-        )
-
-        h_first, h_second = h_ring[1][:, 0:BANK], h_ring[1][:, BANK:S]
-        multiply_h(h_first, damp_by_root(b_abs0, 0, 0, b_abs0[:, 4:8, 0:P]), 0, 0)
-        scatter(0, h_first, wgs_dealt[0], 0, BANK)
-        for jb, k in zip(range(4, BLOCKS), (0, 1, 2, A_BANK + 1)):
-            abs_b(b_abs0, 0, jb, k)
-        root = sb("root", [P, BANK], F32, tag="bf1")
-        multiply_h(h_first, damp_by_root(b_abs0, 0, 1, blocks(root[:])), 0, 1)
-        scatter(0, h_first, wgs_dealt[0], BANK, BANK)
-
+            round_w1(nc.vector.tensor_copy, w1_bf[:], 0, 0, a)
+            quantize_w1(w1_bf[:], 0, 0, a, 1)
+        b_abs0 = sb("b_abs0", [P, PACK * S], F32, tag="b_abs")
         z0 = sb("z0", [P, PACK * M], F32)
         z0_t = [z0[:, t * M : (t + 1) * M] for t in range(PACK)]
-        exemplars = [sb("exemplar%d" % k, [P, M], F32) for k in range(2)]
-        logs = sb("logs", [P, 3 * S], F32, tag="tab_s")
-        acc_first = damp_by_root(b_abs0, 1, 0, blocks(root[:]))
-        acc_second = damp_by_root(b_abs0, 1, 1, blocks(logs[:])[:, 0 : 3 * BLOCKS : 7, :])
-        multiply_h(h_first, acc_first, 1, 0)
-        fetch_exemplar(exemplars[0][:], 0, 0, M)
-        multiply_h(h_second, acc_second, 1, 1)
-        fetch_difference(z0_t[0], exemplars[0][:], 0, 0, M)
-        scatter(1, h_ring[1][:], wgs_dealt[1], 0, S)
-        load_page(5)
-        fetch_exemplar(exemplars[1][:], 1, 0, M)
+        exemplar0 = sb("exemplar0", [P, M], F32)
+        for jb in range(4):
+            abs_b(b_abs0, 0, jb, jb)
+        h0 = sb("h0", [P, BANK], F32, tag="w3_w")
+        damped_a(0, b_abs0[:, BANK:S], h0[:])
+        scatter(0, h0[:], wgs_dealt, 0, BANK)
+        for jb in range(4, BLOCKS):
+            abs_b(b_abs0, 0, jb, jb - 4)
+        log_w, log_b1st = z0[:, BANK : BANK + S], z0[:, BANK + S : BANK + 2 * S]
+        damped_a(1, z0[:, M + BANK // 2 : M + 3 * BANK // 2], h0[:])
+        scatter(0, h0[:], wgs_dealt, BANK, BANK)
 
-        log_w = logs[:, 0:S]
-        log_b0 = {t: logs[:, (t - 1) * S : t * S] for t in (2, 3)}
+        w1_bf = sb("w1_bf01", [P, 4 * PASS], BF16, tag="bf1")
+        for a in range(2):
+            round_w1(nc.vector.tensor_copy, w1_bf[:], 0, 1, a)
+        quantize_w1(w1_bf[:], 0, 1, 0, 2)
+
         nc.scalar.activation(out=log_w, in_=wgs_rows[:], func=ACT.Ln)
-        for t in (2, 3):
-            nc.scalar.activation(out=blocks(log_b0[t]), in_=b_abs0[:, :, t * P : (t + 1) * P], func=ACT.Ln, bias=1.0)
+        nc.scalar.activation(out=log_b1st, in_=b_abs0[:, S : 2 * S], func=ACT.Ln, bias=1.0)
         neg_log_w = [sb("neg_log_w%d" % half, [P, PACK * BANK], F32, tag="tab_w%d" % half) for half in range(2)]
         log_w_turned = []
         for half in range(2):
@@ -318,48 +315,58 @@ def tile_list_stemma_deviation_kernel(
         def spread_log_w(t):
             for half in range(2):
                 rows = log_w_turned[half][:].rearrange("j (b q t) -> j t b q", t=PACK, b=4)[:, t]
+                dst = neg_log_w[half][:, t * BANK : (t + 1) * BANK]
                 nc.scalar.activation(
-                    out=neg_log_w[half][:, t * BANK : (t + 1) * BANK].rearrange("j (b r q) -> j b r q", r=4, q=QUAD),
+                    out=dst.rearrange("j (b r q) -> j b r q", r=4, q=QUAD),
                     in_=rows.unsqueeze(2).to_broadcast([P, 4, 4, QUAD]),
                     func=ACT.Copy,
                     scale=-1.0,
                 )
 
-        copy_a(2, z0_t[1], TURN_BANK)
-        spread_log_w(2)
-        factor_by_logs(lambda jb: log_b0[2][:, jb * P : (jb + 1) * P], 2)
-        scatter(2, z0_t[1], damp_ring[2], 0, S)
-        fetch_difference(z0_t[1], exemplars[1][:], 1, 0, M)
-        load_page(6)
-        fetch_exemplar(exemplars[0][:], 2, 0, M)
-        for a in range(2):
-            w1_bf1 = sb("w1_bf1%d" % a, [P, PASS * PACK], BF16, tag="bf%d" % (a + 1))
-            quantize_w1(a, 1, w1_bf1[:], nc.scalar.copy)
-        a3 = sb("a3", [P, S], F32, tag="slot2")
-        copy_a(3, a3[:], TURN_BANK)
-        spread_log_w(3)
-        factor_by_logs(lambda jb: log_b0[3][:, jb * P : (jb + 1) * P], 3)
-        fetch_difference(z0_t[2], exemplars[0][:], 2, 0, M)
-        load_page(7)
-        scatter(3, a3[:], damp_ring[0], 0, S)
-        fetch_exemplar(exemplars[1][:], 3, 0, M)
+        fetch_z0(0)
+        w3_w = sb("w3_w", [P, 2, N], I32)
+        w3_s = sb("w3_s", [P, N], U8)
+        nc.vector.tensor_copy(
+            out=w3_w[:].rearrange("p a (t m) -> p a m t", t=PACK),
+            in_=w3_w_raw[:].rearrange("p a (m t) -> p a m t", t=PACK),
+        )
+        nc.vector.tensor_copy(
+            out=w3_s[:].rearrange("p (t m) -> p m t", t=PACK),
+            in_=w3_s_raw[:].rearrange("p (m t) -> p m t", t=PACK),
+        )
 
-        log_b1 = sb("log_b1", [P, BLOCKS, PASS], F32, tag="b_abs")
+        log_b0 = {1: log_b1st, 2: z0_t[2], 3: z0_t[3]}
+        for i in range(1, PACK):
+            spread_log_w(i)
+            if i == 1:
+                copy_a(i, 2)
+            factor_by_logs(log_b0[i], i)
+            if i == 1:
+                nc.scalar.activation(
+                    out=z0[:, 2 * M :], in_=b_abs0[:, 2 * S :], func=ACT.Ln, bias=1.0
+                )
+            if i > 1:
+                copy_a(i, tile_banks(i))
+            scatter(i, a_ring[i % RING][:], factor_ring[i % RING], 0, S)
+            load_page(PAGE_SLOTS + i - 1)
+            fetch_z0(i)
+            if i < PACK - 1:
+                pair = i - 1
+                w1_bf = sb("w1_bf1%d" % pair, [P, 4 * PASS], BF16, tag="bf%d" % pair)
+                for a in range(2):
+                    round_w1(nc.scalar.copy, w1_bf[:], 1, pair, a)
+                quantize_w1(w1_bf[:], 1, pair, 0, 2)
+        spread_log_w(0)
+
+        log_b1 = sb("log_b1", [P, PACK * S], F32, tag="b_abs")
         for jb in range(BLOCKS):
-            abs_b(log_b1, 1, jb, 2 + jb % 4 if jb < BLOCKS - 1 else TURN_BANK + 1)
+            abs_b(log_b1, 1, jb, (2 if jb < BLOCKS - 2 else ODD_BANK) + jb % 2)
         nc.scalar.activation(out=log_b1[:], in_=log_b1[:], func=ACT.Ln, bias=1.0)
         for t in range(PACK):
             i = PACK + t
-            if t < 2:
-                spread_log_w(t)
-            factor_by_logs(lambda jb: log_b1[:, jb, t * P : (t + 1) * P], i)
-            if t == 0:
-                copy_a(i, z0_t[PACK - 1], A_BANK)
-                scatter(i, z0_t[PACK - 1], damp_ring[i % 3], 0, S)
-                fetch_difference(z0_t[PACK - 1], exemplars[1][:], PACK - 1, 0, M)
-            else:
-                copy_a(i, h_ring[i % 2][:], TURN_BANK)
-                scatter(i, h_ring[i % 2][:], damp_ring[i % 3], 0, S)
+            factor_by_logs(log_b1[:, t * S : (t + 1) * S], i)
+            copy_a(i, tile_banks(i))
+            scatter(i, a_ring[i % RING][:], factor_ring[i % RING], 0, S)
 
         z0_bf = sb("z0_bf", [P, PACK * M], BF16, tag="b_abs")
         quantize_z(z0[:], z0_bf[:], 0, 0, M, nc.scalar.copy)
@@ -397,9 +404,9 @@ def tile_list_stemma_deviation_kernel(
             nc.vector.quantize_mx(out=y_w[:, cols].bitcast(FP8X4), scales=y_s[:, cols], in_=y_bf[:])
             nc.sync.dma_start(out=y_words[:, cols], in_=y_w[:, cols].bitcast(I32))
 
-        exemplar4 = h_ring[1]
+        exemplar4 = a_ring[(2 * PACK - 1) % RING]
         z1 = sb("z1", [P, PACK * CHUNK], F32)
-        y_tags = ("b_abs", "slot0", "slot1")
+        y_tags = ("w1_raw00", "w1_raw10", "w1_raw11")
         for first in range(0, M, CHUNK):
             for t in range(PACK):
                 fetch_exemplar(exemplar4[:, t * CHUNK : (t + 1) * CHUNK], PACK + t, first, CHUNK)
@@ -419,7 +426,7 @@ def tile_list_stemma_deviation_kernel(
                     )
                 nc.sync.dma_start(out=y_rows[:, :, first : first + CHUNK], in_=y[:])
             else:
-                for u, (z_tag, y_tag, queue) in enumerate((("bf0", "b_abs", nc.sync), ("bf2", "slot2", nc.scalar))):
+                for u, (z_tag, y_tag, queue) in enumerate((("bf0", "b_abs", nc.sync), ("bf2", "tab_w0", nc.scalar))):
                     column = first + u * UNIT
                     z_bf = sb("z1_bf%d" % column, [P, PACK * UNIT], BF16, tag=z_tag)
                     quantize_z(fetch_z1(first, u * UNIT, UNIT), z_bf[:], 1, column, UNIT, nc.vector.tensor_copy)

@@ -27,7 +27,7 @@ QUAD = 32
 LIST_ROWS = 16
 PAGE_SLOTS = 5
 RING = 3
-CHUNK = 256
+CHUNKS = (384, 384, 256)
 UNIT = 128
 EVEN_BANK = 4
 ODD_BANK = 6
@@ -72,10 +72,8 @@ def tile_list_stemma_deviation_kernel(
 
         tab_w = [sb("tab_w%d" % a, [P, T], I32) for a in range(2)]
         w2_w = [sb("w2_w%d" % g, [P, 2, 2 * PASS], U8) for g in range(2)]
-        wgs_dealt = sb("wgs_dealt", [P, S], F32)
         wgs_rows = sb("wgs_rows", [P, S], F32)
         w3_w_raw = sb("w3_w_raw", [P, 2, N], I32)
-        w1_raw = {}
         pages = {}
 
         def load_tab_words(a):
@@ -100,131 +98,132 @@ def tile_list_stemma_deviation_kernel(
                 in_=w2_words[:, :, g * 2 * PASS : (g + 1) * 2 * PASS].bitcast(I32).rearrange("a p c -> p a c"),
             )
 
-        def load_w1(a, g):
-            w1_raw[a, g] = sb("w1_raw%d%d" % (a, g), [P, PACK, PASS], F32)
-            nc.sync.dma_start(
-                out=w1_raw[a, g][:],
-                in_=w1[a * PASS : (a + 1) * PASS, g * PASS : (g + 1) * PASS].rearrange("(p i) c -> p i c", i=PACK),
-            )
-
-        def load_wgs_dealt():
-            rows = wgs.rearrange("(q t) j -> q t j", t=PACK)
-            for quad in range(4):
-                nc.sync.dma_start(out=wgs_dealt[QUAD * quad : QUAD * (quad + 1), :], in_=rows[:, 0, :])
+        def load_w1(name, first, count):
+            raw = sb(name, [P, 2, PACK * count], F32)
+            for a in range(2):
+                nc.sync.dma_start(
+                    out=raw[:, a, :].rearrange("p (i c) -> p i c", i=PACK),
+                    in_=w1[a * PASS : (a + 1) * PASS, first : first + count].rearrange("(p i) c -> p i c", i=PACK),
+                )
+            return raw
 
         def load_page(i):
-            g, t = divmod(i, PACK)
             pages[i] = sb("page%d" % i, [P, T2], F32, tag="page", bufs=PAGE_SLOTS)
-            nc.sync.dma_start(
-                out=pages[i][:], in_=page0[g * PASS : (g + 1) * PASS, :].rearrange("(p t) c -> t p c", t=PACK)[t]
-            )
+            if i < PACK:
+                rows = page0[i * P : (i + 1) * P, :]
+            else:
+                rows = page0[PASS:, :].rearrange("(p t) c -> t p c", t=PACK)[i - PACK]
+            nc.sync.dma_start(out=pages[i][:], in_=rows)
 
+        load_tab_words(0)
         nc.sync.dma_start(idx[:], offs)
         nc.sync.dma_start(idx2[:], offs2)
-        load_w2_words(0)
         load_packed_scales(nc.sync, tab_s, tab_scales)
-        load_tab_words(0)
         load_tab_words(1)
+        load_w2_words(0)
         load_w2_scales(nc.sync)
+        w1_raw0 = load_w1("w1_raw0", 0, P)
         v_s = sb("v_s", [P, S], U8)
         nc.vector.tensor_copy(v_s[:], tab_s[:].indirect(idx[:]))
         live_end = 3 * QUAD + 4
         nc.sync.dma_start(out=v_s_moved[0:live_end, :].bitcast(I32), in_=v_s[4 : live_end + 4, :].bitcast(I32))
-        load_w1(0, 0)
-        load_w1(1, 0)
         load_page(0)
-        load_wgs_dealt()
         nc.sync.dma_start(out=wgs_rows[:], in_=wgs)
+        w1_raw12 = load_w1("w1_raw12", P, 2 * P)
         nc.sync.dma_start(idx4[:], offs4)
         nc.sync.dma_start(idx3[:], offs3)
-        nc.sync.dma_start(out=w3_w_raw[:], in_=w3_words.rearrange("a p c i -> p a (c i)").bitcast(I32))
-        load_packed_scales(nc.sync, w3_s_raw, w3_scales)
         load_page(1)
         load_w2_words(1)
-        load_w1(0, 1)
-        load_w1(1, 1)
-        for i in range(2, PAGE_SLOTS):
+        w1_raw3 = load_w1("w1_raw3", 3 * P, P)
+        nc.sync.dma_start(out=w3_w_raw[:], in_=w3_words.rearrange("a p c i -> p a (c i)").bitcast(I32))
+        load_packed_scales(nc.sync, w3_s_raw, w3_scales)
+        load_page(2)
+        w1_raw_g1 = load_w1("w1_raw_g1", PASS, PASS)
+        for i in range(3, PAGE_SLOTS):
             load_page(i)
+        warm = sb("warm", [P, 1], F32)
+        nc.scalar.activation(out=warm[:], in_=ident[:, 0:1], func=ACT.Abs_reciprocal_sqrt, bias=1.0)
 
-        v_both = sb("v_both", [P, 2 * S], U32, tag="tab_s")
-        v_w = [v_both[:, a * S : (a + 1) * S] for a in range(2)]
-        w1_w = [sb("w1_w%d" % g, [P, 2 * PASS], U32) for g in range(2)]
-        w1_s = [sb("w1_s%d" % g, [P, 2 * PASS], U8) for g in range(2)]
+        w1_w = [sb("w1_w%d" % i, [P, 2 * P], U32) for i in range(2 * PACK)]
+        w1_s = [sb("w1_s%d" % i, [P, 2 * P], U8) for i in range(2 * PACK)]
         factor_ring = [sb("factor%d" % i, [P, S], F32) for i in range(RING)]
-        a_ring = [sb("a%d" % i, [P, S], F32) for i in range(RING)]
+        a_ring = [sb("a%d" % i, [P, S], F32) for i in range(2)]
 
-        def gather_words(a, half):
-            nc.vector.tensor_copy(
-                v_w[a][:, half_cols(half)], tab_w[a][:].bitcast(U32).indirect(entries(idx, half * BANK, BANK))
-            )
+        v_half = {}
 
-        def round_w1(copy, grouped, g, pair, a):
-            copy(
-                out=grouped[:, a * 2 * PASS : (a + 1) * 2 * PASS].rearrange("p (u m i) -> p m u i", u=2, i=PACK),
-                in_=w1_raw[a, g][:].rearrange("p i (m t) -> p m t i", t=PACK)[:, :, 2 * pair : 2 * pair + 2, :],
-            )
-
-        def quantize_w1(grouped, g, pair, first_pass, passes):
-            cols = slice(pair * PASS + first_pass * 2 * P, pair * PASS + (first_pass + passes) * 2 * P)
-            nc.vector.quantize_mx(
-                out=w1_w[g][:, cols].bitcast(FP8X4),
-                scales=w1_s[g][:, cols],
-                in_=grouped[:, first_pass * 2 * PASS : (first_pass + passes) * 2 * PASS],
-            )
-
-        def abs_b(b_abs, g, jb, k):
-            bank = take_bank(k, "b_bank")
-            cols = slice(jb * P, (jb + 1) * P)
+        def gather_words(half, tag):
+            v_half[half] = sb("v_half%d" % half, [P, 2, BANK], U32, tag=tag)
             for a in range(2):
-                nc.tensor.matmul_mx(
-                    out=bank[:],
-                    lhsT=v_w[a][:, cols].bitcast(FP8X4),
-                    lhsT_scale=(v_s, v_s_moved)[a][:, cols],
-                    rhs=w2_w[g][:, a, :].bitcast(FP4X4),
-                    rhs_scale=w2_s[:, a * H + g * PASS : a * H + (g + 1) * PASS],
-                    start=(a == 0),
-                    stop=(a == 1),
+                nc.vector.tensor_copy(
+                    v_half[half][:, a, :], tab_w[a][:].bitcast(U32).indirect(entries(idx, half * BANK, BANK))
                 )
-            nc.scalar.activation(
-                out=b_abs[:].rearrange("j (t s) -> j t s", t=PACK)[:, :, cols],
-                in_=bank[:].rearrange("j (p t) -> j t p", t=PACK),
-                func=ACT.Abs,
+
+        def v_words(a, first, count):
+            half, start = divmod(first, BANK)
+            return v_half[half][:, a, start : start + count].bitcast(FP8X4)
+
+        def quantize_w1(grouped, first_tile):
+            for k in range(grouped.shape[1] // (2 * PASS)):
+                i = first_tile + k
+                nc.vector.quantize_mx(
+                    out=w1_w[i][:].bitcast(FP8X4), scales=w1_s[i][:], in_=grouped[:, k * 2 * PASS : (k + 1) * 2 * PASS]
+                )
+
+        def round_w1_tile(copy, grouped, raw):
+            copy(
+                out=grouped.rearrange("p (a c l i) -> p a c i l", a=2, l=LINE, i=PACK),
+                in_=raw[:].rearrange("p a (i c l) -> p a c i l", i=PACK, l=LINE),
             )
 
-        def product_a(i, half, first_bank):
-            cols = half_cols(half)
-            acc = take_bank(first_bank + half, "acc")
-            g, t = divmod(i, PACK)
+        def product_b(out, g, first, count, j_first, j_count, turned):
             for a in range(2):
-                first = (t // 2) * PASS + a * 2 * P + (t % 2) * P
-                wcols = slice(first, first + P)
+                w_side = w2_w[g][:, a, 2 * first : 2 * (first + count)].bitcast(FP4X4)
+                w_scale = w2_s[:, a * H + g * PASS + first : a * H + g * PASS + first + count]
+                v_side = v_words(a, j_first, j_count)
+                v_scale = (v_s, v_s_moved)[a][:, j_first : j_first + j_count]
+                sides = (v_side, v_scale, w_side, w_scale) if turned else (w_side, w_scale, v_side, v_scale)
+                nc.tensor.matmul_mx(
+                    out=out, lhsT=sides[0], lhsT_scale=sides[1], rhs=sides[2], rhs_scale=sides[3],
+                    start=(a == 0), stop=(a == 1),
+                )
+
+        def product_a(i, half, k):
+            cols = half_cols(half)
+            acc = take_bank(k, "acc")
+            for a in range(2):
+                wcols = slice(a * P, (a + 1) * P)
                 nc.tensor.matmul_mx(
                     out=acc[:],
-                    lhsT=w1_w[g][:, wcols].bitcast(FP8X4),
-                    lhsT_scale=w1_s[g][:, wcols],
-                    rhs=v_w[a][:, cols].bitcast(FP8X4),
+                    lhsT=w1_w[i][:, wcols].bitcast(FP8X4),
+                    lhsT_scale=w1_s[i][:, wcols],
+                    rhs=v_words(a, half * BANK, BANK),
                     rhs_scale=v_s[4 * a : P, cols],
                     start=(a == 0),
                     stop=(a == 1),
                 )
             return acc
 
-        def damped_a(half, root, h):
-            cols = half_cols(half)
-            turned = take_bank(ODD_BANK + half, "turned")
-            for q in range(4):
-                jb = half * 4 + q
-                nc.tensor.transpose(turned[:, q * P : (q + 1) * P], b_abs0[:, jb * P : (jb + 1) * P], ident[:])
-            nc.scalar.activation(out=root, in_=turned[:], func=ACT.Abs_reciprocal_sqrt, bias=1.0)
-            nc.scalar.activation(out=factor_ring[0][:, cols], in_=root, func=ACT.Square)
-            nc.vector.tensor_tensor(h, product_a(0, half, EVEN_BANK)[:], factor_ring[0][:, cols], ALU.mult)
+        def damping(i, half, scratch):
+            b_bank = take_bank(2 * (i % 2), "b_bank")
+            product_b(b_bank[:], 0, i * P, P, half * BANK, BANK, False)
+            nc.scalar.activation(out=scratch, in_=b_bank[:], func=ACT.Abs)
+            nc.scalar.activation(out=scratch, in_=scratch, func=ACT.Abs_reciprocal_sqrt, bias=1.0)
+            nc.scalar.activation(out=factor_ring[i][:, half_cols(half)], in_=scratch, func=ACT.Square)
+
+        def multiply_h(i, half, h):
+            acc = product_a(i, half, tile_banks(i) + min(i, 1) * half)
+            nc.vector.tensor_tensor(h, acc[:], factor_ring[i][:, half_cols(half)], ALU.mult)
+
+        def damped_a(i, half, scratch, h):
+            damping(i, half, scratch)
+            multiply_h(i, half, h)
 
         def tile_banks(i):
             return (EVEN_BANK, ODD_BANK)[i % 2]
 
-        def copy_a(i, first_bank):
+        def copy_a(i, dst):
             for half in range(2):
-                nc.scalar.copy(out=a_ring[i % RING][:, half_cols(half)], in_=product_a(i, half, first_bank)[:])
+                nc.scalar.copy(out=dst[:, half_cols(half)], in_=product_a(i, half, tile_banks(i) + half)[:])
 
         def factor_by_logs(log_b, i):
             t = i % PACK
@@ -233,7 +232,10 @@ def tile_list_stemma_deviation_kernel(
                 for q in range(4):
                     jb = half * 4 + q
                     dst = turned[:, q * P : (q + 1) * P]
-                    neg = neg_log_w[half][:, (t * 4 + q) * P : (t * 4 + q + 1) * P]
+                    if i < PACK:
+                        neg = neg_log_rows[:, jb * P : (jb + 1) * P]
+                    else:
+                        neg = neg_log_w[half][:, (t * 4 + q) * P : (t * 4 + q + 1) * P]
                     nc.tensor.matmul(
                         dst, log_b[:, jb * P : (jb + 1) * P], ident[:], start=True, stop=False, is_transpose=True
                     )
@@ -253,13 +255,6 @@ def tile_list_stemma_deviation_kernel(
         def fetch_difference(dst, exemplar, i, first, count):
             nc.vector.tensor_tensor(dst, pages[i][:].indirect(entries(idx3, first, count)), exemplar, ALU.subtract)
 
-        def fetch_z0(i):
-            for half in range(2):
-                fetch_exemplar(exemplar0[:, half_cols(half)], i, half * BANK, BANK)
-            for half in range(2):
-                cols = half_cols(half)
-                fetch_difference(z0_t[i][:, cols], exemplar0[:, cols], i, half * BANK, BANK)
-
         def interleave(copy, grouped, slices):
             copy(
                 out=grouped.rearrange("p (c i t) -> p c t i", i=LINE, t=PACK),
@@ -274,57 +269,101 @@ def tile_list_stemma_deviation_kernel(
             cols = slice(first, first + count)
             nc.vector.quantize_mx(out=z_w[g][:, cols].bitcast(FP8X4), scales=z_s[g][:, cols], in_=grouped)
 
-        for half in range(2):
-            for a in range(2):
-                gather_words(a, half)
-        w1_bf = sb("w1_bf00", [P, 4 * PASS], BF16, tag="bf0")
-        for a in range(2):
-            round_w1(nc.vector.tensor_copy, w1_bf[:], 0, 0, a)
-            quantize_w1(w1_bf[:], 0, 0, a, 1)
-        b_abs0 = sb("b_abs0", [P, PACK * S], F32, tag="b_abs")
+        gather_words(0, "tab_s")
+        w1_bf0 = sb("w1_bf0", [P, 2 * PASS], BF16, tag="v_late")
+        round_w1_tile(nc.vector.tensor_copy, w1_bf0[:], w1_raw0)
+        quantize_w1(w1_bf0[:], 0)
+        gather_words(1, "v_late")
         z0 = sb("z0", [P, PACK * M], F32)
         z0_t = [z0[:, t * M : (t + 1) * M] for t in range(PACK)]
-        exemplar0 = sb("exemplar0", [P, M], F32)
-        for jb in range(4):
-            abs_b(b_abs0, 0, jb, jb)
-        h0 = sb("h0", [P, BANK], F32, tag="w3_w")
-        damped_a(0, b_abs0[:, BANK:S], h0[:])
-        scatter(0, h0[:], wgs_dealt, 0, BANK)
-        for jb in range(4, BLOCKS):
-            abs_b(b_abs0, 0, jb, jb - 4)
-        log_w, log_b1st = z0[:, BANK : BANK + S], z0[:, BANK + S : BANK + 2 * S]
-        damped_a(1, z0[:, M + BANK // 2 : M + 3 * BANK // 2], h0[:])
-        scatter(0, h0[:], wgs_dealt, BANK, BANK)
+        shared = sb("shared", [P, 2 * M], F32)
+        exemplars = [shared[:, 0:M], shared[:, M:]]
+        h0 = sb("h0", [P, BANK], F32, tag="bf1")
+        damped_a(0, 0, shared[:, M - BANK // 2 : M + BANK // 2], h0[:])
+        scatter(0, h0[:], wgs_rows, 0, BANK)
+        damping(1, 0, shared[:, BANK:M])
+        damped_a(0, 1, shared[:, M : M + BANK], h0[:])
+        scatter(0, h0[:], wgs_rows, BANK, BANK)
 
-        w1_bf = sb("w1_bf01", [P, 4 * PASS], BF16, tag="bf1")
-        for a in range(2):
-            round_w1(nc.vector.tensor_copy, w1_bf[:], 0, 1, a)
-        quantize_w1(w1_bf[:], 0, 1, 0, 2)
+        w1_bf12 = sb("w1_bf12", [P, 4 * PASS], BF16, tag="bf0")
+        for t in range(2):
+            nc.scalar.copy(
+                out=w1_bf12[:].rearrange("p (t a c l i) -> p t a c i l", t=2, a=2, l=LINE, i=PACK)[:, t],
+                in_=w1_raw12[:].rearrange("p a (i t c l) -> p t a c i l", i=PACK, t=2, l=LINE)[:, t],
+            )
+        quantize_w1(w1_bf12[:], 1)
+        multiply_h(1, 0, a_ring[1][:, 0:BANK])
+        damped_a(1, 1, shared[:, M + BANK :], a_ring[1][:, BANK:S])
+        fetch_exemplar(exemplars[0], 0, 0, M)
+        fetch_difference(z0_t[0], exemplars[0], 0, 0, M)
+        scatter(1, a_ring[1][:], wgs_rows, 0, S)
+        load_page(PAGE_SLOTS)
+        log_w = sb("log_w", [P, S], F32)
+        damped_a(2, 0, shared[:, M : M + BANK], a_ring[0][:, 0:BANK])
+        damped_a(2, 1, log_w[:, 0:BANK], a_ring[0][:, BANK:S])
+        fetch_exemplar(exemplars[1], 1, 0, M)
+        fetch_difference(z0_t[1], exemplars[1], 1, 0, M)
+        scatter(2, a_ring[0][:], wgs_rows, 0, S)
+        load_page(PAGE_SLOTS + 1)
 
-        nc.scalar.activation(out=log_w, in_=wgs_rows[:], func=ACT.Ln)
-        nc.scalar.activation(out=log_b1st, in_=b_abs0[:, S : 2 * S], func=ACT.Ln, bias=1.0)
+        w1_bf3 = sb("w1_bf3", [P, 2 * PASS], BF16, tag="bf1")
+        round_w1_tile(nc.scalar.copy, w1_bf3[:], w1_raw3)
+        quantize_w1(w1_bf3[:], 3)
+
+        log_b3 = sb("log_b3", [P, S], F32)
+        for half in range(2):
+            bank = take_bank(2 * half, "b_bank")
+            for q in range(4):
+                product_b(bank[:, q * P : (q + 1) * P], 0, 3 * P, P, half * BANK + q * P, P, True)
+            nc.scalar.activation(out=log_b3[:, half_cols(half)], in_=bank[:], func=ACT.Abs)
+        nc.scalar.activation(out=log_w[:], in_=wgs_rows[:], func=ACT.Ln)
+        nc.scalar.activation(out=log_b3[:], in_=log_b3[:], func=ACT.Ln, bias=1.0)
         neg_log_w = [sb("neg_log_w%d" % half, [P, PACK * BANK], F32, tag="tab_w%d" % half) for half in range(2)]
         log_w_turned = []
         for half in range(2):
-            bank = take_bank(half, "log_w_turned")
+            bank = take_bank(2 * half + 1, "log_w_turned")
             for q in range(4):
                 jb = half * 4 + q
                 nc.tensor.transpose(bank[:, q * P : (q + 1) * P], log_w[:, jb * P : (jb + 1) * P], ident[:])
             log_w_turned.append(bank)
 
-        def spread_log_w(t):
-            for half in range(2):
-                rows = log_w_turned[half][:].rearrange("j (b q t) -> j t b q", t=PACK, b=4)[:, t]
-                dst = neg_log_w[half][:, t * BANK : (t + 1) * BANK]
-                nc.scalar.activation(
-                    out=dst.rearrange("j (b r q) -> j b r q", r=4, q=QUAD),
-                    in_=rows.unsqueeze(2).to_broadcast([P, 4, 4, QUAD]),
-                    func=ACT.Copy,
-                    scale=-1.0,
-                )
+        neg_log_rows = sb("neg_log_rows", [P, S], F32)
+        for half in range(2):
+            nc.scalar.activation(
+                out=neg_log_rows[:, half_cols(half)], in_=log_w_turned[half][:], func=ACT.Copy, scale=-1.0
+            )
 
-        fetch_z0(0)
-        w3_w = sb("w3_w", [P, 2, N], I32)
+        for half in range(2):
+            spread = neg_log_w[half][:].rearrange("j (s r q) -> j s r q", r=4, q=QUAD)
+            nc.scalar.activation(
+                out=spread[:, :, 0, :].rearrange("j (t b) q -> j t b q", t=PACK),
+                in_=log_w_turned[half][:].rearrange("j (b q t) -> j t b q", t=PACK, b=4),
+                func=ACT.Copy,
+                scale=-1.0,
+            )
+            for r in range(1, 4):
+                nc.sync.dma_start(out=spread[:, :, r, :], in_=spread[:, :, 0, :])
+
+        def scatter_by_logs(i, log_b):
+            values = a_ring[i % 2][:]
+            factor_by_logs(log_b, i)
+            copy_a(i, values)
+            scatter(i, values, factor_ring[i % RING], 0, S)
+
+        def round_w1_pair(pair):
+            grouped = sb("w1_bf_pair%d" % pair, [P, PACK * PASS], BF16, tag=("log_w", "w1_w4")[pair])[:]
+            for a in range(2):
+                nc.scalar.copy(
+                    out=grouped.rearrange("p (u a m i) -> p a m u i", u=2, a=2, i=PACK)[:, a],
+                    in_=w1_raw_g1[:, a, :].rearrange("p (i m t) -> p m t i", i=PACK, t=PACK)[
+                        :, :, 2 * pair : 2 * pair + 2, :
+                    ],
+                )
+            quantize_w1(grouped, PACK + 2 * pair)
+
+        round_w1_pair(0)
+        scatter_by_logs(3, log_b3[:])
+        w3_w = sb("w3_w", [P, 2, N], I32, tag="log_b3")
         w3_s = sb("w3_s", [P, N], U8)
         nc.vector.tensor_copy(
             out=w3_w[:].rearrange("p a (t m) -> p a m t", t=PACK),
@@ -334,42 +373,53 @@ def tile_list_stemma_deviation_kernel(
             out=w3_s[:].rearrange("p (t m) -> p m t", t=PACK),
             in_=w3_s_raw[:].rearrange("p (m t) -> p m t", t=PACK),
         )
+        exemplar2 = sb("exemplar2", [P, M], F32, tag="w1_w3")
+        fetch_exemplar(exemplar2[:], 2, 0, M)
+        fetch_difference(z0_t[2], exemplar2[:], 2, 0, M)
+        load_page(PAGE_SLOTS + 2)
+        fetch_exemplar(exemplars[0], 3, 0, M)
+        fetch_difference(z0_t[3], exemplars[0], 3, 0, M)
 
-        log_b0 = {1: log_b1st, 2: z0_t[2], 3: z0_t[3]}
-        for i in range(1, PACK):
-            spread_log_w(i)
-            if i == 1:
-                copy_a(i, 2)
-            factor_by_logs(log_b0[i], i)
-            if i == 1:
-                nc.scalar.activation(
-                    out=z0[:, 2 * M :], in_=b_abs0[:, 2 * S :], func=ACT.Ln, bias=1.0
-                )
-            if i > 1:
-                copy_a(i, tile_banks(i))
-            scatter(i, a_ring[i % RING][:], factor_ring[i % RING], 0, S)
-            load_page(PAGE_SLOTS + i - 1)
-            fetch_z0(i)
-            if i < PACK - 1:
-                pair = i - 1
-                w1_bf = sb("w1_bf1%d" % pair, [P, 4 * PASS], BF16, tag="bf%d" % pair)
-                for a in range(2):
-                    round_w1(nc.scalar.copy, w1_bf[:], 1, pair, a)
-                quantize_w1(w1_bf[:], 1, pair, 0, 2)
-        spread_log_w(0)
 
         log_b1 = sb("log_b1", [P, PACK * S], F32, tag="b_abs")
         for jb in range(BLOCKS):
-            abs_b(log_b1, 1, jb, (2 if jb < BLOCKS - 2 else ODD_BANK) + jb % 2)
+            bank = take_bank(2 * (jb % 2) if jb < BLOCKS - 2 else ODD_BANK + jb % 2, "b_bank")
+            product_b(bank[:], 1, 0, PASS, jb * P, P, True)
+            nc.scalar.activation(
+                out=log_b1[:].rearrange("j (t s) -> j t s", t=PACK)[:, :, jb * P : (jb + 1) * P],
+                in_=bank[:].rearrange("j (p t) -> j t p", t=PACK),
+                func=ACT.Abs,
+            )
         nc.scalar.activation(out=log_b1[:], in_=log_b1[:], func=ACT.Ln, bias=1.0)
         for t in range(PACK):
-            i = PACK + t
-            factor_by_logs(log_b1[:, t * S : (t + 1) * S], i)
-            copy_a(i, tile_banks(i))
-            scatter(i, a_ring[i % RING][:], factor_ring[i % RING], 0, S)
+            scatter_by_logs(PACK + t, log_b1[:, t * S : (t + 1) * S])
+            if t == 0:
+                round_w1_pair(1)
 
-        z0_bf = sb("z0_bf", [P, PACK * M], BF16, tag="b_abs")
-        quantize_z(z0[:], z0_bf[:], 0, 0, M, nc.scalar.copy)
+        z0_turned = sb("z0_turned", [P, BLOCKS, PASS], BF16, tag="log_w")
+        z0_bf = sb("z0_bf", [P, PACK * M], BF16, tag="w1_raw_g1")
+        for pair in range(BLOCKS // 2):
+            back = take_bank(2 * (pair % 2), "z_back")
+            for k in range(2):
+                mb = 2 * pair + k
+                bank = take_bank(EVEN_BANK + k, "z_turned")
+                for i in range(PACK):
+                    nc.tensor.transpose(bank[:, i * P : (i + 1) * P], z0_t[i][:, mb * P : (mb + 1) * P], ident[:])
+                nc.scalar.copy(
+                    out=z0_turned[:, mb, :].rearrange("m (u p e) -> m u p e", u=2, e=2),
+                    in_=bank[:].rearrange("m (p u e) -> m u p e", u=2, e=2),
+                )
+                words = z0_turned[:, mb, :].bitcast(F32)
+                for u in range(2):
+                    first = (2 * k + u) * P
+                    nc.tensor.transpose(back[:, first : first + P], words[:, u * P : (u + 1) * P], ident[:])
+            nc.scalar.copy(
+                out=z0_bf[:, pair * 2 * PASS : (pair + 1) * 2 * PASS].bitcast(F32).rearrange(
+                    "p (k m u) -> p k m u", k=2, u=2
+                ),
+                in_=back[:].rearrange("p (k u m) -> p k m u", k=2, u=2),
+            )
+        nc.vector.quantize_mx(out=z_w[0][:].bitcast(FP8X4), scales=z_s[0][:], in_=z0_bf[:])
 
         y_w = sb("y_w", [P, M], U32)
         y_s = sb("y_s", [P, M], U8)
@@ -392,49 +442,57 @@ def tile_list_stemma_deviation_kernel(
                     )
             return acc
 
-        def fetch_z1(first, start, count):
+        def fetch_z1(first, width, start, count):
             z = z1[:, PACK * start : PACK * (start + count)]
             for t in range(PACK):
-                exemplar = exemplar4[:, t * CHUNK + start : t * CHUNK + start + count]
+                exemplar = exemplar4[:, t * width + start : t * width + start + count]
                 fetch_difference(z[:, t * count : (t + 1) * count], exemplar, PACK + t, first + start, count)
             return z
 
-        def store_planes(first, y_bf):
-            cols = slice(first, first + CHUNK)
-            nc.vector.quantize_mx(out=y_w[:, cols].bitcast(FP8X4), scales=y_s[:, cols], in_=y_bf[:])
-            nc.sync.dma_start(out=y_words[:, cols], in_=y_w[:, cols].bitcast(I32))
+        def abs_float(y, acc):
+            nc.scalar.activation(out=y, in_=acc, func=ACT.Abs)
 
-        exemplar4 = a_ring[(2 * PACK - 1) % RING]
-        z1 = sb("z1", [P, PACK * CHUNK], F32)
-        y_tags = ("w1_raw00", "w1_raw10", "w1_raw11")
-        for first in range(0, M, CHUNK):
+        def abs_rounded(y_bf, acc):
+            nc.scalar.activation(
+                out=y_bf.rearrange("p (m t) -> p m t", t=PACK), in_=acc.rearrange("p t m -> p m t"), func=ACT.Abs
+            )
+
+        exemplar4 = sb("exemplar4", [P, PACK * max(CHUNKS)], F32, tag="w1_w%d" % (2 * PACK - 1))
+        z1 = sb("z1", [P, PACK * max(CHUNKS)], F32, tag="shared")
+        y_tags = ("w1_raw0", "w1_raw12", "w1_raw3")
+        first = 0
+        for chunk, width in enumerate(CHUNKS):
             for t in range(PACK):
-                fetch_exemplar(exemplar4[:, t * CHUNK : (t + 1) * CHUNK], PACK + t, first, CHUNK)
-            y_bf = sb("y_bf%d" % first, [P, CHUNK * PACK], BF16, tag="bf1")
-            y_bf_units = [y_bf[:, u * UNIT * PACK : (u + 1) * UNIT * PACK] for u in range(CHUNK // UNIT)]
-            if first + CHUNK < M:
-                z_bf = sb("z1_bf%d" % first, [P, PACK * CHUNK], BF16, tag="bf0")
-                quantize_z(fetch_z1(first, 0, CHUNK), z_bf[:], 1, first, CHUNK, nc.scalar.copy)
-                y = sb("y%d" % first, [P, PACK, CHUNK], F32, tag=y_tags[first // CHUNK])
-                for u in range(CHUNK // UNIT):
+                fetch_exemplar(exemplar4[:, t * width : (t + 1) * width], PACK + t, first, width)
+            y_bf = sb("y_bf%d" % chunk, [P, width * PACK], BF16, tag="bf1")
+            y_bf_units = [y_bf[:, u * UNIT * PACK : (u + 1) * UNIT * PACK] for u in range(width // UNIT)]
+            if first + width < M:
+                z_bf = sb("z1_bf%d" % chunk, [P, PACK * width], BF16, tag="log_w")
+                quantize_z(fetch_z1(first, width, 0, width), z_bf[:], 1, first, width, nc.scalar.copy)
+                y = sb("y%d" % chunk, [P, PACK, width], F32, tag=y_tags[chunk])
+                for u in range(width // UNIT):
                     acc = product_y(first + u * UNIT)
-                    nc.scalar.activation(out=y[:, :, u * UNIT : (u + 1) * UNIT], in_=acc, func=ACT.Abs)
-                    nc.scalar.activation(
-                        out=y_bf_units[u].rearrange("p (m t) -> p m t", t=PACK),
-                        in_=acc.rearrange("p t m -> p m t"),
-                        func=ACT.Abs,
-                    )
-                nc.sync.dma_start(out=y_rows[:, :, first : first + CHUNK], in_=y[:])
+                    abs_float(y[:, :, u * UNIT : (u + 1) * UNIT], acc)
+                    abs_rounded(y_bf_units[u], acc)
+                nc.sync.dma_start(out=y_rows[:, :, first : first + width], in_=y[:])
             else:
                 for u, (z_tag, y_tag, queue) in enumerate((("bf0", "b_abs", nc.sync), ("bf2", "tab_w0", nc.scalar))):
                     column = first + u * UNIT
                     z_bf = sb("z1_bf%d" % column, [P, PACK * UNIT], BF16, tag=z_tag)
-                    quantize_z(fetch_z1(first, u * UNIT, UNIT), z_bf[:], 1, column, UNIT, nc.vector.tensor_copy)
+                    quantize_z(fetch_z1(first, width, u * UNIT, UNIT), z_bf[:], 1, column, UNIT, nc.vector.tensor_copy)
                     y = sb("y%d" % column, [P, PACK, UNIT], F32, tag=y_tag)
-                    nc.scalar.activation(out=y[:], in_=product_y(column), func=ACT.Abs)
-                    interleave(nc.vector.tensor_copy, y_bf_units[u], y[:])
+                    acc = product_y(column)
+                    if u == 0:
+                        abs_float(y[:], acc)
+                        interleave(nc.vector.tensor_copy, y_bf_units[u], y[:])
+                    else:
+                        abs_rounded(y_bf_units[u], acc)
+                        abs_float(y[:], acc)
                     queue.dma_start(out=y_rows[:, :, column : column + UNIT], in_=y[:])
-            store_planes(first, y_bf)
+            cols = slice(first, first + width)
+            nc.vector.quantize_mx(out=y_w[:, cols].bitcast(FP8X4), scales=y_s[:, cols], in_=y_bf[:])
+            nc.sync.dma_start(out=y_words[:, cols], in_=y_w[:, cols].bitcast(I32))
+            first = first + width
         for q in range(4):
             (nc.sync, nc.scalar)[q % 2].dma_start(
                 out=out_2[0, 4 * q : 4 * q + 4, :].bitcast(I32), in_=y_s[QUAD * q : QUAD * q + 4, :].bitcast(I32)

@@ -129,7 +129,7 @@ def tile_list_stemma_deviation_kernel(
         nc.sync.dma_start(out=v_s_moved[0:live_end, :].bitcast(I32), in_=v_s[4 : live_end + 4, :].bitcast(I32))
         load_page(0)
         nc.sync.dma_start(out=wgs_rows[:], in_=wgs)
-        w1_raw12 = load_w1("w1_raw12", P, 2 * P)
+        w1_raw12 = [load_w1("w1_raw%d" % i, i * P, P) for i in (1, 2)]
         nc.sync.dma_start(idx4[:], offs4)
         nc.sync.dma_start(idx3[:], offs3)
         load_page(1)
@@ -278,20 +278,16 @@ def tile_list_stemma_deviation_kernel(
         z0_t = [z0[:, t * M : (t + 1) * M] for t in range(PACK)]
         shared = sb("shared", [P, 2 * M], F32)
         exemplars = [shared[:, 0:M], shared[:, M:]]
-        h0 = sb("h0", [P, BANK], F32, tag="bf1")
-        damped_a(0, 0, shared[:, M - BANK // 2 : M + BANK // 2], h0[:])
-        scatter(0, h0[:], wgs_rows, 0, BANK)
+        damped_a(0, 0, shared[:, M - BANK // 2 : M + BANK // 2], a_ring[0][:, 0:BANK])
+        scatter(0, a_ring[0][:, 0:BANK], wgs_rows, 0, BANK)
         damping(1, 0, shared[:, BANK:M])
-        damped_a(0, 1, shared[:, M : M + BANK], h0[:])
-        scatter(0, h0[:], wgs_rows, BANK, BANK)
+        damped_a(0, 1, shared[:, M : M + BANK], a_ring[0][:, BANK:S])
+        scatter(0, a_ring[0][:, BANK:S], wgs_rows, BANK, BANK)
 
-        w1_bf12 = sb("w1_bf12", [P, 4 * PASS], BF16, tag="bf0")
-        for t in range(2):
-            nc.scalar.copy(
-                out=w1_bf12[:].rearrange("p (t a c l i) -> p t a c i l", t=2, a=2, l=LINE, i=PACK)[:, t],
-                in_=w1_raw12[:].rearrange("p a (i t c l) -> p t a c i l", i=PACK, t=2, l=LINE)[:, t],
-            )
-        quantize_w1(w1_bf12[:], 1)
+        for i in (1, 2):
+            grouped = sb("w1_bf%d" % i, [P, 2 * PASS], BF16, tag=("bf0", "bf2")[i - 1])
+            round_w1_tile(nc.scalar.copy, grouped[:], w1_raw12[i - 1])
+            quantize_w1(grouped[:], i)
         multiply_h(1, 0, a_ring[1][:, 0:BANK])
         damped_a(1, 1, shared[:, M + BANK :], a_ring[1][:, BANK:S])
         fetch_exemplar(exemplars[0], 0, 0, M)
@@ -327,22 +323,22 @@ def tile_list_stemma_deviation_kernel(
                 nc.tensor.transpose(bank[:, q * P : (q + 1) * P], log_w[:, jb * P : (jb + 1) * P], ident[:])
             log_w_turned.append(bank)
 
-        neg_log_rows = sb("neg_log_rows", [P, S], F32)
+        neg_log_rows = sb("neg_log_rows", [P, S], F32, tag="w1_raw2")
         for half in range(2):
             nc.scalar.activation(
                 out=neg_log_rows[:, half_cols(half)], in_=log_w_turned[half][:], func=ACT.Copy, scale=-1.0
             )
 
-        for half in range(2):
-            spread = neg_log_w[half][:].rearrange("j (s r q) -> j s r q", r=4, q=QUAD)
-            nc.scalar.activation(
-                out=spread[:, :, 0, :].rearrange("j (t b) q -> j t b q", t=PACK),
-                in_=log_w_turned[half][:].rearrange("j (b q t) -> j t b q", t=PACK, b=4),
-                func=ACT.Copy,
-                scale=-1.0,
-            )
-            for r in range(1, 4):
-                nc.sync.dma_start(out=spread[:, :, r, :], in_=spread[:, :, 0, :])
+        def spread_log_w(t):
+            for half in range(2):
+                rows = log_w_turned[half][:].rearrange("j (b q t) -> j t b q", t=PACK, b=4)[:, t]
+                dst = neg_log_w[half][:, t * BANK : (t + 1) * BANK]
+                nc.scalar.activation(
+                    out=dst.rearrange("j (b r q) -> j b r q", r=4, q=QUAD),
+                    in_=rows.unsqueeze(2).to_broadcast([P, 4, 4, QUAD]),
+                    func=ACT.Copy,
+                    scale=-1.0,
+                )
 
         def scatter_by_logs(i, log_b):
             values = a_ring[i % 2][:]
@@ -363,21 +359,21 @@ def tile_list_stemma_deviation_kernel(
 
         round_w1_pair(0)
         scatter_by_logs(3, log_b3[:])
-        w3_w = sb("w3_w", [P, 2, N], I32, tag="log_b3")
-        w3_s = sb("w3_s", [P, N], U8)
+        exemplar2 = sb("exemplar2", [P, M], F32, tag="w1_w3")
+        fetch_exemplar(exemplar2[:], 2, 0, M)
+        w3_w = sb("w3_w", [P, 2, N], I32, tag="w1_s3")
         nc.vector.tensor_copy(
             out=w3_w[:].rearrange("p a (t m) -> p a m t", t=PACK),
             in_=w3_w_raw[:].rearrange("p a (m t) -> p a m t", t=PACK),
         )
+        fetch_difference(z0_t[2], exemplar2[:], 2, 0, M)
+        load_page(PAGE_SLOTS + 2)
+        fetch_exemplar(exemplars[0], 3, 0, M)
+        w3_s = sb("w3_s", [P, N], U8, tag="w1_w3")
         nc.vector.tensor_copy(
             out=w3_s[:].rearrange("p (t m) -> p m t", t=PACK),
             in_=w3_s_raw[:].rearrange("p (m t) -> p m t", t=PACK),
         )
-        exemplar2 = sb("exemplar2", [P, M], F32, tag="w1_w3")
-        fetch_exemplar(exemplar2[:], 2, 0, M)
-        fetch_difference(z0_t[2], exemplar2[:], 2, 0, M)
-        load_page(PAGE_SLOTS + 2)
-        fetch_exemplar(exemplars[0], 3, 0, M)
         fetch_difference(z0_t[3], exemplars[0], 3, 0, M)
 
 
@@ -392,6 +388,7 @@ def tile_list_stemma_deviation_kernel(
             )
         nc.scalar.activation(out=log_b1[:], in_=log_b1[:], func=ACT.Ln, bias=1.0)
         for t in range(PACK):
+            spread_log_w(t)
             scatter_by_logs(PACK + t, log_b1[:, t * S : (t + 1) * S])
             if t == 0:
                 round_w1_pair(1)
@@ -459,7 +456,7 @@ def tile_list_stemma_deviation_kernel(
 
         exemplar4 = sb("exemplar4", [P, PACK * max(CHUNKS)], F32, tag="w1_w%d" % (2 * PACK - 1))
         z1 = sb("z1", [P, PACK * max(CHUNKS)], F32, tag="shared")
-        y_tags = ("w1_raw0", "w1_raw12", "w1_raw3")
+        y_tags = ("w1_raw0", "w1_raw1")
         first = 0
         for chunk, width in enumerate(CHUNKS):
             for t in range(PACK):
@@ -469,12 +466,13 @@ def tile_list_stemma_deviation_kernel(
             if first + width < M:
                 z_bf = sb("z1_bf%d" % chunk, [P, PACK * width], BF16, tag="log_w")
                 quantize_z(fetch_z1(first, width, 0, width), z_bf[:], 1, first, width, nc.scalar.copy)
-                y = sb("y%d" % chunk, [P, PACK, width], F32, tag=y_tags[chunk])
+                y = sb("y%d" % chunk, [P, width // UNIT, PACK, UNIT], F32, tag=y_tags[chunk])
                 for u in range(width // UNIT):
                     acc = product_y(first + u * UNIT)
-                    abs_float(y[:, :, u * UNIT : (u + 1) * UNIT], acc)
+                    abs_float(y[:, u], acc)
+                    column = first + u * UNIT
+                    nc.sync.dma_start(out=y_rows[:, :, column : column + UNIT], in_=y[:, u])
                     abs_rounded(y_bf_units[u], acc)
-                nc.sync.dma_start(out=y_rows[:, :, first : first + width], in_=y[:])
             else:
                 for u, (z_tag, y_tag, queue) in enumerate((("bf0", "b_abs", nc.sync), ("bf2", "tab_w0", nc.scalar))):
                     column = first + u * UNIT
@@ -482,12 +480,8 @@ def tile_list_stemma_deviation_kernel(
                     quantize_z(fetch_z1(first, width, u * UNIT, UNIT), z_bf[:], 1, column, UNIT, nc.vector.tensor_copy)
                     y = sb("y%d" % column, [P, PACK, UNIT], F32, tag=y_tag)
                     acc = product_y(column)
-                    if u == 0:
-                        abs_float(y[:], acc)
-                        interleave(nc.vector.tensor_copy, y_bf_units[u], y[:])
-                    else:
-                        abs_rounded(y_bf_units[u], acc)
-                        abs_float(y[:], acc)
+                    abs_float(y[:], acc)
+                    interleave(nc.vector.tensor_copy, y_bf_units[u], y[:])
                     queue.dma_start(out=y_rows[:, :, column : column + UNIT], in_=y[:])
             cols = slice(first, first + width)
             nc.vector.quantize_mx(out=y_w[:, cols].bitcast(FP8X4), scales=y_s[:, cols], in_=y_bf[:])

@@ -235,7 +235,7 @@ def tile_list_stemma_deviation_kernel(
                     if i < PACK:
                         neg = neg_log_rows[:, jb * P : (jb + 1) * P]
                     else:
-                        neg = neg_log_w[half][:, (t * 4 + q) * P : (t * 4 + q + 1) * P]
+                        neg = neg_log_w[t][:, jb * P : (jb + 1) * P]
                     nc.tensor.matmul(
                         dst, log_b[:, jb * P : (jb + 1) * P], ident[:], start=True, stop=False, is_transpose=True
                     )
@@ -289,32 +289,33 @@ def tile_list_stemma_deviation_kernel(
             round_w1_tile(nc.scalar.copy, grouped[:], w1_raw12[i - 1])
             quantize_w1(grouped[:], i)
         multiply_h(1, 0, a_ring[1][:, 0:BANK])
-        damped_a(1, 1, shared[:, M + BANK :], a_ring[1][:, BANK:S])
+        log_w = sb("log_w", [P, S], F32, tag="w1_raw0")
+        damped_a(1, 1, log_w[:, 0:BANK], a_ring[1][:, BANK:S])
         fetch_exemplar(exemplars[0], 0, 0, M)
         fetch_difference(z0_t[0], exemplars[0], 0, 0, M)
         scatter(1, a_ring[1][:], wgs_rows, 0, S)
         load_page(PAGE_SLOTS)
-        log_w = sb("log_w", [P, S], F32)
-        damped_a(2, 0, shared[:, M : M + BANK], a_ring[0][:, 0:BANK])
-        damped_a(2, 1, log_w[:, 0:BANK], a_ring[0][:, BANK:S])
-        fetch_exemplar(exemplars[1], 1, 0, M)
-        fetch_difference(z0_t[1], exemplars[1], 1, 0, M)
-        scatter(2, a_ring[0][:], wgs_rows, 0, S)
-        load_page(PAGE_SLOTS + 1)
 
+        log_b0 = sb("log_b0", [P, 2 * S], F32, tag="tab_w0")
+        for pair in range(BLOCKS // 2):
+            bank = take_bank(2 * (pair % 2), "b_bank")
+            for k in range(2):
+                product_b(bank[:, k * 2 * P : (k + 1) * 2 * P], 0, 2 * P, 2 * P, (2 * pair + k) * P, P, True)
+            nc.scalar.activation(
+                out=log_b0[:].rearrange("j (t b p) -> j t b p", t=2, p=P)[:, :, 2 * pair : 2 * pair + 2, :],
+                in_=bank[:].rearrange("j (b t p) -> j t b p", t=2, p=P),
+                func=ACT.Abs,
+            )
         w1_bf3 = sb("w1_bf3", [P, 2 * PASS], BF16, tag="bf1")
         round_w1_tile(nc.scalar.copy, w1_bf3[:], w1_raw3)
         quantize_w1(w1_bf3[:], 3)
-
-        log_b3 = sb("log_b3", [P, S], F32)
-        for half in range(2):
-            bank = take_bank(2 * half, "b_bank")
-            for q in range(4):
-                product_b(bank[:, q * P : (q + 1) * P], 0, 3 * P, P, half * BANK + q * P, P, True)
-            nc.scalar.activation(out=log_b3[:, half_cols(half)], in_=bank[:], func=ACT.Abs)
+        exemplar1 = sb("exemplar1", [P, M], F32, tag="w1_raw3")
+        fetch_exemplar(exemplar1[:], 1, 0, M)
+        fetch_difference(z0_t[1], exemplar1[:], 1, 0, M)
+        load_page(PAGE_SLOTS + 1)
         nc.scalar.activation(out=log_w[:], in_=wgs_rows[:], func=ACT.Ln)
-        nc.scalar.activation(out=log_b3[:], in_=log_b3[:], func=ACT.Ln, bias=1.0)
-        neg_log_w = [sb("neg_log_w%d" % half, [P, PACK * BANK], F32, tag="tab_w%d" % half) for half in range(2)]
+        nc.scalar.activation(out=log_b0[:], in_=log_b0[:], func=ACT.Ln, bias=1.0)
+        neg_log_w = {}
         log_w_turned = []
         for half in range(2):
             bank = take_bank(2 * half + 1, "log_w_turned")
@@ -330,9 +331,12 @@ def tile_list_stemma_deviation_kernel(
             )
 
         def spread_log_w(t):
+            if t % 2 == 0:
+                both = sb("neg_log_w%d" % t, [P, 2 * S], F32, tag=("tab_w0", "w1_s4")[t // 2])
+                neg_log_w[t], neg_log_w[t + 1] = both[:, 0:S], both[:, S:]
             for half in range(2):
                 rows = log_w_turned[half][:].rearrange("j (b q t) -> j t b q", t=PACK, b=4)[:, t]
-                dst = neg_log_w[half][:, t * BANK : (t + 1) * BANK]
+                dst = neg_log_w[t][:, half_cols(half)]
                 nc.scalar.activation(
                     out=dst.rearrange("j (b r q) -> j b r q", r=4, q=QUAD),
                     in_=rows.unsqueeze(2).to_broadcast([P, 4, 4, QUAD]),
@@ -342,12 +346,15 @@ def tile_list_stemma_deviation_kernel(
 
         def scatter_by_logs(i, log_b):
             values = a_ring[i % 2][:]
+            if i == 2:
+                copy_a(i, values)
             factor_by_logs(log_b, i)
-            copy_a(i, values)
+            if i != 2:
+                copy_a(i, values)
             scatter(i, values, factor_ring[i % RING], 0, S)
 
         def round_w1_pair(pair):
-            grouped = sb("w1_bf_pair%d" % pair, [P, PACK * PASS], BF16, tag=("log_w", "w1_w4")[pair])[:]
+            grouped = sb("w1_bf_pair%d" % pair, [P, PACK * PASS], BF16, tag=("w1_raw2", "w1_w4")[pair])[:]
             for a in range(2):
                 nc.scalar.copy(
                     out=grouped.rearrange("p (u a m i) -> p a m u i", u=2, a=2, i=PACK)[:, a],
@@ -357,8 +364,9 @@ def tile_list_stemma_deviation_kernel(
                 )
             quantize_w1(grouped, PACK + 2 * pair)
 
+        scatter_by_logs(2, log_b0[:, 0:S])
+        scatter_by_logs(3, log_b0[:, S:])
         round_w1_pair(0)
-        scatter_by_logs(3, log_b3[:])
         exemplar2 = sb("exemplar2", [P, M], F32, tag="w1_w3")
         fetch_exemplar(exemplar2[:], 2, 0, M)
         w3_w = sb("w3_w", [P, 2, N], I32, tag="w1_s3")
@@ -393,7 +401,7 @@ def tile_list_stemma_deviation_kernel(
             if t == 0:
                 round_w1_pair(1)
 
-        z0_turned = sb("z0_turned", [P, BLOCKS, PASS], BF16, tag="log_w")
+        z0_turned = sb("z0_turned", [P, BLOCKS, PASS], BF16, tag="tab_w1")
         z0_bf = sb("z0_bf", [P, PACK * M], BF16, tag="w1_raw_g1")
         for pair in range(BLOCKS // 2):
             back = take_bank(2 * (pair % 2), "z_back")
@@ -464,7 +472,7 @@ def tile_list_stemma_deviation_kernel(
             y_bf = sb("y_bf%d" % chunk, [P, width * PACK], BF16, tag="bf1")
             y_bf_units = [y_bf[:, u * UNIT * PACK : (u + 1) * UNIT * PACK] for u in range(width // UNIT)]
             if first + width < M:
-                z_bf = sb("z1_bf%d" % chunk, [P, PACK * width], BF16, tag="log_w")
+                z_bf = sb("z1_bf%d" % chunk, [P, PACK * width], BF16, tag="tab_w1")
                 quantize_z(fetch_z1(first, width, 0, width), z_bf[:], 1, first, width, nc.scalar.copy)
                 y = sb("y%d" % chunk, [P, width // UNIT, PACK, UNIT], F32, tag=y_tags[chunk])
                 for u in range(width // UNIT):

@@ -21,6 +21,7 @@ P = 128
 PACK = 4
 PASS = P * PACK
 BANK = 512
+QUARTER = 256
 BLOCKS = S // P
 LINE = 4
 QUAD = 32
@@ -51,27 +52,33 @@ def tile_list_stemma_deviation_kernel(
         def entries(lst, first, count):
             return lst[:, first // LIST_ROWS : (first + count) // LIST_ROWS]
 
-        def half_cols(half):
-            return slice(half * BANK, (half + 1) * BANK)
+        def span(first, count):
+            return slice(first, first + count)
 
-        def blocks(ap):
-            return ap.rearrange("p (b j) -> p b j", j=P)
+        def half_cols(half):
+            return span(half * BANK, BANK)
 
         idx, idx2, idx3, idx4 = [keep.tile([P, S // LIST_ROWS], U16, name="list%d" % i) for i in range(4)]
+        clocks = sb("clocks", [P, 16], U32)
+
+        def clock(k, ap):
+            nc.gpsimd.tensor_copy(clocks[:, 8 * k : 8 * k + 1], ap.bitcast(U32))
 
         tab_s = sb("tab_s", [P, T], U8)
-        v_s_moved = sb("v_s_moved", [P, S], U8)
+        v_planes = sb("v_planes", [P, 2, S], U8)
         w2_s = sb("w2_s", [P, 2 * H], U8)
         w3_s_raw = sb("w3_s_raw", [P, N], U8)
-        nc.gpsimd.memset(tab_s[:].bitcast(I32), 0)
-        nc.vector.memset(w2_s[:].bitcast(I32), 0)
-        nc.vector.memset(v_s_moved[:].bitcast(I32), 0)
+        nc.gpsimd.memset(w2_s[:].bitcast(I32), 0)
+        nc.vector.memset(tab_s[QUAD : 2 * QUAD, :].bitcast(I32), 0)
+        nc.vector.memset(tab_s[2 * QUAD :, :].bitcast(I32), 0)
+        nc.vector.memset(v_planes[:].rearrange("p a j -> p (a j)").bitcast(I32), 0)
         nc.vector.memset(w3_s_raw[:].bitcast(I32), 0)
         ident = sb("ident", [P, P], F32)
         make_identity(nc, ident[:])
 
         tab_w = [sb("tab_w%d" % a, [P, T], I32) for a in range(2)]
-        w2_w = [sb("w2_w%d" % g, [P, 2, 2 * PASS], U8) for g in range(2)]
+        w2_spans = ((0, P), (P, PASS), (PASS, H))
+        w2_w = [sb("w2_w%d" % k, [P, 2, 2 * (hi - lo)], U8) for k, (lo, hi) in enumerate(w2_spans)]
         wgs_rows = sb("wgs_rows", [P, S], F32)
         w3_w_raw = sb("w3_w_raw", [P, 2, N], I32)
         pages = {}
@@ -79,32 +86,23 @@ def tile_list_stemma_deviation_kernel(
         def load_tab_words(a):
             nc.sync.dma_start(out=tab_w[a][:], in_=tab_words[a].rearrange("p t i -> p (t i)").bitcast(I32))
 
-        def load_packed_scales(queue, dst, src):
-            for q in range(4):
-                queue.dma_start(
-                    out=dst[QUAD * q : QUAD * q + 8, :].bitcast(I32), in_=src[:, 4 * q : 4 * q + 4, :].bitcast(I32)
-                )
-
-        def load_w2_scales(queue):
-            for q in range(4):
-                queue.dma_start(
-                    out=w2_s[QUAD * q : QUAD * q + 4, :].bitcast(I32).rearrange("r (a c) -> r a c", a=2),
-                    in_=w2_scales[:, 4 * q : 4 * q + 4, :].bitcast(I32).rearrange("a r c -> r a c"),
-                )
-
-        def load_w2_words(g):
+        def load_w2_words(k):
+            lo, hi = w2_spans[k]
             nc.sync.dma_start(
-                out=w2_w[g][:].bitcast(I32),
-                in_=w2_words[:, :, g * 2 * PASS : (g + 1) * 2 * PASS].bitcast(I32).rearrange("a p c -> p a c"),
+                out=w2_w[k][:].bitcast(I32),
+                in_=w2_words[:, :, 2 * lo : 2 * hi].bitcast(I32).rearrange("a p c -> p a c"),
             )
 
-        def load_w1(name, first, count):
-            raw = sb(name, [P, 2, PACK * count], F32)
+        def load_w1_pass(dst, a, first, count):
+            nc.sync.dma_start(
+                out=dst.rearrange("p (i c) -> p i c", i=PACK),
+                in_=w1[a * PASS : (a + 1) * PASS, span(first, count)].rearrange("(p i) c -> p i c", i=PACK),
+            )
+
+        def load_w1_tile(i):
+            raw = sb("w1_raw%d" % i, [P, 2, PASS], F32)
             for a in range(2):
-                nc.sync.dma_start(
-                    out=raw[:, a, :].rearrange("p (i c) -> p i c", i=PACK),
-                    in_=w1[a * PASS : (a + 1) * PASS, first : first + count].rearrange("(p i) c -> p i c", i=PACK),
-                )
+                load_w1_pass(raw[:, a, :], a, i * P, P)
             return raw
 
         def load_page(i):
@@ -115,138 +113,160 @@ def tile_list_stemma_deviation_kernel(
                 rows = page0[PASS:, :].rearrange("(p t) c -> t p c", t=PACK)[i - PACK]
             nc.sync.dma_start(out=pages[i][:], in_=rows)
 
-        load_tab_words(0)
         nc.sync.dma_start(idx[:], offs)
-        nc.sync.dma_start(idx2[:], offs2)
-        load_packed_scales(nc.sync, tab_s, tab_scales)
-        load_tab_words(1)
+        nc.sync.dma_start(out=tab_s[0:QUAD, :].bitcast(I32), in_=tab_scales.bitcast(I32).rearrange("a q t -> q a t"))
+        load_tab_words(0)
         load_w2_words(0)
-        load_w2_scales(nc.sync)
-        w1_raw0 = load_w1("w1_raw0", 0, P)
+        for q in range(4):
+            nc.sync.dma_start(
+                out=w2_s[QUAD * q : QUAD * q + 4, :].bitcast(I32).rearrange("r (a c) -> r a c", a=2),
+                in_=w2_scales[:, 4 * q : 4 * q + 4, :].bitcast(I32).rearrange("a r c -> r a c"),
+            )
+        nc.sync.dma_start(idx2[:], offs2)
+        load_tab_words(1)
         v_s = sb("v_s", [P, S], U8)
         nc.vector.tensor_copy(v_s[:], tab_s[:].indirect(idx[:]))
-        live_end = 3 * QUAD + 4
-        nc.sync.dma_start(out=v_s_moved[0:live_end, :].bitcast(I32), in_=v_s[4 : live_end + 4, :].bitcast(I32))
+        for q in range(4):
+            nc.sync.dma_start(
+                out=v_planes[QUAD * q : QUAD * q + 4].bitcast(I32), in_=v_s[8 * q : 8 * q + 8, :].bitcast(I32)
+            )
+        w1_raw0 = [sb("w1_raw0%d" % a, [P, PASS], F32) for a in range(2)]
+        for a in range(2):
+            load_w1_pass(w1_raw0[a][:], a, 0, P)
         load_page(0)
-        nc.sync.dma_start(out=wgs_rows[:], in_=wgs)
-        w1_raw12 = [load_w1("w1_raw%d" % i, i * P, P) for i in (1, 2)]
+        for cols in (span(0, QUARTER), span(QUARTER, S - QUARTER)):
+            nc.sync.dma_start(out=wgs_rows[:, cols], in_=wgs[:, cols])
+        w1_raw = {1: load_w1_tile(1)}
+        load_w2_words(1)
         nc.sync.dma_start(idx4[:], offs4)
         nc.sync.dma_start(idx3[:], offs3)
+        w1_raw[2] = load_w1_tile(2)
         load_page(1)
-        load_w2_words(1)
-        w1_raw3 = load_w1("w1_raw3", 3 * P, P)
-        nc.sync.dma_start(out=w3_w_raw[:], in_=w3_words.rearrange("a p c i -> p a (c i)").bitcast(I32))
-        load_packed_scales(nc.sync, w3_s_raw, w3_scales)
+        w1_raw[3] = load_w1_tile(3)
+        load_w2_words(2)
+        w1_raw_g1 = [sb("w1_raw_g1%d" % a, [P, PACK * PASS], F32) for a in range(2)]
+        for a in range(2):
+            load_w1_pass(w1_raw_g1[a][:], a, PASS, PASS)
         load_page(2)
-        w1_raw_g1 = load_w1("w1_raw_g1", PASS, PASS)
+        nc.sync.dma_start(out=w3_w_raw[:], in_=w3_words.rearrange("a p c i -> p a (c i)").bitcast(I32))
+        for q in range(4):
+            nc.sync.dma_start(
+                out=w3_s_raw[QUAD * q : QUAD * q + 8, :].bitcast(I32),
+                in_=w3_scales[:, 4 * q : 4 * q + 4, :].bitcast(I32),
+            )
         for i in range(3, PAGE_SLOTS):
             load_page(i)
         warm = sb("warm", [P, 1], F32)
         nc.scalar.activation(out=warm[:], in_=ident[:, 0:1], func=ACT.Abs_reciprocal_sqrt, bias=1.0)
 
-        w1_w = [sb("w1_w%d" % i, [P, 2 * P], U32) for i in range(2 * PACK)]
-        w1_s = [sb("w1_s%d" % i, [P, 2 * P], U8) for i in range(2 * PACK)]
+        w1_w, w1_s = {}, {}
         factor_ring = [sb("factor%d" % i, [P, S], F32) for i in range(RING)]
         a_ring = [sb("a%d" % i, [P, S], F32) for i in range(2)]
-
         v_half = {}
 
-        def gather_words(half, tag):
-            v_half[half] = sb("v_half%d" % half, [P, 2, BANK], U32, tag=tag)
-            for a in range(2):
-                nc.vector.tensor_copy(
-                    v_half[half][:, a, :], tab_w[a][:].bitcast(U32).indirect(entries(idx, half * BANK, BANK))
-                )
+        def gather_words(a, first, count, tag=None):
+            words = sb("v%d_%d" % (a, first), [P, count], U32, tag=tag)
+            nc.vector.tensor_copy(words[:], tab_w[a][:].bitcast(U32).indirect(entries(idx, first, count)))
+            for half in range(count // BANK):
+                v_half[a, first // BANK + half] = words[:, half_cols(half)]
 
         def v_words(a, first, count):
             half, start = divmod(first, BANK)
-            return v_half[half][:, a, start : start + count].bitcast(FP8X4)
+            return v_half[a, half][:, span(start, count)].bitcast(FP8X4)
 
-        def quantize_w1(grouped, first_tile):
-            for k in range(grouped.shape[1] // (2 * PASS)):
-                i = first_tile + k
-                nc.vector.quantize_mx(
-                    out=w1_w[i][:].bitcast(FP8X4), scales=w1_s[i][:], in_=grouped[:, k * 2 * PASS : (k + 1) * 2 * PASS]
-                )
+        def quantize_w1(name, grouped, keys):
+            words = sb(name + "_w", [P, P * len(keys)], U32)
+            scales = sb(name + "_s", [P, P * len(keys)], U8)
+            nc.vector.quantize_mx(out=words[:].bitcast(FP8X4), scales=scales[:], in_=grouped)
+            for k, key in enumerate(keys):
+                w1_w[key], w1_s[key] = words[:, span(k * P, P)], scales[:, span(k * P, P)]
 
-        def round_w1_tile(copy, grouped, raw):
+        def interleave(copy, grouped, slices):
             copy(
-                out=grouped.rearrange("p (a c l i) -> p a c i l", a=2, l=LINE, i=PACK),
-                in_=raw[:].rearrange("p a (i c l) -> p a c i l", i=PACK, l=LINE),
+                out=grouped.rearrange("p (c i t) -> p c t i", i=LINE, t=PACK),
+                in_=slices.rearrange("p t (c i) -> p c t i", i=LINE),
             )
 
-        def product_b(out, g, first, count, j_first, j_count, turned):
+        def round_w1_tile(i, grouped):
+            nc.scalar.copy(
+                out=grouped.rearrange("p (a c l i) -> p a c i l", a=2, l=LINE, i=PACK),
+                in_=w1_raw[i][:].rearrange("p a (i c l) -> p a c i l", i=PACK, l=LINE),
+            )
+            quantize_w1("w1_t%d" % i, grouped, [(i, 0), (i, 1)])
+
+        def round_w1_group1(a, grouped):
+            nc.scalar.copy(
+                out=grouped.rearrange("p (t m i) -> p m t i", t=PACK, i=PACK),
+                in_=w1_raw_g1[a][:].rearrange("p (i m t) -> p m t i", i=PACK, t=PACK),
+            )
+            quantize_w1("w1_g1%d" % a, grouped, [(PACK + t, a) for t in range(PACK)])
+
+        def product_b(out, first, count, j_first, j_count, turned):
+            k = max(k for k in range(3) if w2_spans[k][0] <= first)
+            start = first - w2_spans[k][0]
             for a in range(2):
-                w_side = w2_w[g][:, a, 2 * first : 2 * (first + count)].bitcast(FP4X4)
-                w_scale = w2_s[:, a * H + g * PASS + first : a * H + g * PASS + first + count]
+                w_side = w2_w[k][:, a, span(2 * start, 2 * count)].bitcast(FP4X4)
+                w_scale = w2_s[:, span(a * H + first, count)]
                 v_side = v_words(a, j_first, j_count)
-                v_scale = (v_s, v_s_moved)[a][:, j_first : j_first + j_count]
+                v_scale = v_planes[:, a, span(j_first, j_count)]
                 sides = (v_side, v_scale, w_side, w_scale) if turned else (w_side, w_scale, v_side, v_scale)
                 nc.tensor.matmul_mx(
                     out=out, lhsT=sides[0], lhsT_scale=sides[1], rhs=sides[2], rhs_scale=sides[3],
                     start=(a == 0), stop=(a == 1),
                 )
 
-        def product_a(i, half, k):
-            cols = half_cols(half)
-            acc = take_bank(k, "acc")
+        def product_a(i, first, count, k):
+            acc = take_bank(k, "acc")[:, 0:count]
             for a in range(2):
-                wcols = slice(a * P, (a + 1) * P)
                 nc.tensor.matmul_mx(
-                    out=acc[:],
-                    lhsT=w1_w[i][:, wcols].bitcast(FP8X4),
-                    lhsT_scale=w1_s[i][:, wcols],
-                    rhs=v_words(a, half * BANK, BANK),
-                    rhs_scale=v_s[4 * a : P, cols],
+                    out=acc,
+                    lhsT=w1_w[i, a].bitcast(FP8X4),
+                    lhsT_scale=w1_s[i, a],
+                    rhs=v_words(a, first, count),
+                    rhs_scale=v_planes[:, a, span(first, count)],
                     start=(a == 0),
                     stop=(a == 1),
                 )
             return acc
 
-        def damping(i, half, scratch):
-            b_bank = take_bank(2 * (i % 2), "b_bank")
-            product_b(b_bank[:], 0, i * P, P, half * BANK, BANK, False)
-            nc.scalar.activation(out=scratch, in_=b_bank[:], func=ACT.Abs)
-            nc.scalar.activation(out=scratch, in_=scratch, func=ACT.Abs_reciprocal_sqrt, bias=1.0)
-            nc.scalar.activation(out=factor_ring[i][:, half_cols(half)], in_=scratch, func=ACT.Square)
+        def damping(i, first, count, banks, scratch):
+            for k in range(2):
+                b_bank = take_bank(banks[k], "b_bank")[:, 0:count]
+                product_b(b_bank, i * P, P, first + k * count, count, False)
+                nc.scalar.activation(out=scratch[k], in_=b_bank, func=ACT.Abs)
+            for k in range(2):
+                nc.scalar.activation(out=scratch[k], in_=scratch[k], func=ACT.Abs_reciprocal_sqrt, bias=1.0)
+            for k in range(2):
+                nc.scalar.activation(out=factor_ring[i][:, span(first + k * count, count)], in_=scratch[k], func=ACT.Square)
 
-        def multiply_h(i, half, h):
-            acc = product_a(i, half, tile_banks(i) + min(i, 1) * half)
-            nc.vector.tensor_tensor(h, acc[:], factor_ring[i][:, half_cols(half)], ALU.mult)
-
-        def damped_a(i, half, scratch, h):
-            damping(i, half, scratch)
-            multiply_h(i, half, h)
+        def multiply_h(i, first, count, k):
+            cols = span(first, count)
+            nc.vector.tensor_tensor(a_ring[i][:, cols], product_a(i, first, count, k), factor_ring[i][:, cols], ALU.mult)
 
         def tile_banks(i):
             return (EVEN_BANK, ODD_BANK)[i % 2]
 
-        def copy_a(i, dst):
+        def copy_a(i, banks):
             for half in range(2):
-                nc.scalar.copy(out=dst[:, half_cols(half)], in_=product_a(i, half, tile_banks(i) + half)[:])
+                acc = product_a(i, half * BANK, BANK, banks + half)
+                nc.scalar.copy(out=a_ring[i % 2][:, half_cols(half)], in_=acc)
 
-        def factor_by_logs(log_b, i):
-            t = i % PACK
+        def factor_by_logs(i, log_b, neg_log_w):
             for half in range(2):
                 turned = take_bank(tile_banks(i) + half, "turned")
                 for q in range(4):
-                    jb = half * 4 + q
-                    dst = turned[:, q * P : (q + 1) * P]
-                    if i < PACK:
-                        neg = neg_log_rows[:, jb * P : (jb + 1) * P]
-                    else:
-                        neg = neg_log_w[t][:, jb * P : (jb + 1) * P]
-                    nc.tensor.matmul(
-                        dst, log_b[:, jb * P : (jb + 1) * P], ident[:], start=True, stop=False, is_transpose=True
-                    )
-                    nc.tensor.matmul(dst, neg, ident[:], start=False, stop=True, is_transpose=True)
+                    cols = span((half * 4 + q) * P, P)
+                    dst = turned[:, span(q * P, P)]
+                    nc.tensor.matmul(dst, log_b[:, cols], ident[:], start=True, stop=False, is_transpose=True)
+                    nc.tensor.matmul(dst, neg_log_w[:, cols], ident[:], start=False, stop=True, is_transpose=True)
                 nc.scalar.activation(
                     out=factor_ring[i % RING][:, half_cols(half)], in_=turned[:], func=ACT.Exp, scale=-1.0
                 )
 
-        def scatter(i, values, factors, first, count):
+        def scatter(i, factors, first, count):
+            cols = span(first, count)
             nc.vector.tensor_tensor(
-                pages[i][:].indirect(entries(idx2, first, count)), values, factors[:, first : first + count], ALU.mult
+                pages[i][:].indirect(entries(idx2, first, count)), a_ring[i % 2][:, cols], factors[:, cols], ALU.mult
             )
 
         def fetch_exemplar(dst, i, first, count):
@@ -255,154 +275,137 @@ def tile_list_stemma_deviation_kernel(
         def fetch_difference(dst, exemplar, i, first, count):
             nc.vector.tensor_tensor(dst, pages[i][:].indirect(entries(idx3, first, count)), exemplar, ALU.subtract)
 
-        def interleave(copy, grouped, slices):
-            copy(
-                out=grouped.rearrange("p (c i t) -> p c t i", i=LINE, t=PACK),
-                in_=slices.rearrange("p t (c i) -> p c t i", i=LINE),
-            )
+        def fetch_by_halves(dst, exemplar, i):
+            for half in range(2):
+                fetch_exemplar(exemplar[:, half_cols(half)], i, half * BANK, BANK)
+            for half in range(2):
+                cols = half_cols(half)
+                fetch_difference(dst[:, cols], exemplar[:, cols], i, half * BANK, BANK)
 
         z_w = [sb("z_w%d" % g, [P, M], U32) for g in range(2)]
         z_s = [sb("z_s%d" % g, [P, M], U8) for g in range(2)]
 
         def quantize_z(z, grouped, g, first, count, copy):
             interleave(copy, grouped, z.rearrange("p (t m) -> p t m", t=PACK))
-            cols = slice(first, first + count)
+            cols = span(first, count)
             nc.vector.quantize_mx(out=z_w[g][:, cols].bitcast(FP8X4), scales=z_s[g][:, cols], in_=grouped)
 
-        gather_words(0, "tab_s")
-        w1_bf0 = sb("w1_bf0", [P, 2 * PASS], BF16, tag="v_late")
-        round_w1_tile(nc.vector.tensor_copy, w1_bf0[:], w1_raw0)
-        quantize_w1(w1_bf0[:], 0)
-        gather_words(1, "v_late")
-        z0 = sb("z0", [P, PACK * M], F32)
-        z0_t = [z0[:, t * M : (t + 1) * M] for t in range(PACK)]
-        shared = sb("shared", [P, 2 * M], F32)
-        exemplars = [shared[:, 0:M], shared[:, M:]]
-        damped_a(0, 0, shared[:, M - BANK // 2 : M + BANK // 2], a_ring[0][:, 0:BANK])
-        scatter(0, a_ring[0][:, 0:BANK], wgs_rows, 0, BANK)
-        damping(1, 0, shared[:, BANK:M])
-        damped_a(0, 1, shared[:, M : M + BANK], a_ring[0][:, BANK:S])
-        scatter(0, a_ring[0][:, BANK:S], wgs_rows, BANK, BANK)
+        gather_words(0, 0, S)
+        gather_words(1, 0, BANK)
+        for a, copy in enumerate((nc.scalar.copy, nc.vector.tensor_copy)):
+            grouped = sb("w1_bf0%d" % a, [P, PASS], BF16)
+            interleave(copy, grouped[:], w1_raw0[a][:].rearrange("p (i c) -> p i c", i=PACK))
+            quantize_w1("w1_t0%d" % a, grouped[:], [(0, a)])
+        gather_words(1, BANK, BANK, "w1_raw01")
+        arena = sb("arena", [P, 2 * M], F32)
+        log_w = arena[:, 0:S]
+        z0_t = {0: arena[:, S:], 2: sb("z0_2", [P, M], F32)[:], 3: sb("z0_3", [P, M], F32)[:]}
+        for half, scratch in enumerate((sb("scratch0", [P, BANK], F32, tag="w1_raw00")[:], z0_t[2][:, 0:BANK])):
+            runs = [scratch[:, span(k * QUARTER, QUARTER)] for k in range(2)]
+            damping(0, half * BANK, QUARTER, (2 * half, 2 * half + 1), runs)
+        for q in range(2):
+            multiply_h(0, q * QUARTER, QUARTER, EVEN_BANK + q)
+        for q in range(2):
+            scatter(0, wgs_rows, q * QUARTER, QUARTER)
+            multiply_h(0, BANK + q * QUARTER, QUARTER, EVEN_BANK + q)
+        scatter(0, wgs_rows, BANK, BANK)
 
-        for i in (1, 2):
-            grouped = sb("w1_bf%d" % i, [P, 2 * PASS], BF16, tag=("bf0", "bf2")[i - 1])
-            round_w1_tile(nc.scalar.copy, grouped[:], w1_raw12[i - 1])
-            quantize_w1(grouped[:], i)
-        multiply_h(1, 0, a_ring[1][:, 0:BANK])
-        log_w = sb("log_w", [P, S], F32, tag="w1_raw0")
-        damped_a(1, 1, log_w[:, 0:BANK], a_ring[1][:, BANK:S])
-        fetch_exemplar(exemplars[0], 0, 0, M)
-        fetch_difference(z0_t[0], exemplars[0], 0, 0, M)
-        scatter(1, a_ring[1][:], wgs_rows, 0, S)
-        load_page(PAGE_SLOTS)
+        scratch1 = [z0_t[3][:, 0:BANK], arena[:, 0:BANK]]
+        w1_bf1 = sb("w1_bf1", [P, 2 * PASS], BF16)
+        round_w1_tile(1, w1_bf1[:])
+        exemplar = sb("exemplar0", [P, M], F32, tag="w1_raw1")
+        fetch_by_halves(z0_t[0], exemplar[:], 0)
+        damping(1, 0, BANK, (0, 2), scratch1)
+        b_banks = [take_bank(k, "b_bank") for k in (1, 3, EVEN_BANK, EVEN_BANK + 1)]
+        for pair, bank in enumerate(b_banks):
+            for k in range(2):
+                product_b(bank[:, span(k * 2 * P, 2 * P)], 2 * P, 2 * P, (2 * pair + k) * P, P, True)
+        factor1 = sb("factor_t1", [P, S], F32, tag="w1_bf1")
+        nc.gpsimd.tensor_tensor(factor1[:], factor_ring[1][:], wgs_rows[:], ALU.mult)
+        w1_bf2 = sb("w1_bf2", [P, 2 * PASS], BF16)
+        round_w1_tile(2, w1_bf2[:])
 
         log_b0 = sb("log_b0", [P, 2 * S], F32, tag="tab_w0")
-        for pair in range(BLOCKS // 2):
-            bank = take_bank(2 * (pair % 2), "b_bank")
-            for k in range(2):
-                product_b(bank[:, k * 2 * P : (k + 1) * 2 * P], 0, 2 * P, 2 * P, (2 * pair + k) * P, P, True)
+        for pair, bank in enumerate(b_banks):
             nc.scalar.activation(
                 out=log_b0[:].rearrange("j (t b p) -> j t b p", t=2, p=P)[:, :, 2 * pair : 2 * pair + 2, :],
                 in_=bank[:].rearrange("j (b t p) -> j t b p", t=2, p=P),
                 func=ACT.Abs,
             )
-        w1_bf3 = sb("w1_bf3", [P, 2 * PASS], BF16, tag="bf1")
-        round_w1_tile(nc.scalar.copy, w1_bf3[:], w1_raw3)
-        quantize_w1(w1_bf3[:], 3)
-        exemplar1 = sb("exemplar1", [P, M], F32, tag="w1_raw3")
-        fetch_exemplar(exemplar1[:], 1, 0, M)
-        fetch_difference(z0_t[1], exemplar1[:], 1, 0, M)
-        load_page(PAGE_SLOTS + 1)
-        nc.scalar.activation(out=log_w[:], in_=wgs_rows[:], func=ACT.Ln)
+        copy_a(1, EVEN_BANK)
+        scatter(1, factor1, 0, S)
+        load_page(PAGE_SLOTS)
+        nc.scalar.activation(out=log_w, in_=wgs_rows[:], func=ACT.Ln)
         nc.scalar.activation(out=log_b0[:], in_=log_b0[:], func=ACT.Ln, bias=1.0)
-        neg_log_w = {}
+        copy_a(2, EVEN_BANK)
         log_w_turned = []
         for half in range(2):
             bank = take_bank(2 * half + 1, "log_w_turned")
             for q in range(4):
-                jb = half * 4 + q
-                nc.tensor.transpose(bank[:, q * P : (q + 1) * P], log_w[:, jb * P : (jb + 1) * P], ident[:])
+                nc.tensor.transpose(bank[:, span(q * P, P)], log_w[:, span((half * 4 + q) * P, P)], ident[:])
             log_w_turned.append(bank)
-
-        neg_log_rows = sb("neg_log_rows", [P, S], F32, tag="w1_raw2")
+        neg_log_rows = sb("neg_log_rows", [P, S], F32)
         for half in range(2):
             nc.scalar.activation(
                 out=neg_log_rows[:, half_cols(half)], in_=log_w_turned[half][:], func=ACT.Copy, scale=-1.0
             )
-
-        def spread_log_w(t):
-            if t % 2 == 0:
-                both = sb("neg_log_w%d" % t, [P, 2 * S], F32, tag=("tab_w0", "w1_s4")[t // 2])
-                neg_log_w[t], neg_log_w[t + 1] = both[:, 0:S], both[:, S:]
-            for half in range(2):
-                rows = log_w_turned[half][:].rearrange("j (b q t) -> j t b q", t=PACK, b=4)[:, t]
-                dst = neg_log_w[t][:, half_cols(half)]
-                nc.scalar.activation(
-                    out=dst.rearrange("j (b r q) -> j b r q", r=4, q=QUAD),
-                    in_=rows.unsqueeze(2).to_broadcast([P, 4, 4, QUAD]),
-                    func=ACT.Copy,
-                    scale=-1.0,
-                )
-
-        def scatter_by_logs(i, log_b):
-            values = a_ring[i % 2][:]
-            if i == 2:
-                copy_a(i, values)
-            factor_by_logs(log_b, i)
-            if i != 2:
-                copy_a(i, values)
-            scatter(i, values, factor_ring[i % RING], 0, S)
-
-        def round_w1_pair(pair):
-            grouped = sb("w1_bf_pair%d" % pair, [P, PACK * PASS], BF16, tag=("w1_raw2", "w1_w4")[pair])[:]
-            for a in range(2):
-                nc.scalar.copy(
-                    out=grouped.rearrange("p (u a m i) -> p a m u i", u=2, a=2, i=PACK)[:, a],
-                    in_=w1_raw_g1[:, a, :].rearrange("p (i m t) -> p m t i", i=PACK, t=PACK)[
-                        :, :, 2 * pair : 2 * pair + 2, :
-                    ],
-                )
-            quantize_w1(grouped, PACK + 2 * pair)
-
-        scatter_by_logs(2, log_b0[:, 0:S])
-        scatter_by_logs(3, log_b0[:, S:])
-        round_w1_pair(0)
-        exemplar2 = sb("exemplar2", [P, M], F32, tag="w1_w3")
-        fetch_exemplar(exemplar2[:], 2, 0, M)
-        w3_w = sb("w3_w", [P, 2, N], I32, tag="w1_s3")
-        nc.vector.tensor_copy(
-            out=w3_w[:].rearrange("p a (t m) -> p a m t", t=PACK),
-            in_=w3_w_raw[:].rearrange("p a (m t) -> p a m t", t=PACK),
-        )
-        fetch_difference(z0_t[2], exemplar2[:], 2, 0, M)
+        round_w1_tile(3, log_w[:, BANK:].bitcast(BF16))
+        exemplar = sb("exemplar1", [P, M], F32, tag="w1_raw3")
+        z0_t[1] = sb("z0_1", [P, M], F32, tag="w1_raw2")[:]
+        fetch_by_halves(z0_t[1], exemplar[:], 1)
+        load_page(PAGE_SLOTS + 1)
+        for i in (2, 3):
+            factor_by_logs(i, log_b0[:, span((i - 2) * S, S)], neg_log_rows)
+        scatter(2, factor_ring[2], 0, S)
+        round_w1_group1(0, log_b0[:, 0:S].bitcast(BF16))
+        copy_a(3, ODD_BANK)
+        scatter(3, factor_ring[0], 0, S)
+        round_w1_group1(1, sb("w1_bf_g11", [P, PACK * PASS], BF16, tag="neg_log_rows")[:])
+        exemplars = sb("exemplars23", [P, 2 * M], F32, tag="w1_raw_g11")
+        for i in (2, 3):
+            fetch_exemplar(exemplars[:, span((i - 2) * M, M)], i, 0, M)
+        for i in (2, 3):
+            fetch_difference(z0_t[i], exemplars[:, span((i - 2) * M, M)], i, 0, M)
         load_page(PAGE_SLOTS + 2)
-        fetch_exemplar(exemplars[0], 3, 0, M)
-        w3_s = sb("w3_s", [P, N], U8, tag="w1_w3")
-        nc.vector.tensor_copy(
-            out=w3_s[:].rearrange("p (t m) -> p m t", t=PACK),
-            in_=w3_s_raw[:].rearrange("p (m t) -> p m t", t=PACK),
+        w3_s = sb("w3_s", [P, N], U8, tag="neg_log_rows")
+        nc.gpsimd.tensor_copy(
+            out=w3_s[:].rearrange("p (t m) -> p t m", t=PACK),
+            in_=w3_s_raw[:].rearrange("p (m t) -> p t m", t=PACK),
         )
-        fetch_difference(z0_t[3], exemplars[0], 3, 0, M)
-
 
         log_b1 = sb("log_b1", [P, PACK * S], F32, tag="b_abs")
         for jb in range(BLOCKS):
             bank = take_bank(2 * (jb % 2) if jb < BLOCKS - 2 else ODD_BANK + jb % 2, "b_bank")
-            product_b(bank[:], 1, 0, PASS, jb * P, P, True)
+            product_b(bank[:], PASS, PASS, jb * P, P, True)
             nc.scalar.activation(
-                out=log_b1[:].rearrange("j (t s) -> j t s", t=PACK)[:, :, jb * P : (jb + 1) * P],
+                out=log_b1[:].rearrange("j (t s) -> j t s", t=PACK)[:, :, span(jb * P, P)],
                 in_=bank[:].rearrange("j (p t) -> j t p", t=PACK),
                 func=ACT.Abs,
             )
         nc.scalar.activation(out=log_b1[:], in_=log_b1[:], func=ACT.Ln, bias=1.0)
+        neg_pairs = [sb("neg_log_w%d" % k, [P, 2 * S], F32, tag=("w1_t3_w", "tab_w0")[k]) for k in range(2)]
         for t in range(PACK):
-            spread_log_w(t)
-            scatter_by_logs(PACK + t, log_b1[:, t * S : (t + 1) * S])
-            if t == 0:
-                round_w1_pair(1)
+            neg_log_w = neg_pairs[t // 2][:, span((t % 2) * S, S)]
+            for half in range(2):
+                rows = log_w_turned[half][:].rearrange("j (b q t) -> j t b q", t=PACK, b=4)[:, t]
+                nc.scalar.activation(
+                    out=neg_log_w[:, half_cols(half)].rearrange("j (b r q) -> j b r q", r=4, q=QUAD),
+                    in_=rows.unsqueeze(2).to_broadcast([P, 4, 4, QUAD]),
+                    func=ACT.Copy,
+                    scale=-1.0,
+                )
+            factor_by_logs(PACK + t, log_b1[:, span(t * S, S)], neg_log_w)
+            copy_a(PACK + t, tile_banks(t))
+            scatter(PACK + t, factor_ring[(PACK + t) % RING], 0, S)
 
-        z0_turned = sb("z0_turned", [P, BLOCKS, PASS], BF16, tag="tab_w1")
-        z0_bf = sb("z0_bf", [P, PACK * M], BF16, tag="w1_raw_g1")
+        w3_w = sb("w3_w", [P, 2, N], U32, tag="w1_g11_s")
+        nc.scalar.copy(
+            out=w3_w[:].rearrange("p a (t m) -> p a m t", t=PACK),
+            in_=w3_w_raw[:].bitcast(U32).rearrange("p a (m t) -> p a m t", t=PACK),
+        )
+
+        z0_turned = sb("z0_turned", [P, BLOCKS, PASS], BF16, tag="tab_w0")
+        z0_bf = sb("z0_bf", [P, PACK * M], BF16, tag="w1_raw_g10")
         for pair in range(BLOCKS // 2):
             back = take_bank(2 * (pair % 2), "z_back")
             for k in range(2):
@@ -462,17 +465,17 @@ def tile_list_stemma_deviation_kernel(
                 out=y_bf.rearrange("p (m t) -> p m t", t=PACK), in_=acc.rearrange("p t m -> p m t"), func=ACT.Abs
             )
 
-        exemplar4 = sb("exemplar4", [P, PACK * max(CHUNKS)], F32, tag="w1_w%d" % (2 * PACK - 1))
-        z1 = sb("z1", [P, PACK * max(CHUNKS)], F32, tag="shared")
-        y_tags = ("w1_raw0", "w1_raw1")
+        exemplar4 = sb("exemplar4", [P, PACK * max(CHUNKS)], F32, tag="w1_g11_w")
+        z1 = sb("z1", [P, PACK * max(CHUNKS)], F32, tag="w1_raw_g11")
+        y_tags = ("w1_raw1", "w1_raw3")
         first = 0
         for chunk, width in enumerate(CHUNKS):
             for t in range(PACK):
                 fetch_exemplar(exemplar4[:, t * width : (t + 1) * width], PACK + t, first, width)
-            y_bf = sb("y_bf%d" % chunk, [P, width * PACK], BF16, tag="bf1")
+            y_bf = sb("y_bf%d" % chunk, [P, width * PACK], BF16, tag="w1_bf1")
             y_bf_units = [y_bf[:, u * UNIT * PACK : (u + 1) * UNIT * PACK] for u in range(width // UNIT)]
             if first + width < M:
-                z_bf = sb("z1_bf%d" % chunk, [P, PACK * width], BF16, tag="tab_w1")
+                z_bf = sb("z1_bf%d" % chunk, [P, PACK * width], BF16, tag="tab_w0")
                 quantize_z(fetch_z1(first, width, 0, width), z_bf[:], 1, first, width, nc.scalar.copy)
                 y = sb("y%d" % chunk, [P, width // UNIT, PACK, UNIT], F32, tag=y_tags[chunk])
                 for u in range(width // UNIT):
@@ -482,7 +485,7 @@ def tile_list_stemma_deviation_kernel(
                     nc.sync.dma_start(out=y_rows[:, :, column : column + UNIT], in_=y[:, u])
                     abs_rounded(y_bf_units[u], acc)
             else:
-                for u, (z_tag, y_tag, queue) in enumerate((("bf0", "b_abs", nc.sync), ("bf2", "tab_w0", nc.scalar))):
+                for u, (z_tag, y_tag, queue) in enumerate((("w1_bf00", "b_abs", nc.sync), ("w1_bf01", "tab_w1", nc.scalar))):
                     column = first + u * UNIT
                     z_bf = sb("z1_bf%d" % column, [P, PACK * UNIT], BF16, tag=z_tag)
                     quantize_z(fetch_z1(first, width, u * UNIT, UNIT), z_bf[:], 1, column, UNIT, nc.vector.tensor_copy)

@@ -105,6 +105,12 @@ def tile_list_stemma_deviation_kernel(
                 load_w1_pass(raw[:, a, :], a, i * P, P)
             return raw
 
+        def load_w1_passes(i):
+            raw = [sb("w1_raw%d%d" % (i, a), [P, PASS], F32)[:] for a in range(2)]
+            for a in range(2):
+                load_w1_pass(raw[a], a, i * P, P)
+            return raw
+
         def load_page(i):
             pages[i] = sb("page%d" % i, [P, T2], F32, tag="page", bufs=PAGE_SLOTS)
             if i < PACK:
@@ -130,19 +136,20 @@ def tile_list_stemma_deviation_kernel(
             nc.sync.dma_start(
                 out=v_planes[QUAD * q : QUAD * q + 4].bitcast(I32), in_=v_s[8 * q : 8 * q + 8, :].bitcast(I32)
             )
-        w1_raw0 = [sb("w1_raw0%d" % a, [P, PASS], F32) for a in range(2)]
-        for a in range(2):
-            load_w1_pass(w1_raw0[a][:], a, 0, P)
+        w1_raw = {0: load_w1_passes(0)}
         load_page(0)
         for cols in (span(0, QUARTER), span(QUARTER, S - QUARTER)):
             nc.sync.dma_start(out=wgs_rows[:, cols], in_=wgs[:, cols])
-        w1_raw = {1: load_w1_tile(1)}
+        h_late = sb("h_late", [P, QUARTER + PASS], F32)
+        w1_raw[1] = [h_late[:, QUARTER:], sb("w1_raw11", [P, PASS], F32)[:]]
+        for a in range(2):
+            load_w1_pass(w1_raw[1][a], a, P, P)
         load_w2_words(1)
         nc.sync.dma_start(idx4[:], offs4)
         nc.sync.dma_start(idx3[:], offs3)
         w1_raw[2] = load_w1_tile(2)
         load_page(1)
-        w1_raw[3] = load_w1_tile(3)
+        w1_raw[3] = load_w1_passes(3)
         load_w2_words(2)
         w1_raw_g1 = [sb("w1_raw_g1%d" % a, [P, PACK * PASS], F32) for a in range(2)]
         for a in range(2):
@@ -194,6 +201,14 @@ def tile_list_stemma_deviation_kernel(
             )
             quantize_w1("w1_t%d" % i, grouped, [(i, 0), (i, 1)])
 
+        rounded = {}
+
+        def round_w1_pass(copy, i, a, grouped, quantize=True):
+            interleave(copy, grouped, w1_raw[i][a].rearrange("p (i c) -> p i c", i=PACK))
+            rounded[i, a] = grouped
+            if quantize:
+                quantize_w1("w1_t%d%d" % (i, a), grouped, [(i, a)])
+
         def round_w1_group1(a, grouped):
             nc.scalar.copy(
                 out=grouped.rearrange("p (t m i) -> p m t i", t=PACK, i=PACK),
@@ -201,10 +216,10 @@ def tile_list_stemma_deviation_kernel(
             )
             quantize_w1("w1_g1%d" % a, grouped, [(PACK + t, a) for t in range(PACK)])
 
-        def product_b(out, first, count, j_first, j_count, turned):
+        def product_b(out, first, count, j_first, j_count, turned, passes=(0, 1)):
             k = max(k for k in range(3) if w2_spans[k][0] <= first)
             start = first - w2_spans[k][0]
-            for a in range(2):
+            for a in passes:
                 w_side = w2_w[k][:, a, span(2 * start, 2 * count)].bitcast(FP4X4)
                 w_scale = w2_s[:, span(a * H + first, count)]
                 v_side = v_words(a, j_first, j_count)
@@ -212,7 +227,7 @@ def tile_list_stemma_deviation_kernel(
                 sides = (v_side, v_scale, w_side, w_scale) if turned else (w_side, w_scale, v_side, v_scale)
                 nc.tensor.matmul_mx(
                     out=out, lhsT=sides[0], lhsT_scale=sides[1], rhs=sides[2], rhs_scale=sides[3],
-                    start=(a == 0), stop=(a == 1),
+                    start=(a == passes[0]), stop=(a == passes[1]),
                 )
 
         def product_a(i, first, count, k):
@@ -229,31 +244,32 @@ def tile_list_stemma_deviation_kernel(
                 )
             return acc
 
-        def damping(i, first, count, banks, scratch):
+        def damping(i, first, count, banks, scratch, passes=(0, 1)):
             for k in range(2):
                 b_bank = take_bank(banks[k], "b_bank")[:, 0:count]
-                product_b(b_bank, i * P, P, first + k * count, count, False)
+                product_b(b_bank, i * P, P, first + k * count, count, False, passes)
                 nc.scalar.activation(out=scratch[k], in_=b_bank, func=ACT.Abs)
             for k in range(2):
                 nc.scalar.activation(out=scratch[k], in_=scratch[k], func=ACT.Abs_reciprocal_sqrt, bias=1.0)
             for k in range(2):
                 nc.scalar.activation(out=factor_ring[i][:, span(first + k * count, count)], in_=scratch[k], func=ACT.Square)
 
-        def multiply_h(i, first, count, k):
-            cols = span(first, count)
-            nc.vector.tensor_tensor(a_ring[i][:, cols], product_a(i, first, count, k), factor_ring[i][:, cols], ALU.mult)
+        def multiply_h(h, first, k):
+            acc = product_a(0, first, QUARTER, k)
+            nc.vector.tensor_tensor(h, acc, factor_ring[0][:, span(first, QUARTER)], ALU.mult)
 
         def tile_banks(i):
-            return (EVEN_BANK, ODD_BANK)[i % 2]
+            first = (EVEN_BANK, ODD_BANK)[i % 2]
+            return (first, first + 1)
 
         def copy_a(i, banks):
             for half in range(2):
-                acc = product_a(i, half * BANK, BANK, banks + half)
+                acc = product_a(i, half * BANK, BANK, banks[half])
                 nc.scalar.copy(out=a_ring[i % 2][:, half_cols(half)], in_=acc)
 
         def factor_by_logs(i, log_b, neg_log_w):
             for half in range(2):
-                turned = take_bank(tile_banks(i) + half, "turned")
+                turned = take_bank(tile_banks(i)[half], "turned")
                 for q in range(4):
                     cols = span((half * 4 + q) * P, P)
                     dst = turned[:, span(q * P, P)]
@@ -263,24 +279,18 @@ def tile_list_stemma_deviation_kernel(
                     out=factor_ring[i % RING][:, half_cols(half)], in_=turned[:], func=ACT.Exp, scale=-1.0
                 )
 
-        def scatter(i, factors, first, count):
-            cols = span(first, count)
-            nc.vector.tensor_tensor(
-                pages[i][:].indirect(entries(idx2, first, count)), a_ring[i % 2][:, cols], factors[:, cols], ALU.mult
-            )
+        def scatter_part(values, first, count):
+            factors = wgs_rows[:, span(first, count)]
+            nc.vector.tensor_tensor(pages[0][:].indirect(entries(idx2, first, count)), values, factors, ALU.mult)
+
+        def scatter(i, factors):
+            nc.vector.tensor_tensor(pages[i][:].indirect(idx2[:]), a_ring[i % 2][:], factors[:], ALU.mult)
 
         def fetch_exemplar(dst, i, first, count):
             nc.vector.tensor_copy(dst, pages[i][:].indirect(entries(idx4, first, count)))
 
         def fetch_difference(dst, exemplar, i, first, count):
             nc.vector.tensor_tensor(dst, pages[i][:].indirect(entries(idx3, first, count)), exemplar, ALU.subtract)
-
-        def fetch_by_halves(dst, exemplar, i):
-            for half in range(2):
-                fetch_exemplar(exemplar[:, half_cols(half)], i, half * BANK, BANK)
-            for half in range(2):
-                cols = half_cols(half)
-                fetch_difference(dst[:, cols], exemplar[:, cols], i, half * BANK, BANK)
 
         z_w = [sb("z_w%d" % g, [P, M], U32) for g in range(2)]
         z_s = [sb("z_s%d" % g, [P, M], U8) for g in range(2)]
@@ -293,29 +303,29 @@ def tile_list_stemma_deviation_kernel(
         gather_words(0, 0, S)
         gather_words(1, 0, BANK)
         for a, copy in enumerate((nc.scalar.copy, nc.vector.tensor_copy)):
-            grouped = sb("w1_bf0%d" % a, [P, PASS], BF16)
-            interleave(copy, grouped[:], w1_raw0[a][:].rearrange("p (i c) -> p i c", i=PACK))
-            quantize_w1("w1_t0%d" % a, grouped[:], [(0, a)])
+            round_w1_pass(copy, 0, a, sb("w1_bf0%d" % a, [P, PASS], BF16)[:])
         gather_words(1, BANK, BANK, "w1_raw01")
-        arena = sb("arena", [P, 2 * M], F32)
-        log_w = arena[:, 0:S]
-        z0_t = {0: arena[:, S:], 2: sb("z0_2", [P, M], F32)[:], 3: sb("z0_3", [P, M], F32)[:]}
+        log_w = sb("log_w", [P, S], F32)[:]
+        z0_t = {2: sb("z0_2", [P, M], F32)[:], 3: sb("z0_3", [P, M], F32)[:]}
         for half, scratch in enumerate((sb("scratch0", [P, BANK], F32, tag="w1_raw00")[:], z0_t[2][:, 0:BANK])):
             runs = [scratch[:, span(k * QUARTER, QUARTER)] for k in range(2)]
-            damping(0, half * BANK, QUARTER, (2 * half, 2 * half + 1), runs)
+            damping(0, half * BANK, QUARTER, (2 * half, 2 * half + 1), runs, (half, 1 - half))
+        h_early = [a_ring[0][:, span(q * QUARTER, QUARTER)] for q in range(2)]
         for q in range(2):
-            multiply_h(0, q * QUARTER, QUARTER, EVEN_BANK + q)
-        for q in range(2):
-            scatter(0, wgs_rows, q * QUARTER, QUARTER)
-            multiply_h(0, BANK + q * QUARTER, QUARTER, EVEN_BANK + q)
-        scatter(0, wgs_rows, BANK, BANK)
+            multiply_h(h_early[q], q * QUARTER, EVEN_BANK + q)
+        scatter_part(h_early[0], 0, QUARTER)
+        multiply_h(h_late[:, 0:QUARTER], BANK, EVEN_BANK)
+        scatter_part(h_early[1], QUARTER, QUARTER)
+        round_w1_pass(nc.scalar.copy, 1, 0, sb("w1_bf10", [P, PASS], BF16)[:], quantize=False)
+        multiply_h(h_late[:, span(QUARTER, QUARTER)], BANK + QUARTER, EVEN_BANK + 1)
+        quantize_w1("w1_t10", rounded[1, 0], [(1, 0)])
+        scatter_part(h_late[:, 0:BANK], BANK, BANK)
 
-        scratch1 = [z0_t[3][:, 0:BANK], arena[:, 0:BANK]]
-        w1_bf1 = sb("w1_bf1", [P, 2 * PASS], BF16)
-        round_w1_tile(1, w1_bf1[:])
-        exemplar = sb("exemplar0", [P, M], F32, tag="w1_raw1")
-        fetch_by_halves(z0_t[0], exemplar[:], 0)
+        scratch1 = [z0_t[3][:, 0:BANK], log_w[:, 0:BANK]]
         damping(1, 0, BANK, (0, 2), scratch1)
+        round_w1_pass(nc.scalar.copy, 1, 1, sb("w1_bf1", [P, PASS], BF16)[:])
+        exemplar = sb("exemplar0", [P, M], F32, tag="w1_raw11")
+        fetch_exemplar(exemplar[:], 0, 0, M)
         b_banks = [take_bank(k, "b_bank") for k in (1, 3, EVEN_BANK, EVEN_BANK + 1)]
         for pair, bank in enumerate(b_banks):
             for k in range(2):
@@ -324,6 +334,8 @@ def tile_list_stemma_deviation_kernel(
         nc.gpsimd.tensor_tensor(factor1[:], factor_ring[1][:], wgs_rows[:], ALU.mult)
         w1_bf2 = sb("w1_bf2", [P, 2 * PASS], BF16)
         round_w1_tile(2, w1_bf2[:])
+        z0_t[0] = sb("z0_0", [P, M], F32, tag="w1_raw2")[:]
+        fetch_difference(z0_t[0], exemplar[:], 0, 0, M)
 
         log_b0 = sb("log_b0", [P, 2 * S], F32, tag="tab_w0")
         for pair, bank in enumerate(b_banks):
@@ -332,12 +344,12 @@ def tile_list_stemma_deviation_kernel(
                 in_=bank[:].rearrange("j (b t p) -> j t b p", t=2, p=P),
                 func=ACT.Abs,
             )
-        copy_a(1, EVEN_BANK)
-        scatter(1, factor1, 0, S)
+        copy_a(1, (1, 3))
+        scatter(1, factor1)
         load_page(PAGE_SLOTS)
         nc.scalar.activation(out=log_w, in_=wgs_rows[:], func=ACT.Ln)
         nc.scalar.activation(out=log_b0[:], in_=log_b0[:], func=ACT.Ln, bias=1.0)
-        copy_a(2, EVEN_BANK)
+        copy_a(2, tile_banks(2))
         log_w_turned = []
         for half in range(2):
             bank = take_bank(2 * half + 1, "log_w_turned")
@@ -349,25 +361,27 @@ def tile_list_stemma_deviation_kernel(
             nc.scalar.activation(
                 out=neg_log_rows[:, half_cols(half)], in_=log_w_turned[half][:], func=ACT.Copy, scale=-1.0
             )
-        round_w1_tile(3, log_w[:, BANK:].bitcast(BF16))
-        exemplar = sb("exemplar1", [P, M], F32, tag="w1_raw3")
-        z0_t[1] = sb("z0_1", [P, M], F32, tag="w1_raw2")[:]
-        fetch_by_halves(z0_t[1], exemplar[:], 1)
+        round_w1_pass(nc.scalar.copy, 3, 0, log_w[:, span(BANK, QUARTER)].bitcast(BF16))
+        exemplar = sb("exemplar1", [P, M], F32, tag="w1_raw30")
+        fetch_exemplar(exemplar[:], 1, 0, M)
+        round_w1_pass(nc.scalar.copy, 3, 1, log_w[:, span(BANK + QUARTER, QUARTER)].bitcast(BF16))
+        z0_t[1] = sb("z0_1", [P, M], F32, tag="w1_raw31")[:]
+        fetch_difference(z0_t[1], exemplar[:], 1, 0, M)
         load_page(PAGE_SLOTS + 1)
         for i in (2, 3):
             factor_by_logs(i, log_b0[:, span((i - 2) * S, S)], neg_log_rows)
-        scatter(2, factor_ring[2], 0, S)
+        scatter(2, factor_ring[2])
         round_w1_group1(0, log_b0[:, 0:S].bitcast(BF16))
-        copy_a(3, ODD_BANK)
-        scatter(3, factor_ring[0], 0, S)
-        round_w1_group1(1, sb("w1_bf_g11", [P, PACK * PASS], BF16, tag="neg_log_rows")[:])
+        copy_a(3, tile_banks(3))
+        scatter(3, factor_ring[0])
+        round_w1_group1(1, sb("w1_bf_g11", [P, PACK * PASS], BF16, tag="w1_t31_w")[:])
         exemplars = sb("exemplars23", [P, 2 * M], F32, tag="w1_raw_g11")
         for i in (2, 3):
             fetch_exemplar(exemplars[:, span((i - 2) * M, M)], i, 0, M)
         for i in (2, 3):
             fetch_difference(z0_t[i], exemplars[:, span((i - 2) * M, M)], i, 0, M)
         load_page(PAGE_SLOTS + 2)
-        w3_s = sb("w3_s", [P, N], U8, tag="neg_log_rows")
+        w3_s = sb("w3_s", [P, N], U8, tag="w1_t31_w")
         nc.gpsimd.tensor_copy(
             out=w3_s[:].rearrange("p (t m) -> p t m", t=PACK),
             in_=w3_s_raw[:].rearrange("p (m t) -> p t m", t=PACK),
@@ -383,7 +397,7 @@ def tile_list_stemma_deviation_kernel(
                 func=ACT.Abs,
             )
         nc.scalar.activation(out=log_b1[:], in_=log_b1[:], func=ACT.Ln, bias=1.0)
-        neg_pairs = [sb("neg_log_w%d" % k, [P, 2 * S], F32, tag=("w1_t3_w", "tab_w0")[k]) for k in range(2)]
+        neg_pairs = [sb("neg_log_w%d" % k, [P, 2 * S], F32, tag=("w1_t31_s", "tab_w0")[k]) for k in range(2)]
         for t in range(PACK):
             neg_log_w = neg_pairs[t // 2][:, span((t % 2) * S, S)]
             for half in range(2):
@@ -396,7 +410,7 @@ def tile_list_stemma_deviation_kernel(
                 )
             factor_by_logs(PACK + t, log_b1[:, span(t * S, S)], neg_log_w)
             copy_a(PACK + t, tile_banks(t))
-            scatter(PACK + t, factor_ring[(PACK + t) % RING], 0, S)
+            scatter(PACK + t, factor_ring[(PACK + t) % RING])
 
         w3_w = sb("w3_w", [P, 2, N], U32, tag="w1_g11_s")
         nc.scalar.copy(
@@ -467,7 +481,7 @@ def tile_list_stemma_deviation_kernel(
 
         exemplar4 = sb("exemplar4", [P, PACK * max(CHUNKS)], F32, tag="w1_g11_w")
         z1 = sb("z1", [P, PACK * max(CHUNKS)], F32, tag="w1_raw_g11")
-        y_tags = ("w1_raw1", "w1_raw3")
+        y_tags = ("w1_raw11", "w1_raw30")
         first = 0
         for chunk, width in enumerate(CHUNKS):
             for t in range(PACK):

@@ -140,20 +140,17 @@ def tile_list_stemma_deviation_kernel(
         load_page(0)
         for cols in (span(0, QUARTER), span(QUARTER, S - QUARTER)):
             nc.sync.dma_start(out=wgs_rows[:, cols], in_=wgs[:, cols])
-        h_late = sb("h_late", [P, QUARTER + PASS], F32)
-        w1_raw[1] = [h_late[:, QUARTER:], sb("w1_raw11", [P, PASS], F32)[:]]
-        for a in range(2):
-            load_w1_pass(w1_raw[1][a], a, P, P)
         load_w2_words(1)
+        w1_raw[1] = load_w1_tile(1)
         nc.sync.dma_start(idx4[:], offs4)
         nc.sync.dma_start(idx3[:], offs3)
         w1_raw[2] = load_w1_tile(2)
         load_page(1)
-        w1_raw[3] = load_w1_passes(3)
+        w1_raw[3] = load_w1_tile(3)
         load_w2_words(2)
-        w1_raw_g1 = [sb("w1_raw_g1%d" % a, [P, PACK * PASS], F32) for a in range(2)]
+        w1_raw_g1 = sb("w1_raw_g1", [P, 2 * PACK * PASS], F32)
         for a in range(2):
-            load_w1_pass(w1_raw_g1[a][:], a, PASS, PASS)
+            load_w1_pass(w1_raw_g1[:, span(a * PACK * PASS, PACK * PASS)], a, PASS, PASS)
         load_page(2)
         nc.sync.dma_start(out=w3_w_raw[:], in_=w3_words.rearrange("a p c i -> p a (c i)").bitcast(I32))
         for q in range(4):
@@ -201,20 +198,27 @@ def tile_list_stemma_deviation_kernel(
             )
             quantize_w1("w1_t%d" % i, grouped, [(i, 0), (i, 1)])
 
-        rounded = {}
-
-        def round_w1_pass(copy, i, a, grouped, quantize=True):
+        def round_w1_pass(copy, i, a, grouped):
             interleave(copy, grouped, w1_raw[i][a].rearrange("p (i c) -> p i c", i=PACK))
-            rounded[i, a] = grouped
-            if quantize:
-                quantize_w1("w1_t%d%d" % (i, a), grouped, [(i, a)])
+            quantize_w1("w1_t%d%d" % (i, a), grouped, [(i, a)])
 
-        def round_w1_group1(a, grouped):
+        def round_on_gpsimd(out, in_):
+            nc.gpsimd.tensor_scalar(out, in_, 1.0, 0.0, ALU.mult, ALU.add)
+
+        def fetch_both(i, both):
+            fetch_exemplar(both[:, 0:M], i, 0, M)
+            nc.vector.tensor_copy(both[:, M:], pages[i][:].indirect(idx3[:]))
+
+        def subtract(dst, both):
+            nc.gpsimd.tensor_tensor(dst, both[:, M:], both[:, 0:M], ALU.subtract)
+
+        def round_w1_pair(pair, grouped):
             nc.scalar.copy(
-                out=grouped.rearrange("p (t m i) -> p m t i", t=PACK, i=PACK),
-                in_=w1_raw_g1[a][:].rearrange("p (i m t) -> p m t i", i=PACK, t=PACK),
+                out=grouped.rearrange("p (u a m i) -> p a m u i", u=2, a=2, i=PACK),
+                in_=w1_raw_g1[:].rearrange("p (a i m t) -> p a m t i", a=2, i=PACK, t=PACK)[:, :, :, span(2 * pair, 2), :],
             )
-            quantize_w1("w1_g1%d" % a, grouped, [(PACK + t, a) for t in range(PACK)])
+            keys = [(PACK + 2 * pair + u, a) for u in range(2) for a in range(2)]
+            quantize_w1("w1_pair%d" % pair, grouped, keys)
 
         def product_b(out, first, count, j_first, j_count, turned, passes=(0, 1)):
             k = max(k for k in range(3) if w2_spans[k][0] <= first)
@@ -267,7 +271,7 @@ def tile_list_stemma_deviation_kernel(
                 acc = product_a(i, half * BANK, BANK, banks[half])
                 nc.scalar.copy(out=a_ring[i % 2][:, half_cols(half)], in_=acc)
 
-        def factor_by_logs(i, log_b, neg_log_w):
+        def factor_by_logs(i, log_b, neg_log_w, factor):
             for half in range(2):
                 turned = take_bank(tile_banks(i)[half], "turned")
                 for q in range(4):
@@ -275,9 +279,7 @@ def tile_list_stemma_deviation_kernel(
                     dst = turned[:, span(q * P, P)]
                     nc.tensor.matmul(dst, log_b[:, cols], ident[:], start=True, stop=False, is_transpose=True)
                     nc.tensor.matmul(dst, neg_log_w[:, cols], ident[:], start=False, stop=True, is_transpose=True)
-                nc.scalar.activation(
-                    out=factor_ring[i % RING][:, half_cols(half)], in_=turned[:], func=ACT.Exp, scale=-1.0
-                )
+                nc.scalar.activation(out=factor[:, half_cols(half)], in_=turned[:], func=ACT.Exp, scale=-1.0)
 
         def scatter_part(values, first, count):
             factors = wgs_rows[:, span(first, count)]
@@ -310,22 +312,19 @@ def tile_list_stemma_deviation_kernel(
         for half, scratch in enumerate((sb("scratch0", [P, BANK], F32, tag="w1_raw00")[:], z0_t[2][:, 0:BANK])):
             runs = [scratch[:, span(k * QUARTER, QUARTER)] for k in range(2)]
             damping(0, half * BANK, QUARTER, (2 * half, 2 * half + 1), runs, (half, 1 - half))
-        h_early = [a_ring[0][:, span(q * QUARTER, QUARTER)] for q in range(2)]
+        h = [a_ring[0][:, span(q * QUARTER, QUARTER)] for q in range(4)]
         for q in range(2):
-            multiply_h(h_early[q], q * QUARTER, EVEN_BANK + q)
-        scatter_part(h_early[0], 0, QUARTER)
-        multiply_h(h_late[:, 0:QUARTER], BANK, EVEN_BANK)
-        scatter_part(h_early[1], QUARTER, QUARTER)
-        round_w1_pass(nc.scalar.copy, 1, 0, sb("w1_bf10", [P, PASS], BF16)[:], quantize=False)
-        multiply_h(h_late[:, span(QUARTER, QUARTER)], BANK + QUARTER, EVEN_BANK + 1)
-        quantize_w1("w1_t10", rounded[1, 0], [(1, 0)])
-        scatter_part(h_late[:, 0:BANK], BANK, BANK)
+            multiply_h(h[q], q * QUARTER, EVEN_BANK + q)
+        for q in range(2):
+            scatter_part(h[q], q * QUARTER, QUARTER)
+            multiply_h(h[2 + q], BANK + q * QUARTER, EVEN_BANK + q)
+        scatter_part(a_ring[0][:, BANK:], BANK, BANK)
 
-        scratch1 = [z0_t[3][:, 0:BANK], log_w[:, 0:BANK]]
-        damping(1, 0, BANK, (0, 2), scratch1)
-        round_w1_pass(nc.scalar.copy, 1, 1, sb("w1_bf1", [P, PASS], BF16)[:])
-        exemplar = sb("exemplar0", [P, M], F32, tag="w1_raw11")
-        fetch_exemplar(exemplar[:], 0, 0, M)
+        w1_bf1 = sb("w1_bf1", [P, 2 * PASS], BF16)
+        round_w1_tile(1, w1_bf1[:])
+        both0 = sb("both0", [P, 2 * M], F32, tag="w1_raw1")
+        fetch_both(0, both0)
+        damping(1, 0, BANK, (0, 2), [z0_t[3][:, 0:BANK], log_w[:, 0:BANK]])
         b_banks = [take_bank(k, "b_bank") for k in (1, 3, EVEN_BANK, EVEN_BANK + 1)]
         for pair, bank in enumerate(b_banks):
             for k in range(2):
@@ -334,8 +333,6 @@ def tile_list_stemma_deviation_kernel(
         nc.gpsimd.tensor_tensor(factor1[:], factor_ring[1][:], wgs_rows[:], ALU.mult)
         w1_bf2 = sb("w1_bf2", [P, 2 * PASS], BF16)
         round_w1_tile(2, w1_bf2[:])
-        z0_t[0] = sb("z0_0", [P, M], F32, tag="w1_raw2")[:]
-        fetch_difference(z0_t[0], exemplar[:], 0, 0, M)
 
         log_b0 = sb("log_b0", [P, 2 * S], F32, tag="tab_w0")
         for pair, bank in enumerate(b_banks):
@@ -347,45 +344,39 @@ def tile_list_stemma_deviation_kernel(
         copy_a(1, (1, 3))
         scatter(1, factor1)
         load_page(PAGE_SLOTS)
+        both1 = sb("both1", [P, 2 * M], F32, tag="tab_w1")
+        fetch_both(1, both1)
+        load_page(PAGE_SLOTS + 1)
+        w1_bf3 = sb("w1_bf3", [P, 2, PASS], BF16, tag="w1_bf1")
+        for a in range(2):
+            interleave(round_on_gpsimd, w1_bf3[:, a, :], w1_raw[3][:, a, :].rearrange("p (i c) -> p i c", i=PACK))
+        quantize_w1("w1_t3", w1_bf3[:].rearrange("p a c -> p (a c)"), [(3, 0), (3, 1)])
+        z0_t[0] = sb("z0_0", [P, M], F32, tag="w1_raw3")[:]
+        subtract(z0_t[0], both0)
+
         nc.scalar.activation(out=log_w, in_=wgs_rows[:], func=ACT.Ln)
-        nc.scalar.activation(out=log_b0[:], in_=log_b0[:], func=ACT.Ln, bias=1.0)
-        copy_a(2, tile_banks(2))
         log_w_turned = []
         for half in range(2):
             bank = take_bank(2 * half + 1, "log_w_turned")
             for q in range(4):
                 nc.tensor.transpose(bank[:, span(q * P, P)], log_w[:, span((half * 4 + q) * P, P)], ident[:])
             log_w_turned.append(bank)
+        log_b = {i: log_b0[:, span((i - 2) * S, S)] for i in (2, 3)}
+        nc.scalar.activation(out=log_b[2], in_=log_b[2], func=ACT.Ln, bias=1.0)
+        copy_a(2, tile_banks(2))
         neg_log_rows = sb("neg_log_rows", [P, S], F32)
         for half in range(2):
             nc.scalar.activation(
                 out=neg_log_rows[:, half_cols(half)], in_=log_w_turned[half][:], func=ACT.Copy, scale=-1.0
             )
-        round_w1_pass(nc.scalar.copy, 3, 0, log_w[:, span(BANK, QUARTER)].bitcast(BF16))
-        exemplar = sb("exemplar1", [P, M], F32, tag="w1_raw30")
-        fetch_exemplar(exemplar[:], 1, 0, M)
-        round_w1_pass(nc.scalar.copy, 3, 1, log_w[:, span(BANK + QUARTER, QUARTER)].bitcast(BF16))
-        z0_t[1] = sb("z0_1", [P, M], F32, tag="w1_raw31")[:]
-        fetch_difference(z0_t[1], exemplar[:], 1, 0, M)
-        load_page(PAGE_SLOTS + 1)
-        for i in (2, 3):
-            factor_by_logs(i, log_b0[:, span((i - 2) * S, S)], neg_log_rows)
+        nc.scalar.activation(out=log_b[3], in_=log_b[3], func=ACT.Ln, bias=1.0)
+        factor3 = sb("factor3", [P, S], F32)
+        factor_by_logs(2, log_b[2], neg_log_rows, factor_ring[2])
+        factor_by_logs(3, log_b[3], neg_log_rows, factor3)
         scatter(2, factor_ring[2])
-        round_w1_group1(0, log_b0[:, 0:S].bitcast(BF16))
+        round_w1_pair(0, log_b[2].bitcast(BF16))
         copy_a(3, tile_banks(3))
-        scatter(3, factor_ring[0])
-        round_w1_group1(1, sb("w1_bf_g11", [P, PACK * PASS], BF16, tag="w1_t31_w")[:])
-        exemplars = sb("exemplars23", [P, 2 * M], F32, tag="w1_raw_g11")
-        for i in (2, 3):
-            fetch_exemplar(exemplars[:, span((i - 2) * M, M)], i, 0, M)
-        for i in (2, 3):
-            fetch_difference(z0_t[i], exemplars[:, span((i - 2) * M, M)], i, 0, M)
-        load_page(PAGE_SLOTS + 2)
-        w3_s = sb("w3_s", [P, N], U8, tag="w1_t31_w")
-        nc.gpsimd.tensor_copy(
-            out=w3_s[:].rearrange("p (t m) -> p t m", t=PACK),
-            in_=w3_s_raw[:].rearrange("p (m t) -> p t m", t=PACK),
-        )
+        scatter(3, factor3)
 
         log_b1 = sb("log_b1", [P, PACK * S], F32, tag="b_abs")
         for jb in range(BLOCKS):
@@ -396,30 +387,54 @@ def tile_list_stemma_deviation_kernel(
                 in_=bank[:].rearrange("j (p t) -> j t p", t=PACK),
                 func=ACT.Abs,
             )
-        nc.scalar.activation(out=log_b1[:], in_=log_b1[:], func=ACT.Ln, bias=1.0)
-        neg_pairs = [sb("neg_log_w%d" % k, [P, 2 * S], F32, tag=("w1_t31_s", "tab_w0")[k]) for k in range(2)]
-        for t in range(PACK):
-            neg_log_w = neg_pairs[t // 2][:, span((t % 2) * S, S)]
+        slices = [log_b1[:, span(t * S, S)] for t in range(PACK)]
+        early_logs = sb("early_logs", [P, 2 * S], F32)
+        logs = [early_logs[:, 0:S], early_logs[:, S:], slices[2], slices[3]]
+        neg_log_w = [sb("neg_log_w", [P, S], F32, tag="w1_t3_s")[:], logs[0], logs[1], logs[2]]
+
+        def spread_log_w(t):
             for half in range(2):
                 rows = log_w_turned[half][:].rearrange("j (b q t) -> j t b q", t=PACK, b=4)[:, t]
                 nc.scalar.activation(
-                    out=neg_log_w[:, half_cols(half)].rearrange("j (b r q) -> j b r q", r=4, q=QUAD),
+                    out=neg_log_w[t][:, half_cols(half)].rearrange("j (b r q) -> j b r q", r=4, q=QUAD),
                     in_=rows.unsqueeze(2).to_broadcast([P, 4, 4, QUAD]),
                     func=ACT.Copy,
                     scale=-1.0,
                 )
-            factor_by_logs(PACK + t, log_b1[:, span(t * S, S)], neg_log_w)
-            copy_a(PACK + t, tile_banks(t))
-            scatter(PACK + t, factor_ring[(PACK + t) % RING])
 
-        w3_w = sb("w3_w", [P, 2, N], U32, tag="w1_g11_s")
+        spread_log_w(0)
+        nc.scalar.activation(out=early_logs[:], in_=log_b1[:, 0 : 2 * S], func=ACT.Ln, bias=1.0)
+        nc.scalar.activation(out=log_b1[:, 2 * S :], in_=log_b1[:, 2 * S :], func=ACT.Ln, bias=1.0)
+        for i in (2, 3):
+            fetch_exemplar(slices[i - 2], i, 0, M)
+        for i in (2, 3):
+            fetch_difference(z0_t[i], slices[i - 2], i, 0, M)
+        load_page(PAGE_SLOTS + 2)
+        z0_t[1] = sb("z0_1", [P, M], F32, tag="factor3")[:]
+        subtract(z0_t[1], both1)
+        w3_s = sb("w3_s", [P, N], U8, tag="tab_w1")
+        nc.gpsimd.tensor_copy(
+            out=w3_s[:].rearrange("p (t m) -> p t m", t=PACK),
+            in_=w3_s_raw[:].rearrange("p (m t) -> p t m", t=PACK),
+        )
+        for t in range(PACK):
+            if t > 0:
+                spread_log_w(t)
+            factor = factor_ring[(PACK + t) % RING]
+            factor_by_logs(PACK + t, logs[t], neg_log_w[t], factor)
+            copy_a(PACK + t, tile_banks(t))
+            scatter(PACK + t, factor)
+            if t == 0:
+                round_w1_pair(1, sb("w1_bf_pair1", [P, PACK * PASS], BF16, tag="w1_t3_s")[:])
+
+        w3_w = sb("w3_w", [P, 2, N], U32, tag="w1_pair1_s")
         nc.scalar.copy(
             out=w3_w[:].rearrange("p a (t m) -> p a m t", t=PACK),
             in_=w3_w_raw[:].bitcast(U32).rearrange("p a (m t) -> p a m t", t=PACK),
         )
 
-        z0_turned = sb("z0_turned", [P, BLOCKS, PASS], BF16, tag="tab_w0")
-        z0_bf = sb("z0_bf", [P, PACK * M], BF16, tag="w1_raw_g10")
+        z0_turned = sb("z0_turned", [P, BLOCKS, PASS], BF16, tag="b_abs")
+        z0_bf = sb("z0_bf", [P, PACK * M], BF16, tag="w1_raw_g1")
         for pair in range(BLOCKS // 2):
             back = take_bank(2 * (pair % 2), "z_back")
             for k in range(2):
@@ -479,9 +494,9 @@ def tile_list_stemma_deviation_kernel(
                 out=y_bf.rearrange("p (m t) -> p m t", t=PACK), in_=acc.rearrange("p t m -> p m t"), func=ACT.Abs
             )
 
-        exemplar4 = sb("exemplar4", [P, PACK * max(CHUNKS)], F32, tag="w1_g11_w")
-        z1 = sb("z1", [P, PACK * max(CHUNKS)], F32, tag="w1_raw_g11")
-        y_tags = ("w1_raw11", "w1_raw30")
+        exemplar4 = sb("exemplar4", [P, PACK * max(CHUNKS)], F32, tag="w1_pair1_w")
+        z1 = sb("z1", [P, PACK * max(CHUNKS)], F32, tag="early_logs")
+        y_tags = ("w1_raw1", "w1_raw2")
         first = 0
         for chunk, width in enumerate(CHUNKS):
             for t in range(PACK):
@@ -489,7 +504,7 @@ def tile_list_stemma_deviation_kernel(
             y_bf = sb("y_bf%d" % chunk, [P, width * PACK], BF16, tag="w1_bf1")
             y_bf_units = [y_bf[:, u * UNIT * PACK : (u + 1) * UNIT * PACK] for u in range(width // UNIT)]
             if first + width < M:
-                z_bf = sb("z1_bf%d" % chunk, [P, PACK * width], BF16, tag="tab_w0")
+                z_bf = sb("z1_bf%d" % chunk, [P, PACK * width], BF16, tag="b_abs")
                 quantize_z(fetch_z1(first, width, 0, width), z_bf[:], 1, first, width, nc.scalar.copy)
                 y = sb("y%d" % chunk, [P, width // UNIT, PACK, UNIT], F32, tag=y_tags[chunk])
                 for u in range(width // UNIT):
@@ -499,7 +514,7 @@ def tile_list_stemma_deviation_kernel(
                     nc.sync.dma_start(out=y_rows[:, :, column : column + UNIT], in_=y[:, u])
                     abs_rounded(y_bf_units[u], acc)
             else:
-                for u, (z_tag, y_tag, queue) in enumerate((("w1_bf00", "b_abs", nc.sync), ("w1_bf01", "tab_w1", nc.scalar))):
+                for u, (z_tag, y_tag, queue) in enumerate((("w1_bf00", "tab_w0", nc.sync), ("w1_bf01", "log_w", nc.scalar))):
                     column = first + u * UNIT
                     z_bf = sb("z1_bf%d" % column, [P, PACK * UNIT], BF16, tag=z_tag)
                     quantize_z(fetch_z1(first, width, u * UNIT, UNIT), z_bf[:], 1, column, UNIT, nc.vector.tensor_copy)

@@ -202,15 +202,12 @@ def tile_list_stemma_deviation_kernel(
             interleave(copy, grouped, w1_raw[i][a].rearrange("p (i c) -> p i c", i=PACK))
             quantize_w1("w1_t%d%d" % (i, a), grouped, [(i, a)])
 
-        def round_on_gpsimd(out, in_):
-            nc.gpsimd.tensor_scalar(out, in_, 1.0, 0.0, ALU.mult, ALU.add)
-
-        def fetch_both(i, both):
-            fetch_exemplar(both[:, 0:M], i, 0, M)
-            nc.vector.tensor_copy(both[:, M:], pages[i][:].indirect(idx3[:]))
-
-        def subtract(dst, both):
-            nc.gpsimd.tensor_tensor(dst, both[:, M:], both[:, 0:M], ALU.subtract)
+        def fetch_by_halves(dst, exemplar, i):
+            for half in range(2):
+                fetch_exemplar(exemplar[:, half_cols(half)], i, half * BANK, BANK)
+            for half in range(2):
+                cols = half_cols(half)
+                fetch_difference(dst[:, cols], exemplar[:, cols], i, half * BANK, BANK)
 
         def round_w1_pair(pair, grouped):
             nc.scalar.copy(
@@ -322,8 +319,8 @@ def tile_list_stemma_deviation_kernel(
 
         w1_bf1 = sb("w1_bf1", [P, 2 * PASS], BF16)
         round_w1_tile(1, w1_bf1[:])
-        both0 = sb("both0", [P, 2 * M], F32, tag="w1_raw1")
-        fetch_both(0, both0)
+        z0_t[0] = sb("z0_0", [P, M], F32)[:]
+        fetch_by_halves(z0_t[0], sb("exemplar0", [P, M], F32, tag="w1_raw1")[:], 0)
         damping(1, 0, BANK, (0, 2), [z0_t[3][:, 0:BANK], log_w[:, 0:BANK]])
         b_banks = [take_bank(k, "b_bank") for k in (1, 3, EVEN_BANK, EVEN_BANK + 1)]
         for pair, bank in enumerate(b_banks):
@@ -344,15 +341,10 @@ def tile_list_stemma_deviation_kernel(
         copy_a(1, (1, 3))
         scatter(1, factor1)
         load_page(PAGE_SLOTS)
-        both1 = sb("both1", [P, 2 * M], F32, tag="tab_w1")
-        fetch_both(1, both1)
+        round_w1_tile(3, sb("w1_bf3", [P, 2 * PASS], BF16, tag="w1_t1_w")[:])
+        z0_t[1] = sb("z0_1", [P, M], F32)[:]
+        fetch_by_halves(z0_t[1], sb("exemplar1", [P, M], F32, tag="w1_raw3")[:], 1)
         load_page(PAGE_SLOTS + 1)
-        w1_bf3 = sb("w1_bf3", [P, 2, PASS], BF16, tag="w1_bf1")
-        for a in range(2):
-            interleave(round_on_gpsimd, w1_bf3[:, a, :], w1_raw[3][:, a, :].rearrange("p (i c) -> p i c", i=PACK))
-        quantize_w1("w1_t3", w1_bf3[:].rearrange("p a c -> p (a c)"), [(3, 0), (3, 1)])
-        z0_t[0] = sb("z0_0", [P, M], F32, tag="w1_raw3")[:]
-        subtract(z0_t[0], both0)
 
         nc.scalar.activation(out=log_w, in_=wgs_rows[:], func=ACT.Ln)
         log_w_turned = []
@@ -410,9 +402,7 @@ def tile_list_stemma_deviation_kernel(
         for i in (2, 3):
             fetch_difference(z0_t[i], slices[i - 2], i, 0, M)
         load_page(PAGE_SLOTS + 2)
-        z0_t[1] = sb("z0_1", [P, M], F32, tag="factor3")[:]
-        subtract(z0_t[1], both1)
-        w3_s = sb("w3_s", [P, N], U8, tag="tab_w1")
+        w3_s = sb("w3_s", [P, N], U8, tag="factor3")
         nc.gpsimd.tensor_copy(
             out=w3_s[:].rearrange("p (t m) -> p t m", t=PACK),
             in_=w3_s_raw[:].rearrange("p (m t) -> p t m", t=PACK),
@@ -480,7 +470,7 @@ def tile_list_stemma_deviation_kernel(
             return acc
 
         def fetch_z1(first, width, start, count):
-            z = z1[:, PACK * start : PACK * (start + count)]
+            z = z1[:, span(PACK * start + (2 * UNIT if count > UNIT else 0), PACK * count)]
             for t in range(PACK):
                 exemplar = exemplar4[:, t * width + start : t * width + start + count]
                 fetch_difference(z[:, t * count : (t + 1) * count], exemplar, PACK + t, first + start, count)
@@ -495,13 +485,13 @@ def tile_list_stemma_deviation_kernel(
             )
 
         exemplar4 = sb("exemplar4", [P, PACK * max(CHUNKS)], F32, tag="w1_pair1_w")
-        z1 = sb("z1", [P, PACK * max(CHUNKS)], F32, tag="early_logs")
+        z1 = sb("z1", [P, PACK * max(CHUNKS) + 2 * UNIT], F32, tag="early_logs")
         y_tags = ("w1_raw1", "w1_raw2")
         first = 0
         for chunk, width in enumerate(CHUNKS):
             for t in range(PACK):
                 fetch_exemplar(exemplar4[:, t * width : (t + 1) * width], PACK + t, first, width)
-            y_bf = sb("y_bf%d" % chunk, [P, width * PACK], BF16, tag="w1_bf1")
+            y_bf = sb("y_bf%d" % chunk, [P, width * PACK], BF16, tag="w1_raw3")
             y_bf_units = [y_bf[:, u * UNIT * PACK : (u + 1) * UNIT * PACK] for u in range(width // UNIT)]
             if first + width < M:
                 z_bf = sb("z1_bf%d" % chunk, [P, PACK * width], BF16, tag="b_abs")
@@ -512,7 +502,10 @@ def tile_list_stemma_deviation_kernel(
                     abs_float(y[:, u], acc)
                     column = first + u * UNIT
                     nc.sync.dma_start(out=y_rows[:, :, column : column + UNIT], in_=y[:, u])
-                    abs_rounded(y_bf_units[u], acc)
+                    if column < M - 3 * UNIT:
+                        abs_rounded(y_bf_units[u], acc)
+                    else:
+                        interleave(nc.vector.tensor_copy, y_bf_units[u], y[:, u])
             else:
                 for u, (z_tag, y_tag, queue) in enumerate((("w1_bf00", "tab_w0", nc.sync), ("w1_bf01", "log_w", nc.scalar))):
                     column = first + u * UNIT

@@ -29,6 +29,7 @@ LIST_ROWS = 16
 PAGE_SLOTS = 5
 RING = 3
 CHUNKS = (384, 384, 256)
+PLANE_ENDS = (384, 640, 1024)
 UNIT = 128
 EVEN_BANK = 4
 ODD_BANK = 6
@@ -217,10 +218,10 @@ def tile_list_stemma_deviation_kernel(
             keys = [(PACK + 2 * pair + u, a) for u in range(2) for a in range(2)]
             quantize_w1("w1_pair%d" % pair, grouped, keys)
 
-        def product_b(out, first, count, j_first, j_count, turned, passes=(0, 1)):
+        def product_b(out, first, count, j_first, j_count, turned):
             k = max(k for k in range(3) if w2_spans[k][0] <= first)
             start = first - w2_spans[k][0]
-            for a in passes:
+            for a in range(2):
                 w_side = w2_w[k][:, a, span(2 * start, 2 * count)].bitcast(FP4X4)
                 w_scale = w2_s[:, span(a * H + first, count)]
                 v_side = v_words(a, j_first, j_count)
@@ -228,7 +229,7 @@ def tile_list_stemma_deviation_kernel(
                 sides = (v_side, v_scale, w_side, w_scale) if turned else (w_side, w_scale, v_side, v_scale)
                 nc.tensor.matmul_mx(
                     out=out, lhsT=sides[0], lhsT_scale=sides[1], rhs=sides[2], rhs_scale=sides[3],
-                    start=(a == passes[0]), stop=(a == passes[1]),
+                    start=(a == 0), stop=(a == 1),
                 )
 
         def product_a(i, first, count, k):
@@ -245,10 +246,10 @@ def tile_list_stemma_deviation_kernel(
                 )
             return acc
 
-        def damping(i, first, count, banks, scratch, passes=(0, 1)):
+        def damping(i, first, count, banks, scratch):
             for k in range(2):
                 b_bank = take_bank(banks[k], "b_bank")[:, 0:count]
-                product_b(b_bank, i * P, P, first + k * count, count, False, passes)
+                product_b(b_bank, i * P, P, first + k * count, count, False)
                 nc.scalar.activation(out=scratch[k], in_=b_bank, func=ACT.Abs)
             for k in range(2):
                 nc.scalar.activation(out=scratch[k], in_=scratch[k], func=ACT.Abs_reciprocal_sqrt, bias=1.0)
@@ -308,7 +309,7 @@ def tile_list_stemma_deviation_kernel(
         z0_t = {2: sb("z0_2", [P, M], F32)[:], 3: sb("z0_3", [P, M], F32)[:]}
         for half, scratch in enumerate((sb("scratch0", [P, BANK], F32, tag="w1_raw00")[:], z0_t[2][:, 0:BANK])):
             runs = [scratch[:, span(k * QUARTER, QUARTER)] for k in range(2)]
-            damping(0, half * BANK, QUARTER, (2 * half, 2 * half + 1), runs, (half, 1 - half))
+            damping(0, half * BANK, QUARTER, (2 * half, 2 * half + 1), runs)
         h = [a_ring[0][:, span(q * QUARTER, QUARTER)] for q in range(4)]
         for q in range(2):
             multiply_h(h[q], q * QUARTER, EVEN_BANK + q)
@@ -487,12 +488,21 @@ def tile_list_stemma_deviation_kernel(
         exemplar4 = sb("exemplar4", [P, PACK * max(CHUNKS)], F32, tag="w1_pair1_w")
         z1 = sb("z1", [P, PACK * max(CHUNKS) + 2 * UNIT], F32, tag="early_logs")
         y_tags = ("w1_raw1", "w1_raw2")
+        y_bf = sb("y_bf", [P, PACK * M], BF16, tag="tab_w1")
+
+        def store_planes(end):
+            first = ([0] + list(PLANE_ENDS))[PLANE_ENDS.index(end)]
+            cols = slice(first, end)
+            nc.vector.quantize_mx(
+                out=y_w[:, cols].bitcast(FP8X4), scales=y_s[:, cols], in_=y_bf[:, first * PACK : end * PACK]
+            )
+            nc.sync.dma_start(out=y_words[:, cols], in_=y_w[:, cols].bitcast(I32))
+
         first = 0
         for chunk, width in enumerate(CHUNKS):
             for t in range(PACK):
                 fetch_exemplar(exemplar4[:, t * width : (t + 1) * width], PACK + t, first, width)
-            y_bf = sb("y_bf%d" % chunk, [P, width * PACK], BF16, tag="w1_raw3")
-            y_bf_units = [y_bf[:, u * UNIT * PACK : (u + 1) * UNIT * PACK] for u in range(width // UNIT)]
+            y_bf_units = [y_bf[:, span((first + u * UNIT) * PACK, UNIT * PACK)] for u in range(width // UNIT)]
             if first + width < M:
                 z_bf = sb("z1_bf%d" % chunk, [P, PACK * width], BF16, tag="b_abs")
                 quantize_z(fetch_z1(first, width, 0, width), z_bf[:], 1, first, width, nc.scalar.copy)
@@ -506,6 +516,8 @@ def tile_list_stemma_deviation_kernel(
                         abs_rounded(y_bf_units[u], acc)
                     else:
                         interleave(nc.vector.tensor_copy, y_bf_units[u], y[:, u])
+                    if column + UNIT in PLANE_ENDS:
+                        store_planes(column + UNIT)
             else:
                 for u, (z_tag, y_tag, queue) in enumerate((("w1_bf00", "tab_w0", nc.sync), ("w1_bf01", "log_w", nc.scalar))):
                     column = first + u * UNIT
@@ -516,10 +528,8 @@ def tile_list_stemma_deviation_kernel(
                     abs_float(y[:], acc)
                     interleave(nc.vector.tensor_copy, y_bf_units[u], y[:])
                     queue.dma_start(out=y_rows[:, :, column : column + UNIT], in_=y[:])
-            cols = slice(first, first + width)
-            nc.vector.quantize_mx(out=y_w[:, cols].bitcast(FP8X4), scales=y_s[:, cols], in_=y_bf[:])
-            nc.sync.dma_start(out=y_words[:, cols], in_=y_w[:, cols].bitcast(I32))
             first = first + width
+        store_planes(M)
         for q in range(4):
             (nc.sync, nc.scalar)[q % 2].dma_start(
                 out=out_2[0, 4 * q : 4 * q + 4, :].bitcast(I32), in_=y_s[QUAD * q : QUAD * q + 4, :].bitcast(I32)

@@ -367,9 +367,12 @@ def tile_list_stemma_deviation_kernel(
         factor_by_logs(2, log_b[2], neg_log_rows, factor_ring[2])
         factor_by_logs(3, log_b[3], neg_log_rows, factor3)
         scatter(2, factor_ring[2])
+        fetch_by_halves(z0_t[2], sb("exemplar2", [P, M], F32, tag="w1_raw3")[:], 2)
+        load_page(PAGE_SLOTS + 2)
         round_w1_pair(0, log_b[2].bitcast(BF16))
         copy_a(3, tile_banks(3))
         scatter(3, factor3)
+        fetch_by_halves(z0_t[3], sb("exemplar3", [P, M], F32, tag="w1_raw3")[:], 3)
 
         log_b1 = sb("log_b1", [P, PACK * S], F32, tag="b_abs")
         for jb in range(BLOCKS):
@@ -380,9 +383,7 @@ def tile_list_stemma_deviation_kernel(
                 in_=bank[:].rearrange("j (p t) -> j t p", t=PACK),
                 func=ACT.Abs,
             )
-        slices = [log_b1[:, span(t * S, S)] for t in range(PACK)]
-        early_logs = sb("early_logs", [P, 2 * S], F32)
-        logs = [early_logs[:, 0:S], early_logs[:, S:], slices[2], slices[3]]
+        logs = [log_b1[:, span(t * S, S)] for t in range(PACK)]
         neg_log_w = [sb("neg_log_w", [P, S], F32, tag="w1_t3_s")[:], logs[0], logs[1], logs[2]]
 
         def spread_log_w(t):
@@ -396,13 +397,8 @@ def tile_list_stemma_deviation_kernel(
                 )
 
         spread_log_w(0)
-        nc.scalar.activation(out=early_logs[:], in_=log_b1[:, 0 : 2 * S], func=ACT.Ln, bias=1.0)
-        nc.scalar.activation(out=log_b1[:, 2 * S :], in_=log_b1[:, 2 * S :], func=ACT.Ln, bias=1.0)
-        for i in (2, 3):
-            fetch_exemplar(slices[i - 2], i, 0, M)
-        for i in (2, 3):
-            fetch_difference(z0_t[i], slices[i - 2], i, 0, M)
-        load_page(PAGE_SLOTS + 2)
+        for t in range(PACK):
+            nc.scalar.activation(out=logs[t], in_=logs[t], func=ACT.Ln, bias=1.0)
         w3_s = sb("w3_s", [P, N], U8, tag="factor3")
         nc.gpsimd.tensor_copy(
             out=w3_s[:].rearrange("p (t m) -> p t m", t=PACK),
@@ -486,7 +482,7 @@ def tile_list_stemma_deviation_kernel(
             )
 
         exemplar4 = sb("exemplar4", [P, PACK * max(CHUNKS)], F32, tag="w1_pair1_w")
-        z1 = sb("z1", [P, PACK * max(CHUNKS) + 2 * UNIT], F32, tag="early_logs")
+        z1 = sb("z1", [P, PACK * max(CHUNKS) + 2 * UNIT], F32, tag="tab_w0")
         y_tags = ("w1_raw1", "w1_raw2")
         y_bf = sb("y_bf", [P, PACK * M], BF16, tag="tab_w1")
 
@@ -519,7 +515,7 @@ def tile_list_stemma_deviation_kernel(
                     if column + UNIT in PLANE_ENDS:
                         store_planes(column + UNIT)
             else:
-                for u, (z_tag, y_tag, queue) in enumerate((("w1_bf00", "tab_w0", nc.sync), ("w1_bf01", "log_w", nc.scalar))):
+                for u, (z_tag, y_tag, queue) in enumerate((("w1_bf00", "neg_log_rows", nc.sync), ("w1_bf01", "log_w", nc.scalar))):
                     column = first + u * UNIT
                     z_bf = sb("z1_bf%d" % column, [P, PACK * UNIT], BF16, tag=z_tag)
                     quantize_z(fetch_z1(first, width, u * UNIT, UNIT), z_bf[:], 1, column, UNIT, nc.vector.tensor_copy)

@@ -269,9 +269,9 @@ def tile_list_stemma_deviation_kernel(
                 acc = product_a(i, half * BANK, BANK, banks[half])
                 nc.scalar.copy(out=a_ring[i % 2][:, half_cols(half)], in_=acc)
 
-        def factor_by_logs(i, log_b, neg_log_w, factor):
+        def factor_by_logs(banks, log_b, neg_log_w, factor):
             for half in range(2):
-                turned = take_bank(tile_banks(i)[half], "turned")
+                turned = take_bank(banks[half], "turned")
                 for q in range(4):
                     cols = span((half * 4 + q) * P, P)
                     dst = turned[:, span(q * P, P)]
@@ -364,12 +364,12 @@ def tile_list_stemma_deviation_kernel(
             )
         nc.scalar.activation(out=log_b[3], in_=log_b[3], func=ACT.Ln, bias=1.0)
         factor3 = sb("factor3", [P, S], F32)
-        factor_by_logs(2, log_b[2], neg_log_rows, factor_ring[2])
-        factor_by_logs(3, log_b[3], neg_log_rows, factor3)
+        factor_by_logs((0, 2), log_b[2], neg_log_rows, factor_ring[2])
+        factor_by_logs(tile_banks(3), log_b[3], neg_log_rows, factor3)
         scatter(2, factor_ring[2])
         fetch_by_halves(z0_t[2], sb("exemplar2", [P, M], F32, tag="w1_raw3")[:], 2)
         load_page(PAGE_SLOTS + 2)
-        round_w1_pair(0, log_b[2].bitcast(BF16))
+        round_w1_pair(0, log_b[3].bitcast(BF16))
         copy_a(3, tile_banks(3))
         scatter(3, factor3)
         fetch_by_halves(z0_t[3], sb("exemplar3", [P, M], F32, tag="w1_raw3")[:], 3)
@@ -408,7 +408,7 @@ def tile_list_stemma_deviation_kernel(
             if t > 0:
                 spread_log_w(t)
             factor = factor_ring[(PACK + t) % RING]
-            factor_by_logs(PACK + t, logs[t], neg_log_w[t], factor)
+            factor_by_logs(tile_banks(t), logs[t], neg_log_w[t], factor)
             copy_a(PACK + t, tile_banks(t))
             scatter(PACK + t, factor)
             if t == 0:

@@ -28,9 +28,10 @@ QUAD = 32
 LIST_ROWS = 16
 PAGE_SLOTS = 5
 RING = 3
-CHUNKS = (384, 384, 256)
-PLANE_ENDS = (384, 640, 1024)
 UNIT = 128
+CHUNKS = (384, 384, 256)
+VECTOR_UNITS = 3
+PLANE_ENDS = (CHUNKS[0], M - VECTOR_UNITS * UNIT, M)
 EVEN_BANK = 4
 ODD_BANK = 6
 
@@ -60,10 +61,6 @@ def tile_list_stemma_deviation_kernel(
             return span(half * BANK, BANK)
 
         idx, idx2, idx3, idx4 = [keep.tile([P, S // LIST_ROWS], U16, name="list%d" % i) for i in range(4)]
-        clocks = sb("clocks", [P, 16], U32)
-
-        def clock(k, ap):
-            nc.gpsimd.tensor_copy(clocks[:, 8 * k : 8 * k + 1], ap.bitcast(U32))
 
         tab_s = sb("tab_s", [P, T], U8)
         v_planes = sb("v_planes", [P, 2, S], U8)
@@ -106,12 +103,6 @@ def tile_list_stemma_deviation_kernel(
                 load_w1_pass(raw[:, a, :], a, i * P, P)
             return raw
 
-        def load_w1_passes(i):
-            raw = [sb("w1_raw%d%d" % (i, a), [P, PASS], F32)[:] for a in range(2)]
-            for a in range(2):
-                load_w1_pass(raw[a], a, i * P, P)
-            return raw
-
         def load_page(i):
             pages[i] = sb("page%d" % i, [P, T2], F32, tag="page", bufs=PAGE_SLOTS)
             if i < PACK:
@@ -137,12 +128,14 @@ def tile_list_stemma_deviation_kernel(
             nc.sync.dma_start(
                 out=v_planes[QUAD * q : QUAD * q + 4].bitcast(I32), in_=v_s[8 * q : 8 * q + 8, :].bitcast(I32)
             )
-        w1_raw = {0: load_w1_passes(0)}
+        w1_raw0 = [sb("w1_raw0%d" % a, [P, PASS], F32) for a in range(2)]
+        for a in range(2):
+            load_w1_pass(w1_raw0[a][:], a, 0, P)
         load_page(0)
         for cols in (span(0, QUARTER), span(QUARTER, S - QUARTER)):
             nc.sync.dma_start(out=wgs_rows[:, cols], in_=wgs[:, cols])
         load_w2_words(1)
-        w1_raw[1] = load_w1_tile(1)
+        w1_raw = {1: load_w1_tile(1)}
         nc.sync.dma_start(idx4[:], offs4)
         nc.sync.dma_start(idx3[:], offs3)
         w1_raw[2] = load_w1_tile(2)
@@ -199,30 +192,21 @@ def tile_list_stemma_deviation_kernel(
             )
             quantize_w1("w1_t%d" % i, grouped, [(i, 0), (i, 1)])
 
-        def round_w1_pass(copy, i, a, grouped):
-            interleave(copy, grouped, w1_raw[i][a].rearrange("p (i c) -> p i c", i=PACK))
-            quantize_w1("w1_t%d%d" % (i, a), grouped, [(i, a)])
-
-        def fetch_by_halves(dst, exemplar, i):
-            for half in range(2):
-                fetch_exemplar(exemplar[:, half_cols(half)], i, half * BANK, BANK)
-            for half in range(2):
-                cols = half_cols(half)
-                fetch_difference(dst[:, cols], exemplar[:, cols], i, half * BANK, BANK)
-
         def round_w1_pair(pair, grouped):
             nc.scalar.copy(
                 out=grouped.rearrange("p (u a m i) -> p a m u i", u=2, a=2, i=PACK),
-                in_=w1_raw_g1[:].rearrange("p (a i m t) -> p a m t i", a=2, i=PACK, t=PACK)[:, :, :, span(2 * pair, 2), :],
+                in_=w1_raw_g1[:].rearrange("p (a i m t) -> p a m t i", a=2, i=PACK, t=PACK)[
+                    :, :, :, span(2 * pair, 2), :
+                ],
             )
             keys = [(PACK + 2 * pair + u, a) for u in range(2) for a in range(2)]
             quantize_w1("w1_pair%d" % pair, grouped, keys)
 
-        def product_b(out, first, count, j_first, j_count, turned):
-            k = max(k for k in range(3) if w2_spans[k][0] <= first)
-            start = first - w2_spans[k][0]
-            for a in range(2):
-                w_side = w2_w[k][:, a, span(2 * start, 2 * count)].bitcast(FP4X4)
+        def product_b(out, first, count, j_first, j_count, turned, passes=(0, 1)):
+            part = max(k for k, (lo, hi) in enumerate(w2_spans) if lo <= first)
+            start = first - w2_spans[part][0]
+            for a in passes:
+                w_side = w2_w[part][:, a, span(2 * start, 2 * count)].bitcast(FP4X4)
                 w_scale = w2_s[:, span(a * H + first, count)]
                 v_side = v_words(a, j_first, j_count)
                 v_scale = v_planes[:, a, span(j_first, j_count)]
@@ -246,15 +230,18 @@ def tile_list_stemma_deviation_kernel(
                 )
             return acc
 
-        def damping(i, first, count, banks, scratch):
+        def damping(i, first, count, banks, scratch, steps=((0, 1),)):
+            b_runs = [take_bank(banks[k], "b_bank")[:, 0:count] for k in range(2)]
+            for passes in steps:
+                for k in range(2):
+                    product_b(b_runs[k], i * P, P, first + k * count, count, False, passes)
             for k in range(2):
-                b_bank = take_bank(banks[k], "b_bank")[:, 0:count]
-                product_b(b_bank, i * P, P, first + k * count, count, False)
-                nc.scalar.activation(out=scratch[k], in_=b_bank, func=ACT.Abs)
+                nc.scalar.activation(out=scratch[k], in_=b_runs[k], func=ACT.Abs)
             for k in range(2):
                 nc.scalar.activation(out=scratch[k], in_=scratch[k], func=ACT.Abs_reciprocal_sqrt, bias=1.0)
             for k in range(2):
-                nc.scalar.activation(out=factor_ring[i][:, span(first + k * count, count)], in_=scratch[k], func=ACT.Square)
+                damped = factor_ring[i][:, span(first + k * count, count)]
+                nc.scalar.activation(out=damped, in_=scratch[k], func=ACT.Square)
 
         def multiply_h(h, first, k):
             acc = product_a(0, first, QUARTER, k)
@@ -292,24 +279,28 @@ def tile_list_stemma_deviation_kernel(
         def fetch_difference(dst, exemplar, i, first, count):
             nc.vector.tensor_tensor(dst, pages[i][:].indirect(entries(idx3, first, count)), exemplar, ALU.subtract)
 
+        def fetch_by_halves(dst, exemplar, i):
+            for half in range(2):
+                fetch_exemplar(exemplar[:, half_cols(half)], i, half * BANK, BANK)
+            for half in range(2):
+                cols = half_cols(half)
+                fetch_difference(dst[:, cols], exemplar[:, cols], i, half * BANK, BANK)
+
         z_w = [sb("z_w%d" % g, [P, M], U32) for g in range(2)]
         z_s = [sb("z_s%d" % g, [P, M], U8) for g in range(2)]
-
-        def quantize_z(z, grouped, g, first, count, copy):
-            interleave(copy, grouped, z.rearrange("p (t m) -> p t m", t=PACK))
-            cols = span(first, count)
-            nc.vector.quantize_mx(out=z_w[g][:, cols].bitcast(FP8X4), scales=z_s[g][:, cols], in_=grouped)
 
         gather_words(0, 0, S)
         gather_words(1, 0, BANK)
         for a, copy in enumerate((nc.scalar.copy, nc.vector.tensor_copy)):
-            round_w1_pass(copy, 0, a, sb("w1_bf0%d" % a, [P, PASS], BF16)[:])
+            grouped = sb("w1_bf0%d" % a, [P, PASS], BF16)[:]
+            interleave(copy, grouped, w1_raw0[a][:].rearrange("p (i c) -> p i c", i=PACK))
+            quantize_w1("w1_t0%d" % a, grouped, [(0, a)])
         gather_words(1, BANK, BANK, "w1_raw01")
         log_w = sb("log_w", [P, S], F32)[:]
-        z0_t = {2: sb("z0_2", [P, M], F32)[:], 3: sb("z0_3", [P, M], F32)[:]}
+        z0_t = {2: sb("z0_2", [P, BANK], F32)[:], 3: sb("z0_3", [P, M], F32)[:]}
         for half, scratch in enumerate((sb("scratch0", [P, BANK], F32, tag="w1_raw00")[:], z0_t[2][:, 0:BANK])):
             runs = [scratch[:, span(k * QUARTER, QUARTER)] for k in range(2)]
-            damping(0, half * BANK, QUARTER, (2 * half, 2 * half + 1), runs)
+            damping(0, half * BANK, QUARTER, (2 * half, 2 * half + 1), runs, ((0,), (1,)))
         h = [a_ring[0][:, span(q * QUARTER, QUARTER)] for q in range(4)]
         for q in range(2):
             multiply_h(h[q], q * QUARTER, EVEN_BANK + q)
@@ -367,12 +358,13 @@ def tile_list_stemma_deviation_kernel(
         factor_by_logs((0, 2), log_b[2], neg_log_rows, factor_ring[2])
         factor_by_logs(tile_banks(3), log_b[3], neg_log_rows, factor3)
         scatter(2, factor_ring[2])
-        fetch_by_halves(z0_t[2], sb("exemplar2", [P, M], F32, tag="w1_raw3")[:], 2)
-        load_page(PAGE_SLOTS + 2)
+        exemplar2 = sb("exemplar2", [P, M], F32, tag="w1_raw2")
+        for half in range(2):
+            fetch_exemplar(exemplar2[:, half_cols(half)], 2, half * BANK, BANK)
+        fetch_difference(z0_t[2][:, 0:BANK], exemplar2[:, 0:BANK], 2, 0, BANK)
         round_w1_pair(0, log_b[3].bitcast(BF16))
         copy_a(3, tile_banks(3))
         scatter(3, factor3)
-        fetch_by_halves(z0_t[3], sb("exemplar3", [P, M], F32, tag="w1_raw3")[:], 3)
 
         log_b1 = sb("log_b1", [P, PACK * S], F32, tag="b_abs")
         for jb in range(BLOCKS):
@@ -383,6 +375,10 @@ def tile_list_stemma_deviation_kernel(
                 in_=bank[:].rearrange("j (p t) -> j t p", t=PACK),
                 func=ACT.Abs,
             )
+        z0_2_late = sb("z0_2_late", [P, BANK], F32, tag="w2_w2")
+        fetch_difference(z0_2_late[:], exemplar2[:, BANK:], 2, BANK, BANK)
+        load_page(PAGE_SLOTS + 2)
+        fetch_by_halves(z0_t[3], sb("exemplar3", [P, M], F32, tag="w2_s")[:], 3)
         logs = [log_b1[:, span(t * S, S)] for t in range(PACK)]
         neg_log_w = [sb("neg_log_w", [P, S], F32, tag="w1_t3_s")[:], logs[0], logs[1], logs[2]]
 
@@ -428,7 +424,9 @@ def tile_list_stemma_deviation_kernel(
                 mb = 2 * pair + k
                 bank = take_bank(EVEN_BANK + k, "z_turned")
                 for i in range(PACK):
-                    nc.tensor.transpose(bank[:, i * P : (i + 1) * P], z0_t[i][:, mb * P : (mb + 1) * P], ident[:])
+                    late = i == 2 and mb * P >= BANK
+                    block = z0_2_late[:, span(mb * P - BANK, P)] if late else z0_t[i][:, span(mb * P, P)]
+                    nc.tensor.transpose(bank[:, span(i * P, P)], block, ident[:])
                 nc.scalar.copy(
                     out=z0_turned[:, mb, :].rearrange("m (u p e) -> m u p e", u=2, e=2),
                     in_=bank[:].rearrange("m (p u e) -> m u p e", u=2, e=2),
@@ -466,64 +464,66 @@ def tile_list_stemma_deviation_kernel(
                     )
             return acc
 
-        def fetch_z1(first, width, start, count):
-            z = z1[:, span(PACK * start + (2 * UNIT if count > UNIT else 0), PACK * count)]
-            for t in range(PACK):
-                exemplar = exemplar4[:, t * width + start : t * width + start + count]
-                fetch_difference(z[:, t * count : (t + 1) * count], exemplar, PACK + t, first + start, count)
-            return z
-
-        def abs_float(y, acc):
-            nc.scalar.activation(out=y, in_=acc, func=ACT.Abs)
-
-        def abs_rounded(y_bf, acc):
-            nc.scalar.activation(
-                out=y_bf.rearrange("p (m t) -> p m t", t=PACK), in_=acc.rearrange("p t m -> p m t"), func=ACT.Abs
-            )
-
         exemplar4 = sb("exemplar4", [P, PACK * max(CHUNKS)], F32, tag="w1_pair1_w")
-        z1 = sb("z1", [P, PACK * max(CHUNKS) + 2 * UNIT], F32, tag="tab_w0")
-        y_tags = ("w1_raw1", "w1_raw2")
+        chunk_z_start = 2 * UNIT
+        z1 = sb("z1", [P, PACK * max(CHUNKS) + chunk_z_start], F32, tag="tab_w0")
         y_bf = sb("y_bf", [P, PACK * M], BF16, tag="tab_w1")
 
+        def make_z1(first, width, start, count, z_start, grouped, copy):
+            z = z1[:, span(z_start, PACK * count)]
+            for t in range(PACK):
+                exemplar = exemplar4[:, span(t * width + start, count)]
+                fetch_difference(z[:, span(t * count, count)], exemplar, PACK + t, first + start, count)
+            interleave(copy, grouped, z.rearrange("p (t m) -> p t m", t=PACK))
+            cols = span(first + start, count)
+            nc.vector.quantize_mx(out=z_w[1][:, cols].bitcast(FP8X4), scales=z_s[1][:, cols], in_=grouped)
+
+        def rounded_unit(column):
+            return y_bf[:, span(column * PACK, UNIT * PACK)]
+
         def store_planes(end):
-            first = ([0] + list(PLANE_ENDS))[PLANE_ENDS.index(end)]
-            cols = slice(first, end)
+            begin = max([0] + [e for e in PLANE_ENDS if e < end])
+            cols = slice(begin, end)
             nc.vector.quantize_mx(
-                out=y_w[:, cols].bitcast(FP8X4), scales=y_s[:, cols], in_=y_bf[:, first * PACK : end * PACK]
+                out=y_w[:, cols].bitcast(FP8X4), scales=y_s[:, cols], in_=y_bf[:, begin * PACK : end * PACK]
             )
             nc.sync.dma_start(out=y_words[:, cols], in_=y_w[:, cols].bitcast(I32))
 
+        chunk_y_tags = ("w1_raw1", "w1_raw2")
+        last_units = (("w1_bf00", "neg_log_rows", nc.sync), ("w1_bf01", "log_w", nc.scalar))
         first = 0
         for chunk, width in enumerate(CHUNKS):
             for t in range(PACK):
-                fetch_exemplar(exemplar4[:, t * width : (t + 1) * width], PACK + t, first, width)
-            y_bf_units = [y_bf[:, span((first + u * UNIT) * PACK, UNIT * PACK)] for u in range(width // UNIT)]
+                fetch_exemplar(exemplar4[:, span(t * width, width)], PACK + t, first, width)
             if first + width < M:
                 z_bf = sb("z1_bf%d" % chunk, [P, PACK * width], BF16, tag="b_abs")
-                quantize_z(fetch_z1(first, width, 0, width), z_bf[:], 1, first, width, nc.scalar.copy)
-                y = sb("y%d" % chunk, [P, width // UNIT, PACK, UNIT], F32, tag=y_tags[chunk])
+                make_z1(first, width, 0, width, chunk_z_start, z_bf[:], nc.scalar.copy)
+                y = sb("y%d" % chunk, [P, width // UNIT, PACK, UNIT], F32, tag=chunk_y_tags[chunk])
                 for u in range(width // UNIT):
-                    acc = product_y(first + u * UNIT)
-                    abs_float(y[:, u], acc)
                     column = first + u * UNIT
-                    nc.sync.dma_start(out=y_rows[:, :, column : column + UNIT], in_=y[:, u])
-                    if column < M - 3 * UNIT:
-                        abs_rounded(y_bf_units[u], acc)
+                    acc = product_y(column)
+                    nc.scalar.activation(out=y[:, u], in_=acc, func=ACT.Abs)
+                    nc.sync.dma_start(out=y_rows[:, :, span(column, UNIT)], in_=y[:, u])
+                    if column < M - VECTOR_UNITS * UNIT:
+                        nc.scalar.activation(
+                            out=rounded_unit(column).rearrange("p (m t) -> p m t", t=PACK),
+                            in_=acc.rearrange("p t m -> p m t"),
+                            func=ACT.Abs,
+                        )
                     else:
-                        interleave(nc.vector.tensor_copy, y_bf_units[u], y[:, u])
+                        interleave(nc.vector.tensor_copy, rounded_unit(column), y[:, u])
                     if column + UNIT in PLANE_ENDS:
                         store_planes(column + UNIT)
             else:
-                for u, (z_tag, y_tag, queue) in enumerate((("w1_bf00", "neg_log_rows", nc.sync), ("w1_bf01", "log_w", nc.scalar))):
+                for u, (z_tag, y_tag, queue) in enumerate(last_units):
                     column = first + u * UNIT
                     z_bf = sb("z1_bf%d" % column, [P, PACK * UNIT], BF16, tag=z_tag)
-                    quantize_z(fetch_z1(first, width, u * UNIT, UNIT), z_bf[:], 1, column, UNIT, nc.vector.tensor_copy)
+                    make_z1(first, width, u * UNIT, UNIT, u * PACK * UNIT, z_bf[:], nc.vector.tensor_copy)
                     y = sb("y%d" % column, [P, PACK, UNIT], F32, tag=y_tag)
                     acc = product_y(column)
-                    abs_float(y[:], acc)
-                    interleave(nc.vector.tensor_copy, y_bf_units[u], y[:])
-                    queue.dma_start(out=y_rows[:, :, column : column + UNIT], in_=y[:])
+                    nc.scalar.activation(out=y[:], in_=acc, func=ACT.Abs)
+                    interleave(nc.vector.tensor_copy, rounded_unit(column), y[:])
+                    queue.dma_start(out=y_rows[:, :, span(column, UNIT)], in_=y[:])
             first = first + width
         store_planes(M)
         for q in range(4):

from contextlib import ExitStack

import concourse.mybir as mybir
from concourse.masks import make_identity

K, H, N, T, S, T2, M = 1024, 1024, 512, 2048, 1024, 2048, 1024
FLOPS = 2 * (2 * K * H * S) + 2 * H * N * M

F32 = mybir.dt.float32
BF16 = mybir.dt.bfloat16
I32 = mybir.dt.int32
U32 = mybir.dt.uint32
U16 = mybir.dt.uint16
U8 = mybir.dt.uint8
FP8X4 = mybir.dt.float8_e4m3fn_x4
FP4X4 = mybir.dt.float4_e2m1fn_x4
ALU = mybir.AluOpType
ACT = mybir.ActivationFunctionType

P = 128
PACK = 4
PASS = P * PACK
BANK = 512
QUARTER = 256
BLOCKS = S // P
LINE = 4
QUAD = 32
LIST_ROWS = 16
PAGE_SLOTS = 5
RING = 3
UNIT = 128
CHUNKS = (384, 384, 256)
VECTOR_UNITS = 3
PLANE_ENDS = (CHUNKS[0], M - VECTOR_UNITS * UNIT, M)
EVEN_BANK = 4
ODD_BANK = 6


def tile_list_stemma_deviation_kernel(
    tc, tab_words, tab_scales, offs, offs2, offs3, offs4, w1, w2_words, w2_scales,
    w3_words, w3_scales, wgs, page0, out_0, out_1, out_2,
):
    nc = tc.nc
    with ExitStack() as ctx:
        keep = ctx.enter_context(tc.tile_pool(name="keep", bufs=1))
        psum = ctx.enter_context(tc.psum_pool(name="psum", bufs=1))

        def sb(name, shape, dtype, tag=None, bufs=1):
            return keep.tile(shape, dtype, name=name, tag=tag or name, bufs=bufs, align_bytes=64)

        def take_bank(k, name):
            return psum.tile([P, BANK], F32, name=name, tag="bank%d" % k)

        def entries(lst, first, count):
            return lst[:, first // LIST_ROWS : (first + count) // LIST_ROWS]

        def span(first, count):
            return slice(first, first + count)

        def half_cols(half):
            return span(half * BANK, BANK)

        idx, idx2, idx3, idx4 = [keep.tile([P, S // LIST_ROWS], U16, name="list%d" % i) for i in range(4)]

        tab_s = sb("tab_s", [P, T], U8)
        v_planes = sb("v_planes", [P, 2, S], U8)
        w2_s = sb("w2_s", [P, 2 * H], U8)
        w3_s_raw = sb("w3_s_raw", [P, N], U8)
        nc.gpsimd.memset(w2_s[:].bitcast(I32), 0)
        nc.vector.memset(tab_s[QUAD : 2 * QUAD, :].bitcast(I32), 0)
        nc.vector.memset(tab_s[2 * QUAD :, :].bitcast(I32), 0)
        nc.vector.memset(v_planes[:].rearrange("p a j -> p (a j)").bitcast(I32), 0)
        nc.vector.memset(w3_s_raw[:].bitcast(I32), 0)
        ident = sb("ident", [P, P], F32)
        make_identity(nc, ident[:])

        tab_w = [sb("tab_w%d" % a, [P, T], I32) for a in range(2)]
        w2_spans = ((0, P), (P, PASS), (PASS, H))
        w2_w = [sb("w2_w%d" % k, [P, 2, 2 * (hi - lo)], U8) for k, (lo, hi) in enumerate(w2_spans)]
        wgs_rows = sb("wgs_rows", [P, S], F32)
        w3_w_raw = sb("w3_w_raw", [P, 2, N], I32)
        pages = {}

        def load_tab_words(a):
            nc.sync.dma_start(out=tab_w[a][:], in_=tab_words[a].rearrange("p t i -> p (t i)").bitcast(I32))

        def load_w2_words(k):
            lo, hi = w2_spans[k]
            nc.sync.dma_start(
                out=w2_w[k][:].bitcast(I32),
                in_=w2_words[:, :, 2 * lo : 2 * hi].bitcast(I32).rearrange("a p c -> p a c"),
            )

        def load_w1_pass(dst, a, first, count):
            nc.sync.dma_start(
                out=dst.rearrange("p (i c) -> p i c", i=PACK),
                in_=w1[a * PASS : (a + 1) * PASS, span(first, count)].rearrange("(p i) c -> p i c", i=PACK),
            )

        def load_w1_tile(i):
            raw = sb("w1_raw%d" % i, [P, 2, PASS], F32)
            for a in range(2):
                load_w1_pass(raw[:, a, :], a, i * P, P)
            return raw

        def load_page(i):
            pages[i] = sb("page%d" % i, [P, T2], F32, tag="page", bufs=PAGE_SLOTS)
            if i < PACK:
                rows = page0[i * P : (i + 1) * P, :]
            else:
                rows = page0[PASS:, :].rearrange("(p t) c -> t p c", t=PACK)[i - PACK]
            nc.sync.dma_start(out=pages[i][:], in_=rows)

        nc.sync.dma_start(idx[:], offs)
        nc.sync.dma_start(out=tab_s[0:QUAD, :].bitcast(I32), in_=tab_scales.bitcast(I32).rearrange("a q t -> q a t"))
        load_tab_words(0)
        load_w2_words(0)
        for q in range(4):
            nc.sync.dma_start(
                out=w2_s[QUAD * q : QUAD * q + 4, :].bitcast(I32).rearrange("r (a c) -> r a c", a=2),
                in_=w2_scales[:, 4 * q : 4 * q + 4, :].bitcast(I32).rearrange("a r c -> r a c"),
            )
        nc.sync.dma_start(idx2[:], offs2)
        load_tab_words(1)
        v_s = sb("v_s", [P, S], U8)
        nc.vector.tensor_copy(v_s[:], tab_s[:].indirect(idx[:]))
        for q in range(4):
            nc.sync.dma_start(
                out=v_planes[QUAD * q : QUAD * q + 4].bitcast(I32), in_=v_s[8 * q : 8 * q + 8, :].bitcast(I32)
            )
        w1_raw0 = [sb("w1_raw0%d" % a, [P, PASS], F32) for a in range(2)]
        for a in range(2):
            load_w1_pass(w1_raw0[a][:], a, 0, P)
        load_page(0)
        for cols in (span(0, QUARTER), span(QUARTER, S - QUARTER)):
            nc.sync.dma_start(out=wgs_rows[:, cols], in_=wgs[:, cols])
        load_w2_words(1)
        w1_raw = {1: load_w1_tile(1)}
        nc.sync.dma_start(idx4[:], offs4)
        nc.sync.dma_start(idx3[:], offs3)
        w1_raw[2] = load_w1_tile(2)
        load_page(1)
        w1_raw[3] = load_w1_tile(3)
        load_w2_words(2)
        w1_raw_g1 = sb("w1_raw_g1", [P, 2 * PACK * PASS], F32)
        for a in range(2):
            load_w1_pass(w1_raw_g1[:, span(a * PACK * PASS, PACK * PASS)], a, PASS, PASS)
        load_page(2)
        nc.sync.dma_start(out=w3_w_raw[:], in_=w3_words.rearrange("a p c i -> p a (c i)").bitcast(I32))
        for q in range(4):
            nc.sync.dma_start(
                out=w3_s_raw[QUAD * q : QUAD * q + 8, :].bitcast(I32),
                in_=w3_scales[:, 4 * q : 4 * q + 4, :].bitcast(I32),
            )
        for i in range(3, PAGE_SLOTS):
            load_page(i)
        warm = sb("warm", [P, 1], F32)
        nc.scalar.activation(out=warm[:], in_=ident[:, 0:1], func=ACT.Abs_reciprocal_sqrt, bias=1.0)

        w1_w, w1_s = {}, {}
        factor_ring = [sb("factor%d" % i, [P, S], F32) for i in range(RING)]
        a_ring = [sb("a%d" % i, [P, S], F32) for i in range(2)]
        v_half = {}

        def gather_words(a, first, count, tag=None):
            words = sb("v%d_%d" % (a, first), [P, count], U32, tag=tag)
            nc.vector.tensor_copy(words[:], tab_w[a][:].bitcast(U32).indirect(entries(idx, first, count)))
            for half in range(count // BANK):
                v_half[a, first // BANK + half] = words[:, half_cols(half)]

        def v_words(a, first, count):
            half, start = divmod(first, BANK)
            return v_half[a, half][:, span(start, count)].bitcast(FP8X4)

        def quantize_w1(name, grouped, keys):
            words = sb(name + "_w", [P, P * len(keys)], U32)
            scales = sb(name + "_s", [P, P * len(keys)], U8)
            nc.vector.quantize_mx(out=words[:].bitcast(FP8X4), scales=scales[:], in_=grouped)
            for k, key in enumerate(keys):
                w1_w[key], w1_s[key] = words[:, span(k * P, P)], scales[:, span(k * P, P)]

        def interleave(copy, grouped, slices):
            copy(
                out=grouped.rearrange("p (c i t) -> p c t i", i=LINE, t=PACK),
                in_=slices.rearrange("p t (c i) -> p c t i", i=LINE),
            )

        def round_w1_tile(i, grouped):
            nc.scalar.copy(
                out=grouped.rearrange("p (a c l i) -> p a c i l", a=2, l=LINE, i=PACK),
                in_=w1_raw[i][:].rearrange("p a (i c l) -> p a c i l", i=PACK, l=LINE),
            )
            quantize_w1("w1_t%d" % i, grouped, [(i, 0), (i, 1)])

        def round_w1_pair(pair, grouped):
            nc.scalar.copy(
                out=grouped.rearrange("p (u a m i) -> p a m u i", u=2, a=2, i=PACK),
                in_=w1_raw_g1[:].rearrange("p (a i m t) -> p a m t i", a=2, i=PACK, t=PACK)[
                    :, :, :, span(2 * pair, 2), :
                ],
            )
            keys = [(PACK + 2 * pair + u, a) for u in range(2) for a in range(2)]
            quantize_w1("w1_pair%d" % pair, grouped, keys)

        def product_b(out, first, count, j_first, j_count, turned, passes=(0, 1)):
            part = max(k for k, (lo, hi) in enumerate(w2_spans) if lo <= first)
            start = first - w2_spans[part][0]
            for a in passes:
                w_side = w2_w[part][:, a, span(2 * start, 2 * count)].bitcast(FP4X4)
                w_scale = w2_s[:, span(a * H + first, count)]
                v_side = v_words(a, j_first, j_count)
                v_scale = v_planes[:, a, span(j_first, j_count)]
                sides = (v_side, v_scale, w_side, w_scale) if turned else (w_side, w_scale, v_side, v_scale)
                nc.tensor.matmul_mx(
                    out=out, lhsT=sides[0], lhsT_scale=sides[1], rhs=sides[2], rhs_scale=sides[3],
                    start=(a == 0), stop=(a == 1),
                )

        def product_a(i, first, count, k):
            acc = take_bank(k, "acc")[:, 0:count]
            for a in range(2):
                nc.tensor.matmul_mx(
                    out=acc,
                    lhsT=w1_w[i, a].bitcast(FP8X4),
                    lhsT_scale=w1_s[i, a],
                    rhs=v_words(a, first, count),
                    rhs_scale=v_planes[:, a, span(first, count)],
                    start=(a == 0),
                    stop=(a == 1),
                )
            return acc

        def damping(i, first, count, banks, scratch, steps=((0, 1),)):
            b_runs = [take_bank(banks[k], "b_bank")[:, 0:count] for k in range(2)]
            for passes in steps:
                for k in range(2):
                    product_b(b_runs[k], i * P, P, first + k * count, count, False, passes)
            for k in range(2):
                nc.scalar.activation(out=scratch[k], in_=b_runs[k], func=ACT.Abs)
            for k in range(2):
                nc.scalar.activation(out=scratch[k], in_=scratch[k], func=ACT.Abs_reciprocal_sqrt, bias=1.0)
            for k in range(2):
                damped = factor_ring[i][:, span(first + k * count, count)]
                nc.scalar.activation(out=damped, in_=scratch[k], func=ACT.Square)

        def multiply_h(h, first, k):
            acc = product_a(0, first, QUARTER, k)
            nc.vector.tensor_tensor(h, acc, factor_ring[0][:, span(first, QUARTER)], ALU.mult)

        def tile_banks(i):
            first = (EVEN_BANK, ODD_BANK)[i % 2]
            return (first, first + 1)

        def copy_a(i, banks):
            for half in range(2):
                acc = product_a(i, half * BANK, BANK, banks[half])
                nc.scalar.copy(out=a_ring[i % 2][:, half_cols(half)], in_=acc)

        def factor_by_logs(banks, log_b, neg_log_w, factor):
            for half in range(2):
                turned = take_bank(banks[half], "turned")
                for q in range(4):
                    cols = span((half * 4 + q) * P, P)
                    dst = turned[:, span(q * P, P)]
                    nc.tensor.matmul(dst, log_b[:, cols], ident[:], start=True, stop=False, is_transpose=True)
                    nc.tensor.matmul(dst, neg_log_w[:, cols], ident[:], start=False, stop=True, is_transpose=True)
                nc.scalar.activation(out=factor[:, half_cols(half)], in_=turned[:], func=ACT.Exp, scale=-1.0)

        def scatter_part(values, first, count):
            factors = wgs_rows[:, span(first, count)]
            nc.vector.tensor_tensor(pages[0][:].indirect(entries(idx2, first, count)), values, factors, ALU.mult)

        def scatter(i, factors):
            nc.vector.tensor_tensor(pages[i][:].indirect(idx2[:]), a_ring[i % 2][:], factors[:], ALU.mult)

        def fetch_exemplar(dst, i, first, count):
            nc.vector.tensor_copy(dst, pages[i][:].indirect(entries(idx4, first, count)))

        def fetch_difference(dst, exemplar, i, first, count):
            nc.vector.tensor_tensor(dst, pages[i][:].indirect(entries(idx3, first, count)), exemplar, ALU.subtract)

        def fetch_by_halves(dst, exemplar, i):
            for half in range(2):
                fetch_exemplar(exemplar[:, half_cols(half)], i, half * BANK, BANK)
            for half in range(2):
                cols = half_cols(half)
                fetch_difference(dst[:, cols], exemplar[:, cols], i, half * BANK, BANK)

        z_w = [sb("z_w%d" % g, [P, M], U32) for g in range(2)]
        z_s = [sb("z_s%d" % g, [P, M], U8) for g in range(2)]

        gather_words(0, 0, S)
        gather_words(1, 0, BANK)
        for a, copy in enumerate((nc.scalar.copy, nc.vector.tensor_copy)):
            grouped = sb("w1_bf0%d" % a, [P, PASS], BF16)[:]
            interleave(copy, grouped, w1_raw0[a][:].rearrange("p (i c) -> p i c", i=PACK))
            quantize_w1("w1_t0%d" % a, grouped, [(0, a)])
        gather_words(1, BANK, BANK, "w1_raw01")
        log_w = sb("log_w", [P, S], F32)[:]
        z0_t = {2: sb("z0_2", [P, BANK], F32)[:], 3: sb("z0_3", [P, M], F32)[:]}
        for half, scratch in enumerate((sb("scratch0", [P, BANK], F32, tag="w1_raw00")[:], z0_t[2][:, 0:BANK])):
            runs = [scratch[:, span(k * QUARTER, QUARTER)] for k in range(2)]
            damping(0, half * BANK, QUARTER, (2 * half, 2 * half + 1), runs, ((0,), (1,)))
        h = [a_ring[0][:, span(q * QUARTER, QUARTER)] for q in range(4)]
        for q in range(2):
            multiply_h(h[q], q * QUARTER, EVEN_BANK + q)
        for q in range(2):
            scatter_part(h[q], q * QUARTER, QUARTER)
            multiply_h(h[2 + q], BANK + q * QUARTER, EVEN_BANK + q)
        scatter_part(a_ring[0][:, BANK:], BANK, BANK)

        w1_bf1 = sb("w1_bf1", [P, 2 * PASS], BF16)
        round_w1_tile(1, w1_bf1[:])
        z0_t[0] = sb("z0_0", [P, M], F32)[:]
        fetch_by_halves(z0_t[0], sb("exemplar0", [P, M], F32, tag="w1_raw1")[:], 0)
        damping(1, 0, BANK, (0, 2), [z0_t[3][:, 0:BANK], log_w[:, 0:BANK]])
        b_banks = [take_bank(k, "b_bank") for k in (1, 3, EVEN_BANK, EVEN_BANK + 1)]
        for pair, bank in enumerate(b_banks):
            for k in range(2):
                product_b(bank[:, span(k * 2 * P, 2 * P)], 2 * P, 2 * P, (2 * pair + k) * P, P, True)
        factor1 = sb("factor_t1", [P, S], F32, tag="w1_bf1")
        nc.gpsimd.tensor_tensor(factor1[:], factor_ring[1][:], wgs_rows[:], ALU.mult)
        w1_bf2 = sb("w1_bf2", [P, 2 * PASS], BF16)
        round_w1_tile(2, w1_bf2[:])

        log_b0 = sb("log_b0", [P, 2 * S], F32, tag="tab_w0")
        for pair, bank in enumerate(b_banks):
            nc.scalar.activation(
                out=log_b0[:].rearrange("j (t b p) -> j t b p", t=2, p=P)[:, :, 2 * pair : 2 * pair + 2, :],
                in_=bank[:].rearrange("j (b t p) -> j t b p", t=2, p=P),
                func=ACT.Abs,
            )
        copy_a(1, (1, 3))
        scatter(1, factor1)
        load_page(PAGE_SLOTS)
        round_w1_tile(3, sb("w1_bf3", [P, 2 * PASS], BF16, tag="w1_t1_w")[:])
        z0_t[1] = sb("z0_1", [P, M], F32)[:]
        fetch_by_halves(z0_t[1], sb("exemplar1", [P, M], F32, tag="w1_raw3")[:], 1)
        load_page(PAGE_SLOTS + 1)

        nc.scalar.activation(out=log_w, in_=wgs_rows[:], func=ACT.Ln)
        log_w_turned = []
        for half in range(2):
            bank = take_bank(2 * half + 1, "log_w_turned")
            for q in range(4):
                nc.tensor.transpose(bank[:, span(q * P, P)], log_w[:, span((half * 4 + q) * P, P)], ident[:])
            log_w_turned.append(bank)
        log_b = {i: log_b0[:, span((i - 2) * S, S)] for i in (2, 3)}
        nc.scalar.activation(out=log_b[2], in_=log_b[2], func=ACT.Ln, bias=1.0)
        copy_a(2, tile_banks(2))
        neg_log_rows = sb("neg_log_rows", [P, S], F32)
        for half in range(2):
            nc.scalar.activation(
                out=neg_log_rows[:, half_cols(half)], in_=log_w_turned[half][:], func=ACT.Copy, scale=-1.0
            )
        nc.scalar.activation(out=log_b[3], in_=log_b[3], func=ACT.Ln, bias=1.0)
        factor3 = sb("factor3", [P, S], F32)
        factor_by_logs((0, 2), log_b[2], neg_log_rows, factor_ring[2])
        factor_by_logs(tile_banks(3), log_b[3], neg_log_rows, factor3)
        scatter(2, factor_ring[2])
        exemplar2 = sb("exemplar2", [P, M], F32, tag="w1_raw2")
        for half in range(2):
            fetch_exemplar(exemplar2[:, half_cols(half)], 2, half * BANK, BANK)
        fetch_difference(z0_t[2][:, 0:BANK], exemplar2[:, 0:BANK], 2, 0, BANK)
        round_w1_pair(0, log_b[3].bitcast(BF16))
        copy_a(3, tile_banks(3))
        scatter(3, factor3)

        log_b1 = sb("log_b1", [P, PACK * S], F32, tag="b_abs")
        for jb in range(BLOCKS):
            bank = take_bank(2 * (jb % 2) if jb < BLOCKS - 2 else ODD_BANK + jb % 2, "b_bank")
            product_b(bank[:], PASS, PASS, jb * P, P, True)
            nc.scalar.activation(
                out=log_b1[:].rearrange("j (t s) -> j t s", t=PACK)[:, :, span(jb * P, P)],
                in_=bank[:].rearrange("j (p t) -> j t p", t=PACK),
                func=ACT.Abs,
            )
        z0_2_late = sb("z0_2_late", [P, BANK], F32, tag="w2_w2")
        fetch_difference(z0_2_late[:], exemplar2[:, BANK:], 2, BANK, BANK)
        load_page(PAGE_SLOTS + 2)
        fetch_by_halves(z0_t[3], sb("exemplar3", [P, M], F32, tag="w2_s")[:], 3)
        logs = [log_b1[:, span(t * S, S)] for t in range(PACK)]
        neg_log_w = [sb("neg_log_w", [P, S], F32, tag="w1_t3_s")[:], logs[0], logs[1], logs[2]]

        def spread_log_w(t):
            for half in range(2):
                rows = log_w_turned[half][:].rearrange("j (b q t) -> j t b q", t=PACK, b=4)[:, t]
                nc.scalar.activation(
                    out=neg_log_w[t][:, half_cols(half)].rearrange("j (b r q) -> j b r q", r=4, q=QUAD),
                    in_=rows.unsqueeze(2).to_broadcast([P, 4, 4, QUAD]),
                    func=ACT.Copy,
                    scale=-1.0,
                )

        spread_log_w(0)
        for t in range(PACK):
            nc.scalar.activation(out=logs[t], in_=logs[t], func=ACT.Ln, bias=1.0)
        w3_s = sb("w3_s", [P, N], U8, tag="factor3")
        nc.gpsimd.tensor_copy(
            out=w3_s[:].rearrange("p (t m) -> p t m", t=PACK),
            in_=w3_s_raw[:].rearrange("p (m t) -> p t m", t=PACK),
        )
        for t in range(PACK):
            if t > 0:
                spread_log_w(t)
            factor = factor_ring[(PACK + t) % RING]
            factor_by_logs(tile_banks(t), logs[t], neg_log_w[t], factor)
            copy_a(PACK + t, tile_banks(t))
            scatter(PACK + t, factor)
            if t == 0:
                round_w1_pair(1, sb("w1_bf_pair1", [P, PACK * PASS], BF16, tag="w1_t3_s")[:])

        w3_w = sb("w3_w", [P, 2, N], U32, tag="w1_pair1_s")
        nc.scalar.copy(
            out=w3_w[:].rearrange("p a (t m) -> p a m t", t=PACK),
            in_=w3_w_raw[:].bitcast(U32).rearrange("p a (m t) -> p a m t", t=PACK),
        )

        z0_turned = sb("z0_turned", [P, BLOCKS, PASS], BF16, tag="b_abs")
        z0_bf = sb("z0_bf", [P, PACK * M], BF16, tag="w1_raw_g1")
        for pair in range(BLOCKS // 2):
            back = take_bank(2 * (pair % 2), "z_back")
            for k in range(2):
                mb = 2 * pair + k
                bank = take_bank(EVEN_BANK + k, "z_turned")
                for i in range(PACK):
                    late = i == 2 and mb * P >= BANK
                    block = z0_2_late[:, span(mb * P - BANK, P)] if late else z0_t[i][:, span(mb * P, P)]
                    nc.tensor.transpose(bank[:, span(i * P, P)], block, ident[:])
                nc.scalar.copy(
                    out=z0_turned[:, mb, :].rearrange("m (u p e) -> m u p e", u=2, e=2),
                    in_=bank[:].rearrange("m (p u e) -> m u p e", u=2, e=2),
                )
                words = z0_turned[:, mb, :].bitcast(F32)
                for u in range(2):
                    first = (2 * k + u) * P
                    nc.tensor.transpose(back[:, first : first + P], words[:, u * P : (u + 1) * P], ident[:])
            nc.scalar.copy(
                out=z0_bf[:, pair * 2 * PASS : (pair + 1) * 2 * PASS].bitcast(F32).rearrange(
                    "p (k m u) -> p k m u", k=2, u=2
                ),
                in_=back[:].rearrange("p (k u m) -> p k m u", k=2, u=2),
            )
        nc.vector.quantize_mx(out=z_w[0][:].bitcast(FP8X4), scales=z_s[0][:], in_=z0_bf[:])

        y_w = sb("y_w", [P, M], U32)
        y_s = sb("y_s", [P, M], U8)
        y_rows = out_0.rearrange("(p t) m -> p t m", t=PACK)
        y_words = out_1[0].rearrange("p m t -> p (m t)").bitcast(I32)

        def product_y(first):
            cols = slice(first, first + UNIT)
            acc = take_bank(first // UNIT, "y_acc")[:].rearrange("p (t m) -> p t m", t=PACK)
            for g in range(2):
                for t in range(PACK):
                    nc.tensor.matmul_mx(
                        out=acc[:, t, :],
                        lhsT=w3_w[:, g, t * P : (t + 1) * P].bitcast(FP8X4),
                        lhsT_scale=w3_s[4 * g : P, t * P : (t + 1) * P],
                        rhs=z_w[g][:, cols].bitcast(FP8X4),
                        rhs_scale=z_s[g][:, cols],
                        start=(g == 0 and t == 0),
                        stop=(g == 1 and t == PACK - 1),
                    )
            return acc

        exemplar4 = sb("exemplar4", [P, PACK * max(CHUNKS)], F32, tag="w1_pair1_w")
        chunk_z_start = 2 * UNIT
        z1 = sb("z1", [P, PACK * max(CHUNKS) + chunk_z_start], F32, tag="tab_w0")
        y_bf = sb("y_bf", [P, PACK * M], BF16, tag="tab_w1")

        def make_z1(first, width, start, count, z_start, grouped, copy):
            z = z1[:, span(z_start, PACK * count)]
            for t in range(PACK):
                exemplar = exemplar4[:, span(t * width + start, count)]
                fetch_difference(z[:, span(t * count, count)], exemplar, PACK + t, first + start, count)
            interleave(copy, grouped, z.rearrange("p (t m) -> p t m", t=PACK))
            cols = span(first + start, count)
            nc.vector.quantize_mx(out=z_w[1][:, cols].bitcast(FP8X4), scales=z_s[1][:, cols], in_=grouped)

        def rounded_unit(column):
            return y_bf[:, span(column * PACK, UNIT * PACK)]

        def store_planes(end):
            begin = max([0] + [e for e in PLANE_ENDS if e < end])
            cols = slice(begin, end)
            nc.vector.quantize_mx(
                out=y_w[:, cols].bitcast(FP8X4), scales=y_s[:, cols], in_=y_bf[:, begin * PACK : end * PACK]
            )
            nc.sync.dma_start(out=y_words[:, cols], in_=y_w[:, cols].bitcast(I32))

        chunk_y_tags = ("w1_raw1", "w1_raw2")
        last_units = (("w1_bf00", "neg_log_rows", nc.sync), ("w1_bf01", "log_w", nc.scalar))
        first = 0
        for chunk, width in enumerate(CHUNKS):
            for t in range(PACK):
                fetch_exemplar(exemplar4[:, span(t * width, width)], PACK + t, first, width)
            if first + width < M:
                z_bf = sb("z1_bf%d" % chunk, [P, PACK * width], BF16, tag="b_abs")
                make_z1(first, width, 0, width, chunk_z_start, z_bf[:], nc.scalar.copy)
                y = sb("y%d" % chunk, [P, width // UNIT, PACK, UNIT], F32, tag=chunk_y_tags[chunk])
                for u in range(width // UNIT):
                    column = first + u * UNIT
                    acc = product_y(column)
                    nc.scalar.activation(out=y[:, u], in_=acc, func=ACT.Abs)
                    nc.sync.dma_start(out=y_rows[:, :, span(column, UNIT)], in_=y[:, u])
                    if column < M - VECTOR_UNITS * UNIT:
                        nc.scalar.activation(
                            out=rounded_unit(column).rearrange("p (m t) -> p m t", t=PACK),
                            in_=acc.rearrange("p t m -> p m t"),
                            func=ACT.Abs,
                        )
                    else:
                        interleave(nc.vector.tensor_copy, rounded_unit(column), y[:, u])
                    if column + UNIT in PLANE_ENDS:
                        store_planes(column + UNIT)
            else:
                for u, (z_tag, y_tag, queue) in enumerate(last_units):
                    column = first + u * UNIT
                    z_bf = sb("z1_bf%d" % column, [P, PACK * UNIT], BF16, tag=z_tag)
                    make_z1(first, width, u * UNIT, UNIT, u * PACK * UNIT, z_bf[:], nc.vector.tensor_copy)
                    y = sb("y%d" % column, [P, PACK, UNIT], F32, tag=y_tag)
                    acc = product_y(column)
                    nc.scalar.activation(out=y[:], in_=acc, func=ACT.Abs)
                    interleave(nc.vector.tensor_copy, rounded_unit(column), y[:])
                    queue.dma_start(out=y_rows[:, :, span(column, UNIT)], in_=y[:])
            first = first + width
        store_planes(M)
        for q in range(4):
            (nc.sync, nc.scalar)[q % 2].dma_start(
                out=out_2[0, 4 * q : 4 * q + 4, :].bitcast(I32), in_=y_s[QUAD * q : QUAD * q + 4, :].bitcast(I32)
            )
